import numpy as np, ml_dtypes
CORES = [242,247,114,119]
N = 4
BF = ml_dtypes.bfloat16
def gentries(a):
    return np.ascontiguousarray(a.reshape(8, 16, -1).transpose(0, 2, 1)).reshape(8, -1)
def gtable(e):
    e = np.asarray(e); return np.ascontiguousarray(e.reshape(8, -1, 16).transpose(0, 2, 1)).reshape(128, -1).astype(np.int32)
WX, WV, C, K, RO, TH = 2048, 2048, 256, 16, 4, 12
def flip(P, m):
    k = np.arange(K); m = np.asarray(m)[..., None]
    return np.take_along_axis(P, np.where(k <= m, m - k, k), -1)
def place(u):
    return (((u * u) >> 5) + 37 * u) & (WV - 1)
def slots(F, w):
    u = np.add.reduce(F * w[:, :, None], axis=1) & 4095
    return u, place(u)
def prints(X, Q):
    n, c = Q.shape[:2]; a = np.take_along_axis(X, Q.reshape(n, 1, c * K), 2).reshape(n, 16, c, K)
    return np.add.reduce(a * np.arange(K), axis=3) & 255
def parts(rng):
    X = rng.integers(0, 256, (N, 8, 16, WX)); w = rng.integers(0, 16, (N, 8, 16)); R = C >> 3; P = []; S = []; gg = np.arange(8)[:, None]
    a = rng.integers(0, WX, (8, R, K)); ma = rng.integers(1, K, (8, R))
    for q in range(N):
        roots = np.concatenate([a, rng.integers(0, WX, (8, R, K))], axis=1); ms = np.concatenate([ma, rng.integers(1, K, (8, R))], axis=1)
        fam = rng.integers(0, 2 * R, (8, C)); root = roots[gg, fam]; m = ms[gg, fam]
        kind = rng.integers(0, 4, (8, C)); m1 = rng.integers(1, K, (8, C)); m2 = rng.integers(0, K, (8, C))
        one = np.where(kind == 1, 0, np.where(kind == 2, m, m1))
        P.append(flip(flip(root, one), np.where(kind == 3, m2, 0)))
        S.append(np.where(kind == 0, m1, np.where(kind == 3, rng.integers(0, K, (8, C)), m)))
    return X, w, np.stack(P), np.stack(S)
def junk(rng, share):
    return np.where(rng.random((N, 8, 1, WV)) < share, rng.integers(0, 256, (N, 8, 16, WV)), 512)
def near(rng, F, tol, n):
    o = np.argsort(rng.random(F.shape), axis=1)
    d = np.where(o < n, np.where(rng.random(F.shape) < 0.5, tol, np.minimum(rng.integers(0, 6, F.shape), tol)), tol + 1 + rng.choice(np.array([0, 0, 1, 40]), F.shape))
    z = np.where(rng.random(F.shape) < 0.5, F + d, F - d)
    return np.where(z < 0, F + d, np.where(z > 255, F - d, z))
def sow(rng, X, V, w, P, s):
    E = 6
    for q in range(N):
        for t in range(RO):
            r = (q - t) % N; c = rng.permutation(C)[:C >> 2]; n = len(c)
            st = P[r][:, c]; m = np.maximum(s[r][:, c], 1)
            if t & 1: st = flip(st, m)
            F = prints(X[q], flip(st, m)); h = slots(F, w[q])[1]
            np.put_along_axis(V[q], h[:, None, :], near(rng, F, rng.integers(2, 6, (8, 1, n)), rng.choice(np.array([11, 12, 12, 13, 16]), (8, 1, n))), 2)
            Q = flip(np.broadcast_to(st[:, :E, None], (8, E, K - 1, K)), np.broadcast_to(np.arange(1, K), (8, E, K - 1))).reshape(8, E * (K - 1), K)
            F = prints(X[q], Q); h = slots(F, w[q])[1]; e = (E >> 1) * (K - 1)
            z = near(rng, F, 2, rng.choice(np.array([12, 13, 16]), (8, 1, E * (K - 1)))); z[:, :, :e] = F[:, :, :e]
            np.put_along_axis(V[q], h[:, None, :], z, 2)
    return V
def pack(X, V, P, s, w):
    return {"x": np.ascontiguousarray(X.reshape(N, 128, WX)).astype(np.float32).astype(BF), "v": np.ascontiguousarray(V.reshape(N, 128, WV)).astype(np.float32).astype(BF),
            "lanes": np.stack([gtable(a.reshape(8, C * K)) for a in P]), "s0": np.ascontiguousarray(s).astype(np.int32), "wt": np.ascontiguousarray(w.reshape(N, 128, 1)).astype(np.int32)}
def setup_inputs(rng):
    X, w, P, s = parts(rng)
    return pack(X, sow(rng, X, junk(rng, 0.2), w, P, s), P, s, w)
def setup_inputs_spread(rng):
    X, w, P, s = parts(rng)
    X = (np.exp2(8 * rng.random((N, 8, 1, WX))) * rng.random((N, 8, 16, WX))).astype(np.int64)
    w = (16 * rng.random((N, 8, 16)) ** 3).astype(np.int64); w[:, :, 5] = 1 + 2 * rng.integers(0, 8, (N, 8))
    tb = (WX * rng.random((8, WX)) ** 3).astype(np.int64); tb[:, 0] = WX - 1
    P = np.stack([tb[g][P[:, g]] for g in range(8)], axis=1)
    s = np.where(rng.random(s.shape) < 0.3, (K * rng.random(s.shape) ** 3).astype(np.int64), s)
    return pack(X, sow(rng, X, junk(rng, 0.5), w, P, s), P, s, w)
def setup_inputs_ends(rng):
    X = 255 * rng.integers(0, 2, (N, 8, 16, WX)); w = 15 * rng.integers(0, 2, (N, 8, 16))
    V = np.where(rng.random((N, 8, 1, WV)) < 0.25, 512 * rng.integers(0, 2, (N, 8, 16, WV)), 512 * rng.integers(0, 2, (N, 8, 1, WV)))
    for g in range(8):
        kind = 3 - (g & 3); o = rng.permutation(16)
        X[:, g, :, 0] = 255 if kind == 1 else 0; X[:, g, :, WX - 1] = 255 if kind == 0 else 0
        if kind == 0: w[:, g] = 15
        if kind == 1: w[:, g, o[0]] = 15; w[:, g, o[1]] = 0
        if kind == 2:
            for i in o[:4]: X[:, g, i, WX - 1] = 255; w[:, g, i] = 15
        if kind == 3:
            for i in o[:3]: X[:, g, i, 0] = 255; w[:, g, i] = 15
    P = np.where(rng.random((N, 8, C, K)) < rng.random((N, 8, C, 1)), WX - 1, 0); s = (K - 1) * rng.integers(0, 2, (N, 8, C))
    for c in (0, 1, C - 2, C - 1): P[:, :, c] = 0
    for c in (2, C - 3): P[:, :, c] = WX - 1
    for c in (3, C - 4): P[:, :, c] = 0; P[:, :, c, 0] = WX - 1; s[:, :, c] = 0
    for c in (4, C - 5): P[:, :, c] = 0; P[:, :, c, K - 1] = WX - 1; s[:, :, c] = K - 1
    V[1::2, :, :, 0] = 512; V[0::2, :, :, 0] = 0
    return pack(X, V, P, s, w)
def setup_inputs_corners(rng):
    X, w, P, s = parts(rng); top = int(np.argmax(place(np.arange(4096))))
    for q in range(N):
        for g in range(8):
            z = (q + g) & 7
            if z == 2: w[q, g] = 0
            if z == 3: w[q, g] = 15
            if z == 4:
                w[q, g] = 15; w[q, g, 0] = 1; X[q, g, :, 0] = 0; X[q, g, :, WX - 1] = 0
                b = top // 15; X[q, g, 0, WX - 1] = top - 15 * b; X[q, g, 1, WX - 1] = min(b, 255); X[q, g, 2, WX - 1] = b - min(b, 255)
                P[q, g, C - 1] = 0; P[q, g, C - 1, 0] = WX - 1; s[q, g, C - 1] = 1; P[q, g, 0] = 0; P[q, g, C - 2] = 0
                e = rng.integers(1, WX - 1, 8); h = slots(prints(X[q, g:g + 1], np.repeat(e, K).reshape(1, 8, K)), w[q, g:g + 1])[1][0]
                P[q, g, 1] = int(e[np.argmax((h != 0) & (h != int(place(np.int64(top)))))])
            if z == 5: P[q, g] = rng.integers(0, WX, (C, 1))
            if z == 7: s[q, g] = rng.choice(np.array([0, 1, K - 1]), C)
    V = sow(rng, X, junk(rng, 0.2), w, P, s)
    for q in range(N):
        for g in range(8):
            z = (q + g) & 7
            if z == 0: V[q, g] = 512
            if z == 1: V[q, g] = np.where(V[q, g] == 512, rng.integers(0, 256, (16, WV)), V[q, g])
            if z == 2:
                P[q, g, :8] = int(rng.integers(0, WX))
                V[q, g][:, 0] = prints(X[q, g:g + 1], P[q, g:g + 1, :1])[0, :, 0]
            if z == 4:
                V[q, g][:, 0] = 512; V[q, g][:, int(place(np.int64(top)))] = 512
                F = prints(X[q, g:g + 1], P[q, g:g + 1, 1:2]); V[q, g][:, int(slots(F, w[q, g:g + 1])[1][0, 0])] = F[0, :, 0]
            if z == 5:
                F = prints(X[q, g:g + 1], P[q, g:g + 1]); h = slots(F, w[q, g:g + 1])[1]
                V[q, g][:, h[0]] = near(rng, F, 2, 12)[0]
            if z == 6:
                F = prints(X[q, g:g + 1], flip(P[q, g:g + 1], np.maximum(s[q, g:g + 1], 1)))[:, :, C >> 1:]; h = slots(F, w[q, g:g + 1])[1][:, :]
                o = np.argsort(rng.random(F.shape), axis=1)
                V[q, g][:, h[0]] = np.where(o < rng.integers(11, 13, (1, 1, F.shape[2])), F, 512)[0]
    return pack(X, V, P, s, w)
def setup_inputs_crowd(rng):
    X, w, P, s = parts(rng); V = junk(rng, 0.2); w[:, :, 3] = 1 + 2 * rng.integers(0, 8, (N, 8))
    for g in range(8):
        root = rng.integers(0, WX, K); m = int(rng.integers(1, K)); mc = rng.integers(1, K, (N, C))
        if g in (0, 2, 4): P[:, g] = root; s[:, g] = rng.integers(0, K, (N, C)) if g == 4 else m
        if g == 2: P[:, g, C - 1] = rng.integers(0, WX, K)
        if g == 3: P[:, g, 0::2] = root; P[:, g, 1::2] = flip(root, m); s[:, g] = m
        if g in (5, 7): P[:, g] = flip(np.broadcast_to(root, (N, C, K)), mc); s[:, g] = mc
        if g in (1, 6): P[:, g] = int(rng.integers(0, WX))
        if g == 6: P[:, g, 0] = rng.integers(0, WX, K)
        if g == 1:
            P[1::2, g] = rng.integers(0, WX, P[1::2, g].shape); s[1::2, g] = rng.integers(1, K, s[1::2, g].shape)
            for q in range(0, N, 2):
                r = (q - 1) % N; F = prints(X[q, g:g + 1], P[r, g:g + 1]); h = slots(F, w[q, g:g + 1])[1]
                V[q, g][:, h[0]] = near(rng, F, rng.integers(3, 6, (1, 1, C)), rng.integers(12, 17, (1, 1, C)))[0]
        if g == 2:
            for q in range(N):
                F = prints(X[q, g:g + 1], flip(np.broadcast_to(root, (1, K - 1, K)), np.arange(1, K)[None, :])); h = slots(F, w[q, g:g + 1])[1]
                V[q, g][:, h[0]] = near(rng, F, 5, 12)[0]
        if g in (1, 6, 7):
            for q in range(N):
                Q = root if g == 7 else P[0, g, C - 1]
                F = prints(X[q, g:g + 1], Q.reshape(1, 1, K)); h = int(slots(F, w[q, g:g + 1])[1][0, 0])
                V[q, g][:, h] = 512 if g == 1 and q & 1 else F[0, :, 0]
    return pack(X, V, P, s, w)
def setup_inputs_kin(rng):
    X, w, P, s = parts(rng)
    for q in range(1, N):
        o = rng.permutation(C); P[q] = P[0][:, o]; s[q] = s[0][:, o]
    return pack(X, np.full((N, 8, 16, WV), 512), P, s, w)
def check_inputs(d):
    bad = []
    for k, lo, hi in (("x", 0, 255), ("v", 0, 512), ("lanes", 0, WX - 1), ("s0", 0, K - 1), ("wt", 0, 15)):
        a = np.asarray(d[k]).astype(np.float64)
        if not np.all((a >= lo) & (a <= hi) & (a == np.floor(a))): bad.append("range of " + k)
    a = np.asarray(d["v"]).astype(np.float64)
    if np.any((a > 255) & (a < 512)): bad.append("v between 255 and 512")
    return bad
def visit(X, V, P, s, w, A):
    a = np.take_along_axis(X, P.reshape(8, 1, C * K), 2).reshape(8, 16, C, K); k = np.arange(K, dtype=np.int32)
    ak = np.add.accumulate(a * k, axis=3, dtype=np.int32); b = np.add.accumulate(a, axis=3, dtype=np.int32)
    F = np.ascontiguousarray(((ak[..., K - 1:] - 2 * ak + k * b) & 255)[..., 1:])
    u, h = slots(F.reshape(8, 16, C * (K - 1)), w)
    D = np.abs(np.take_along_axis(V, h[:, None, :], 2).reshape(F.shape) - F)
    u = u.reshape(8, C, K - 1); h = h.reshape(8, C, K - 1)
    close = D <= (2 + (A & 3)).reshape(8, 1, 1, 1)
    seen = np.add.reduce(close, axis=1, dtype=np.int32) >= TH
    far = np.add.reduce(D, axis=1, dtype=np.int32)
    i = np.argmin(np.where(seen, K, (np.arange(1, K) - s[:, :, None]) & (K - 1)), axis=2); go = np.logical_not(np.all(seen, axis=2))
    hc = np.take_along_axis(h, i[:, :, None], 2)[:, :, 0]; won = np.zeros((8, C), bool)
    for g in range(8):
        c = np.flatnonzero(go[g]); c = c[np.unique(hc[g, c], return_index=True)[1]]
        won[g, c] = True; V[g][:, hc[g, c]] = F[g][:, c, i[g, c]]
    su = np.take_along_axis(u, np.argmin(far, axis=2)[:, :, None], 2)[:, :, 0] & (K - 1)
    return np.where(won[:, :, None], flip(P, i + 1), P), np.where(won, s, su), C - np.add.reduce(won, axis=1, dtype=np.int64)
def reference(x, v, lanes, s0, wt):
    X = x.astype(np.float32).astype(np.int32).reshape(N, 8, 16, WX); V = v.astype(np.float32).astype(np.int32).reshape(N, 8, 16, WV)
    P = np.stack([gentries(a) for a in lanes]).astype(np.int64).reshape(N, 8, C, K); s = s0.astype(np.int64); w = wt.astype(np.int32).reshape(N, 8, 16)
    A = np.zeros((N, 8), np.int64)
    for t in range(RO):
        for q in range(N):
            r = (q - t) % N
            P[r], s[r], A[q] = visit(X[q], V[q], P[r], s[r], w[q], A[q])
    return {"yl": np.stack([gtable(a.reshape(8, C * K)) for a in P]).astype(np.float32), "ys": s.astype(np.float32), "yv": V.reshape(N, 128, WV).astype(np.float32).astype(BF)}

@@ -1,0 +1,606 @@
+import numpy as np
+from concourse.mybir import dt, AluOpType, AxisListType, ActivationFunctionType
+
+A = AluOpType
+AF = ActivationFunctionType
+STEPS = 4
+ROT = 712
+BIG = float(2 ** 23)
+SW = 160
+
+SCRATCH = {
+    "xs": ("sbuf", [128, 2048], "bfloat16"),
+    "vm": ("sbuf", [128, 2304], "bfloat16"),
+    "li": ("sbuf", [128, 256], "int32"),
+    "sraw": ("sbuf", [128, 256], "int32"),
+    "sbf": ("sbuf", [128, 256], "bfloat16"),
+    "wi": ("sbuf", [128, 8], "int32"),
+    "lb": ("sbuf", [128, 8 * SW], "uint16"),
+    "snd": ("sbuf", [128, 8 * SW], "uint16"),
+    "fo": ("sbuf", [128, 512], "float32"),
+    "fl": ("sbuf", [128, 512], "float32"),
+    "pint": ("sbuf", [128, 8], "int32"),
+    "pcol": ("sbuf", [128, 16], "float32"),
+    "ion": ("sbuf", [128, 144], "float32"),
+    "kio": ("sbuf", [128, 256], "float32"),
+    "r16": ("sbuf", [128, 128], "float32"),
+    "idb": ("sbuf", [128, 128], "bfloat16"),
+    "bob": ("sbuf", [128, 128], "bfloat16"),
+    "boh": ("sbuf", [128, 128], "float16"),
+    "bof": ("sbuf", [128, 8], "float32"),
+    "diag": ("sbuf", [128, 128], "float32"),
+    "mc": ("sbuf", [128, 128], "float32"),
+    "m16": ("sbuf", [128, 128], "bfloat16"),
+    "m15": ("sbuf", [128, 240], "float32"),
+    "otmp": ("sbuf", [128, 8], "float32"),
+    "otmi": ("sbuf", [128, 8], "int32"),
+    "rbig": ("sbuf", [128, 240], "float32"),
+    "r01": ("sbuf", [128, 128], "float32"),
+    "zw": ("sbuf", [128, 144], "bfloat16"),
+    "zc": ("sbuf", [128, 144], "bfloat16"),
+    "zs": ("sbuf", [128, 144], "bfloat16"),
+    "c3": ("sbuf", [128, 64], "bfloat16"),
+    "zf": ("sbuf", [128, 144], "float16"),
+    "cf": ("sbuf", [128, 48], "float32"),
+    "coef": ("sbuf", [128, 128], "float16"),
+    "ee": ("sbuf", [128, 256], "float32"),
+    "pm": ("sbuf", [128, 2048], "float16"),
+    "ofc": ("sbuf", [128, 48], "uint16"),
+    "wrow": ("sbuf", [128, 128], "float32"),
+    "wd0": ("sbuf", [128, 128], "float32"),
+    "thr": ("sbuf", [128, 128], "float32"),
+    "wsc": ("sbuf", [128, 128], "float32"),
+    "base": ("sbuf", [128, 64], "int32"),
+    "tol": ("sbuf", [128, 8], "float32"),
+    "toli": ("sbuf", [128, 8], "int32"),
+    "a": ("sbuf", [128, 4096], "bfloat16"),
+    "at": ("sbuf", [128, 4096], "float16"),
+    "q": ("sbuf", [128, 2048], "bfloat16"),
+    "f0": ("sbuf", [128, 2048], "bfloat16"),
+    "f1": ("sbuf", [128, 2048], "bfloat16"),
+    "d": ("sbuf", [128, 4096], "float16"),
+    "ab": ("sbuf", [128, 4096], "float16"),
+    "cl": ("sbuf", [128, 4096], "bfloat16"),
+    "tt0": ("sbuf", [128, 1024], "float32"),
+    "tt1": ("sbuf", [128, 1024], "float32"),
+    "eq": ("sbuf", [128, 17 * 128], "bfloat16"),
+    "fs": ("sbuf", [128, 256], "bfloat16"),
+    "lh": ("sbuf", [128, 256], "float16"),
+    "ui": ("sbuf", [128, 256], "int32"),
+    "u2": ("sbuf", [128, 256], "int32"),
+    "yy": ("sbuf", [128, 256], "float32"),
+    "sq": ("sbuf", [128, 256], "int32"),
+    "h0": ("sbuf", [128, 256], "int32"),
+    "h16": ("sbuf", [128, 256], "uint16"),
+    "ul": ("sbuf", [128, 256], "int32"),
+    "um": ("sbuf", [128, 256], "bfloat16"),
+    "t1": ("sbuf", [128, 256], "int32"),
+    "t2": ("sbuf", [128, 256], "int32"),
+    "b2": ("sbuf", [128, 256], "float32"),
+    "sc": ("sbuf", [128, 512], "float32"),
+    "rb": ("sbuf", [128, 256], "float16"),
+    "rs": ("sbuf", [128, 256], "bfloat16"),
+    "hb": ("sbuf", [128, 256], "float16"),
+    "wd": ("sbuf", [128, 256], "float32"),
+    "ws0": ("sbuf", [128, 128], "bfloat16"),
+    "ws1": ("sbuf", [128, 128], "bfloat16"),
+    "gi": ("sbuf", [128, 256], "int32"),
+    "lp": ("sbuf", [128, 256], "int32"),
+    "sn": ("sbuf", [128, 32], "float32"),
+    "hx": ("sbuf", [128, 16], "float32"),
+    "ti": ("sbuf", [128, 128], "int32"),
+    "dl": ("sbuf", [128, 64], "int32"),
+    "xa": ("sbuf", [128, 64], "float32"),
+    "xb": ("sbuf", [128, 64], "float32"),
+    "pt": ("psum", [128, 1024], "bfloat16"),
+    "pf0": ("psum", [128, 512], "float32"),
+    "pf1": ("psum", [128, 512], "float32"),
+    "pf2": ("psum", [128, 512], "float32"),
+    "pf3": ("psum", [128, 512], "float32"),
+    "pu": ("psum", [128, 512], "float32"),
+    "pc": ("psum", [128, 512], "float32"),
+    "pd": ("psum", [128, 512], "float32"),
+}
+DMA_SEMS = ["dx0", "dx1", "dl", "dw", "ds", "dv0", "dv1", "o0", "o1", "o2", "o3", "o4", "o5"]
+SEMAPHORES = ["cv", "ca", "cp", "cg", "sent"] + DMA_SEMS + ["arr%d" % i for i in range(8)]
+
+CYC = 0.83e-3 * 1.2
+GAT = 1.5
+NENG = 8
+ORDER = [("a", 0), ("b", 0), ("t", 0), ("d", 0), ("a", 1), ("t", 1), ("b", 1), ("w", 0), ("d", 1), ("w", 1)]
+V_GATHER = [(0, 0, 1, 1)] + [(t, h, 0, 1) for t in range(STEPS) for h in range(2)]
+V_TURN = [(0, 0, 0), (0, 0, 1)]
+A_NEAR = [(t, h, 0) for t in range(STEPS) for h in range(2)]
+A_MOD = []
+A_MARK = [(t, h, 1) for t in range(STEPS) for h in range(2)]
+BANKS = {"a": [[0, 1]] * 2, "t": [[2]] * 2, "m": [[3]] * 2}
+SEEDS = [46]
+ROUNDS = 4
+PLAN = {}
+
+
+def build_ops(g, core, T, topo, rank):
+    V, S, P = g.vector, g.scalar, g.tensor
+    ops = []
+    pr = [0]
+    nxt = T.cores[(rank + 1) % len(T.cores)]
+    rid, pid = topo.addr(nxt, core)
+    eng = topo.engines(core, nxt)[:NENG]
+    msk = sum(1 << e for e in eng)
+
+    def op(e, fn, R, W, dur, sem=None, val=0):
+        ops.append({"pr": pr[0], "e": e, "fn": fn, "R": list(R), "W": list(W), "dur": dur, "sem": sem, "val": val})
+
+    def vd(n, c=1.0):
+        return 0.03 + max(64, n * c) * CYC
+
+    def vop(fn, R, W, n, c=1.0):
+        op("v", lambda: [fn()], R, W, vd(n, c))
+
+    def aop(fn, R, W, n, c=1.0):
+        op("a", lambda: [fn()], R, W, 0.06 + max(64, n * c) * CYC)
+
+    def pop(fns, R, W, cyc):
+        op("p", lambda: [f() for f in fns], R, W, 0.08 + cyc * 0.42e-3 * 1.2)
+
+    def gop(fn, R, W, n):
+        op("g", lambda: [fn()], R, W, 0.15 + 2 * n * CYC)
+
+    def dma(out, in_, R, W, sem, dur, e="s"):
+        q = g.sync if e == "s" else g.scalar
+        op(e, lambda: [q.dma_start(out, in_)], R, W, dur, sem, 16)
+
+    def ts(out, in0, s1, s2, o0, o1, R, W, n, c=1.0):
+        if o1 is None:
+            vop(lambda: V.tensor_scalar(out, in0, s1, None, o0), R, W, n, c)
+        else:
+            vop(lambda: V.tensor_scalar(out, in0, s1, s2, o0, o1), R, W, n, c)
+
+    def tt(out, in0, in1, o, R, W, n, c=2.0):
+        vop(lambda: V.tensor_tensor(out, in0, in1, o), R, W, n, c)
+
+    def cp(out, in_, R, W, n, c=1.0):
+        vop(lambda: V.tensor_copy(out, in_), R, W, n, c)
+
+    def act(out, in_, fn, R, W, n, c=1.0, bias=0.0, scale=1.0):
+        aop(lambda: S.activation(out, in_, fn, bias=bias, scale=scale), R, W, n, c)
+
+    def mm(out, l, r, st, sp):
+        return lambda: P.matmul(out, l, r, st, sp)
+
+    dma(T.li[:], T.lanes[:], [], ["li"], "dl", 2.5)
+    dma(T.xs[:, 0:1024], T.x[:, 0:1024], [], ["xs0"], "dx0", 3.5)
+    dma(T.xs[:, 1024:2048], T.x[:, 1024:2048], [], ["xs1"], "dx1", 3.5, "a")
+    dma(T.wi[:, 0:1], T.wt[:], [], ["wi"], "dw", 2.5)
+    vop(lambda: V.memset(T.sraw[:], 0), [], ["sraw"], 256)
+    dma(T.sraw[0:128:16, :], T.s0[:], [], ["sraw"], "ds", 2.5)
+    dma(T.vm[:, ROT:2048], T.v[:, 0:2048 - ROT], [], ["vm"], "dv0", 4.5)
+    dma(T.vm[:, 0:ROT], T.v[:, 2048 - ROT:2048], [], ["vmb"], "dv1", 4.5)
+    XS = ["xs0", "xs1"]
+    VM = ["vm", "vmb"]
+
+    gop(lambda: g.iota(T.pint[:, 0:1], [[0, 1]], 0, 1), [], ["pi0"], 1)
+    gop(lambda: g.iota(T.ion[:], [[1, 144]], 0, 0, allow_small_or_imprecise_dtypes=True), [], ["ion"], 144)
+    gop(lambda: g.iota(T.r16[:], [[0, 8], [1, 16]], 0, 0, allow_small_or_imprecise_dtypes=True), [], ["r16"], 128)
+    gop(lambda: g.iota(T.kio[:], [[1, 16], [0, 16]], 0, 0, allow_small_or_imprecise_dtypes=True), [], ["kio"], 256)
+    ts(T.pint[:, 1:2], T.pint[:, 0:1], 15, None, A.bitwise_and, None, ["pi0"], ["pi1"], 1)
+    ts(T.pint[:, 2:3], T.pint[:, 0:1], 4, None, A.arith_shift_right, None, ["pi0"], ["pi2"], 1)
+    ts(T.pint[:, 3:4], T.pint[:, 0:1], 7, None, A.bitwise_and, None, ["pi0"], ["pi3"], 1)
+    ts(T.pint[:, 4:5], T.pint[:, 0:1], 1, 7, A.arith_shift_right, A.bitwise_and, ["pi0"], ["pi4"], 1)
+    cp(T.pcol[:, 0:5], T.pint[:, 0:5], ["pi0", "pi1", "pi2", "pi3", "pi4"], ["pc"], 5)
+    pP, pK, pG, p7, pH = (T.pcol[:, i:i + 1] for i in range(5))
+    pZ, pW = T.pcol[:, 5:6], T.pcol[:, 6:7]
+    ts(pZ, pG, 16.0, 15.0, A.mult, A.add, ["pc"], ["pz"], 1)
+    cp(pW, T.wi[:, 0:1], ["wi"], ["pw"], 1)
+    ts(T.idb[:], T.ion[:, 0:128], pP, None, A.is_equal, None, ["ion", "pc"], ["idb"], 128)
+    ts(T.bof[:], T.ion[:, 0:8], pG, None, A.is_equal, None, ["ion", "pc"], ["bof"], 8)
+    ts(T.cf[:, 16:32], T.r16[:, 0:16], pK, None, A.subtract, None, ["r16", "pc"], ["cf1"], 16)
+    ts(T.cf[:, 32:48], T.r16[:, 0:16], pK, pK, A.is_lt, A.mult, ["r16", "pc"], ["cf2"], 16)
+    tt(T.cf[:, 0:16], T.cf[:, 16:32], T.cf[:, 32:48], A.max, ["cf1", "cf2"], ["cf"], 16)
+    for r in range(8):
+        ts(T.coef[:, r:120:8], T.cf[:, 1:16], T.bof[:, r:r + 1], None, A.mult, None, ["cf", "bof"], ["coef%d" % r], 16)
+    COEF = ["coef%d" % r for r in range(8)]
+    ts(T.zw[:], T.ion[:], pZ, pW, A.is_equal, A.mult, ["ion", "pz", "pw"], ["zw"], 144)
+    ts(T.zc[:], T.ion[:], pZ, float(2 ** 20), A.is_equal, A.mult, ["ion", "pz"], ["zc"], 144)
+    ts(T.zf[:], T.ion[:], pZ, 256.0, A.is_equal, A.mult, ["ion", "pz"], ["zf"], 144)
+    ts(T.bob[:], T.kio[:, 0:128], pG, None, A.is_equal, None, ["kio", "pc"], ["bob"], 128)
+    act(T.boh[:], T.bob[:], AF.Copy, ["bob"], ["boh"], 128)
+    ts(T.diag[:], T.r16[:], pK, None, A.is_equal, None, ["r16", "pc"], ["diag"], 128)
+    gop(lambda: g.iota(T.m15[:], [[0, 16], [1, 15]], 1, 0, allow_small_or_imprecise_dtypes=True), [], ["m15"], 240)
+    act(T.mc[:], T.m15[:, 0:128], AF.Copy, ["m15"], ["mc"], 128, scale=float(2 ** 15 + 2 ** 11))
+    act(T.m16[:], T.m15[:, 0:128], AF.Copy, ["m15"], ["m16"], 128, scale=16.0)
+    ts(T.rbig[:], T.m15[:], 1.0, BIG, A.is_equal, A.mult, ["m15"], ["rbig"], 240)
+    offM = T.ofc[:, 32:40]
+    ts(T.otmp[:], T.ion[:, 0:128:16], pK, 1.0 / 15, A.add, A.mult, ["ion", "pc"], ["otmp"], 8)
+    ts(T.otmi[:], T.otmp[:], -0.47, None, A.add, None, ["otmp"], ["otmi"], 8)
+    ts(offM, T.otmi[:], 7.0, None, A.min, None, ["otmi"], ["offM"], 8)
+    for h in range(2):
+        vop(lambda h=h: V.memset(T["f%d" % h][:, 0:16], 0.0), [], ["fz%d" % h], 16)
+    act(T.r01[:], T.r16[:], AF.Sign, ["r16"], ["r01"], 128)
+    offE, offW, offK = T.ofc[:, 0:8], T.ofc[:, 8:10], T.ofc[:, 16:32]
+    cp(offE, T.ion[:, 0:8], ["ion"], ["offE"], 8)
+    ts(T.pcol[:, 7:8], p7, 16.0, 15.0, A.mult, A.add, ["pc"], ["pw7"], 1)
+    ts(offW, T.ion[:, 0:2], 0.0, T.pcol[:, 7:8], A.mult, A.add, ["ion", "pw7"], ["offW"], 2)
+    ts(offK, T.ion[:, 0:16], 0.0, pK, A.mult, A.add, ["ion", "pc"], ["offK"], 16)
+    tt(T.ee[:], T.cf[:, 0:16].indirect(offK), T.kio[:], A.is_equal, ["cf", "offK", "kio"], ["ee"], 256, GAT)
+    for r in range(8):
+        act(T.pm[:, r * 256:(r + 1) * 256], T.ee[:], AF.Copy, ["ee", "bof"], ["pm%d" % r], 256, scale=T.bof[:, r:r + 1])
+    PM = ["pm%d" % r for r in range(8)]
+    vop(lambda: V.memset(T.wd0[:], 0.5), [], ["wd0"], 128)
+    vop(lambda: V.memset(T.thr[:], 0.0), [], ["thr"], 128)
+    vop(lambda: V.tensor_tensor_scan(T.wrow[:], T.wd0[:], T.thr[:], float(2 ** 61), A.mult, A.add), ["wd0", "thr"], ["wrow"], 128)
+    tt(T.wd0[:], T.wrow[:], T.diag[:], A.mult, ["wrow", "diag"], ["wd0"], 128)
+    act(T.thr[:], T.wd0[:], AF.Copy, ["wd0"], ["thr"], 128, scale=2.5)
+    vop(lambda: V.tensor_tensor_scan(T.wsc[:], T.r01[:], T.wd0[:], 0.0, A.mult, A.add), ["r01", "wd0"], ["wsc"], 128)
+    for h in range(2):
+        b = h * 32
+        ts(T.base[:, b:b + 8], T.ion[:, 0:8], 8.0, pH, A.mult, A.add, ["ion", "pc"], ["baseT%d" % h], 8)
+        ts(T.base[:, b + 8:b + 16], T.ion[:, 0:128:16], pK, 2048.0 + 128 * h, A.add, A.add, ["ion", "pc"], ["baseS%d" % h], 8)
+        ts(T.base[:, b + 24:b + 32], T.ion[:, 0:8], 240.0, pK, A.mult, A.add, ["ion", "pc"], ["baseF%d" % h], 8)
+    vop(lambda: V.memset(T.tol[:, 0:1], 2.5), [], ["tol"], 1)
+    vop(lambda: V.memset(T.c3[:], -3.0 * 2 ** 20), [], ["c3"], 64)
+    act(T.zs[:], T.zc[:], AF.Copy, ["zc"], ["zs"], 144, scale=0.5)
+
+    for h in range(2):
+        for b in range(2):
+            cp(T.lb[:, h * SW + b * 64:h * SW + b * 64 + 64], T.li[:, h * 128 + b:h * 128 + 128:2], ["li"], ["lb0%d" % h], 64)
+    cp(T.sbf[:], T.sraw[:], ["sraw"], ["sbf"], 256)
+    pop([mm(T.pd[:, 0:16], T.zc[:, 15 - r:143 - r], T.sbf[:, r:256:16], r == 0, r == 15) for r in range(16)],
+        ["zc", "sbf"], ["pd"], 16 * 64)
+    for h in range(2):
+        ts(T.lb[:, h * SW + 144:h * SW + 152], T.pd[:, h * 8:h * 8 + 8], 2.0 ** -20, None, A.mult, None, [], ["pd", "ls0%d" % h], 8)
+
+    bank = {}
+    FB = [T.f0, T.f1]
+    TB = [T.tt0, T.tt1]
+    WS = [T.ws0, T.ws1]
+
+    def nb(kind, h):
+        ring = BANKS[kind][h]
+        key = tuple(ring)
+        bank[key] = (bank.get(key, -1) + 1) % len(ring)
+        return ring[bank[key]]
+
+    def stage_a(t, h):
+        lo = (t * 2 + h) * SW
+        LB = "lb%d%d" % (t, h)
+        F = FB[h]
+        o = h * 2048
+        for Q in range(2):
+            for b in range(2):
+                c0 = b * 64 + Q * 32
+                out, src = T.a[:, o + c0 * 16:o + c0 * 16 + 512], T.xs[:, 0:2048].indirect(T.lb[:, lo + c0:lo + c0 + 32])
+                if (t, h, Q, b) in V_GATHER:
+                    cp(out, src, XS + [LB], ["a%d%d%d" % (h, Q, b)], 512, GAT)
+                else:
+                    act(out, src, AF.Copy, XS + [LB], ["a%d%d%d" % (h, Q, b)], 512, GAT)
+            fns = []
+            for el in range(4):
+                for b in range(2):
+                    c = o + (b * 8 + Q * 4 + el) * 128
+                    fns.append(lambda c=c, j=el * 2 + b: P.transpose(T.pt[:, j * 128:(j + 1) * 128], T.a[:, c:c + 128], T.idb[:]))
+            pop(fns, ["a%d%d0" % (h, Q), "a%d%d1" % (h, Q), "idb"], ["pt"], 1024)
+            ao = o + Q * 1024
+            if (t, h, Q) in V_TURN:
+                ts(T.at[:, ao:ao + 1024], T.pt[:], 288.0, None, A.add, None, [], ["pt", "at%d%d" % (h, Q)], 1024, 0.5)
+            else:
+                act(T.at[:, ao:ao + 1024], T.pt[:], AF.Identity, [], ["pt", "at%d%d" % (h, Q)], 1024, bias=288.0)
+            for n2 in range(2):
+                n = Q * 2 + n2
+                k = nb("a", h)
+                pf = T["pf%d" % k]
+                fns = []
+                for j in range(4):
+                    c = ao + (n2 * 4 + j) * 128
+                    s = (j >> 1) * 240
+                    fns.append(mm(pf[:, s + (j & 1):s + 240:2], T.at[:, c:c + 128], T.coef[:, 0:120], j == 0, j == 3))
+                pop(fns, ["at%d%d" % (h, Q)] + COEF, ["pf%d" % k], 480)
+                qq = T.q[:, k * 512:k * 512 + 480]
+                act(qq, pf[:, 0:480], AF.Identity, [], ["pf%d" % k, "q%d" % k], 480, bias=127.5, scale=-1.0)
+                if (t, h, n) in A_MOD:
+                    fns = [mm(pf[:, 0:480], T.idb[:], qq, True, False)]
+                    for j in range(4):
+                        c = ao + (n2 * 4 + j) * 128
+                        s = (j >> 1) * 240
+                        fns.append(mm(pf[:, s + (j & 1):s + 240:2], T.at[:, c:c + 128], T.coef[:, 0:120], False, j == 3))
+                    pop(fns, ["at%d%d" % (h, Q), "q%d" % k, "idb"] + COEF, ["pf%d" % k], 960)
+                    act(F[:, 16 + n * 480:496 + n * 480], pf[:, 0:480], AF.Copy, [], ["pf%d" % k, "f%d%d" % (h, n)], 480)
+                else:
+                    tt(F[:, 16 + n * 480:496 + n * 480], pf[:, 0:480], qq, A.add, ["q%d" % k], ["pf%d" % k, "f%d%d" % (h, n)], 480, 1.0)
+            pop([mm(T.pu[:, Q * 60:Q * 60 + 60], T.zw[:, 15 - r:143 - r], F[:, 16 + Q * 960 + r:976 + Q * 960:16], r == 0, r == 15)
+                 for r in range(16)], ["zw", "f%d%d" % (h, 2 * Q), "f%d%d" % (h, 2 * Q + 1)], ["pu"], 1024)
+            c = slice(h * 128 + Q * 60, h * 128 + Q * 60 + 60)
+            H = "%d%d" % (h, Q)
+            cp(T.ui[:, c], T.pu[:, Q * 60:Q * 60 + 60], [], ["pu", "ui" + H], 60)
+            ts(T.u2[:, c], T.ui[:, c], 4095, None, A.bitwise_and, None, ["ui" + H], ["u2" + H], 60)
+            ts(T.yy[:, c], T.u2[:, c], 592.0, None, A.add, None, ["u2" + H], ["yy" + H], 60)
+            tt(T.sq[:, c], T.yy[:, c], T.yy[:, c], A.mult, ["yy" + H], ["sq" + H], 60)
+            ts(T.h0[:, c], T.sq[:, c], 5, 2047, A.arith_shift_right, A.bitwise_and, ["sq" + H], ["h0" + H], 60)
+            cp(T.h16[:, c], T.h0[:, c], ["h0" + H], ["h16" + H], 60)
+        c = slice(h * 128, h * 128 + 120)
+        H = str(h)
+        ts(T.ul[:, c], T.ui[:, c], 15, None, A.bitwise_and, None, ["ui%d0" % h, "ui%d1" % h], ["ul" + H], 120)
+        cp(T.um[:, c], T.ul[:, c], ["ul" + H], ["um" + H], 120)
+        LS = ("ls%d%d" if t == 0 else "lb%d%d") % (t, h)
+        sN, sF = T.sn[:, h * 16:h * 16 + 8], T.sn[:, h * 16 + 8:h * 16 + 16]
+        ts(sN, T.lb[:, lo + 144:lo + 152], -32768.0, None, A.mult, None, [LS], ["sN" + H], 8)
+        cp(sF, T.lb[:, lo + 144:lo + 152], [LS], ["sF" + H], 8)
+        tt(T.t1[:, h * 128:h * 128 + 128], sN.indirect(offM), T.mc[:], A.add, ["sN" + H, "offM", "mc"], ["t1" + H], 128, GAT)
+        ts(T.t2[:, c], T.t1[:, c], 0xFFFFF, None, A.bitwise_and, None, ["t1" + H], ["t2" + H], 120)
+        tt(T.b2[:, c], T.t2[:, c], T.h0[:, c], A.add, ["t2" + H, "h0%d0" % h, "h0%d1" % h], ["b2" + H], 120)
+
+    def stage_t(t, h):
+        lo = (t * 2 + h) * SW
+        LB = "lb%d%d" % (t, h)
+        H = str(h)
+        o = h * 128
+        ts(T.lh[:, o:o + 64], T.lb[:, lo:lo + 64], 1.0 / 2048, None, A.mult, None, [LB], ["lh0" + H], 64, 0.5)
+        ts(T.lh[:, o + 64:o + 128], T.lb[:, lo + 64:lo + 128], 1.0, None, A.mult, None, [LB], ["lh1" + H], 64, 0.5)
+        for n in range(2):
+            k = nb("t", h)
+            pf = T["pf%d" % k]
+            fns = []
+            for m in range(8):
+                for b in range(2):
+                    fns.append(mm(pf[:, m * 64:m * 64 + 64], T.pm[:, n * 8 + m:2048:16], T.lh[:, o + b * 64:o + b * 64 + 64], b == 0, b == 1))
+            pop(fns, PM + ["lh0" + H, "lh1" + H], ["pf%d" % k], 1024)
+            act(TB[h][:, n * 512:(n + 1) * 512], pf[:], AF.Copy, [], ["pf%d" % k, "tt%d%d" % (h, n)], 512, scale=2048.0)
+
+    def stage_b(t, h):
+        F = FB[h]
+        H = str(h)
+        o = h * 2048
+        for Q in range(2):
+            for n in (2 * Q, 2 * Q + 1):
+                c = slice(o + n * 480, o + n * 480 + 480)
+                K = "%d%d" % (h, n)
+                if (t, h, n) in A_MARK:
+                    k = nb("m", h)
+                    pf = T["pf%d" % k]
+                    mk = T.q[:, k * 512:k * 512 + 480]
+                    act(mk, T.vm[:, 0:2048].indirect(T.h16[:, h * 128 + n * 30:h * 128 + n * 30 + 30]), AF.Copy,
+                        VM + ["h16%d%d" % (h, Q)], ["q%d" % k], 480, GAT, scale=-1.0)
+                    pop([mm(pf[:, 0:480], T.idb[:], F[:, 16 + n * 480:496 + n * 480], True, False), mm(pf[:, 0:480], T.idb[:], mk, False, True)],
+                        ["idb", "q%d" % k, "f" + K], ["pf%d" % k], 960)
+                    act(T.ab[:, c], pf[:, 0:480], AF.Abs, [], ["pf%d" % k, "ab" + K], 480)
+                    continue
+                tt(T.d[:, c], T.vm[:, 0:2048].indirect(T.h16[:, h * 128 + n * 30:h * 128 + n * 30 + 30]), F[:, 16 + n * 480:496 + n * 480],
+                   A.subtract, VM + ["h16%d%d" % (h, Q), "f" + K], ["d" + K], 480, GAT)
+                act(T.ab[:, c], T.d[:, c], AF.Abs, ["d" + K], ["ab" + K], 480)
+            s = o + Q * 960
+            K2 = ["%d%d" % (h, 2 * Q), "%d%d" % (h, 2 * Q + 1)]
+            sign = (t, h, Q) in A_NEAR
+            if sign:
+                act(T.cl[:, s:s + 960], T.ab[:, s:s + 960], AF.Sign, ["tol"] + ["ab" + k for k in K2], ["cl%d%d" % (h, Q)], 960,
+                    bias=T.tol[:, 0:1], scale=-1.0)
+            else:
+                ts(T.cl[:, s:s + 960], T.ab[:, s:s + 960], T.tol[:, 0:1], -0.6875, A.is_le, A.add, ["tol"] + ["ab" + k for k in K2],
+                   ["cl%d%d" % (h, Q)], 960, 0.5)
+            far = T.pc[:, 120 + Q * 60:180 + Q * 60]
+            pop([mm(far, T.zf[:, 15 - r:143 - r], T.ab[:, s + r:s + 960:16], r == 0, False) for r in range(16)]
+                + [mm(far, T.idb[:], T.m16[:, 0:60], False, False),
+                   mm(far, T.idb[:], T.um[:, h * 128 + Q * 60:h * 128 + Q * 60 + 60], False, True)],
+                ["zf", "idb", "m16", "um" + H] + ["ab" + k for k in K2], ["pc"], 1152)
+            cnt = T.pc[:, Q * 60:Q * 60 + 60]
+            if sign:
+                pop([mm(cnt, T.idb[:], T.c3[:, 0:60], True, False)]
+                    + [mm(cnt, T.zs[:, 15 - r:143 - r], T.cl[:, s + r:s + 960:16], False, r == 15) for r in range(16)],
+                    ["zs", "c3", "idb", "cl%d%d" % (h, Q)], ["pc"], 1088)
+            else:
+                pop([mm(cnt, T.zc[:, 15 - r:143 - r], T.cl[:, s + r:s + 960:16], r == 0, r == 15) for r in range(16)],
+                    ["zc", "cl%d%d" % (h, Q)], ["pc"], 1024)
+        tt(T.pc[:, 0:120], T.pc[:, 0:120], T.b2[:, h * 128:h * 128 + 120], A.max, ["b2" + H], ["pc"], 120, 1.0)
+        vop(lambda: V.tensor_tensor_scan(T.sc[:, h * 256:h * 256 + 240], T.rbig[:], T.pc[:, 0:240], 0.0, A.add, A.min), ["rbig"], ["pc", "sc" + H], 240)
+
+    def stage_d(t, h):
+        H = str(h)
+        c = slice(h * 128, h * 128 + 128)
+        ti = lambda j: T.ti[:, h * 64 + j * 8:h * 64 + j * 8 + 8]
+        hx = T.hx[:, h * 8:h * 8 + 8]
+        sF = T.sn[:, h * 16 + 8:h * 16 + 16]
+        b = h * 32
+        cp(T.ti[:, h * 64:h * 64 + 16], T.sc[:, h * 256 + 14:h * 256 + 240:15], ["sc" + H], ["ki" + H], 16)
+        ts(ti(2), ti(0), 0x7007FF, None, A.bitwise_and, None, ["ki" + H], ["hi" + H], 8)
+        ts(hx, ti(2), 2048.0, None, A.min, None, ["hi" + H], ["hx" + H], 8)
+        tt(T.rb[:, c], hx.indirect(offE), T.diag[:], A.mult, ["hx" + H, "offE", "diag"], ["rb" + H], 128, GAT)
+        pop([mm(T.pd[:, 0:128], T.boh[:], T.rb[:, c], True, True)], ["boh", "rb" + H], ["pd"], 128)
+        cp(T.hb[:, c], T.pd[:, 0:128], [], ["pd", "hb" + H], 128)
+        ne = 9 if h == 0 else 17
+        for j in range(ne):
+            out = T.eq[:, j * 128:(j + 1) * 128]
+            if j < 8:
+                ts(out, T.hb[:, c], T.hx[:, h * 8 + j:h * 8 + j + 1], T.wsc[:, j * 16 + 15:j * 16 + 16], A.is_equal, A.mult,
+                   ["hb" + H, "hx" + H, "wsc"], ["eq%d" % j], 128, 0.5)
+            elif j == 8:
+                ts(out, T.hb[:, c], 2048.0, float(2 ** 62), A.is_equal, A.mult, ["hb" + H], ["eq%d" % j], 128, 0.5)
+            else:
+                ts(out, T.hb[:, c], T.hx[:, j - 9:j - 8], float(2 ** 62), A.is_equal, A.mult, ["hb" + H, "hx0"], ["eq%d" % j], 128, 0.5)
+        grp = [list(range(0, 5)), list(range(5, 9))] + ([list(range(9, 13)), list(range(13, 17))] if h else [])
+        for gi_, js in enumerate(grp):
+            pop([mm(T.pd[:, 128:256], T.bob[:], T.eq[:, j * 128:(j + 1) * 128], j == 0, j == ne - 1) for j in js],
+                ["bob"] + ["eq%d" % j for j in js], ["pd"], 128 * len(js))
+        ts(T.dl[:, b:b + 8], ti(0), 5, 15 * 64, A.arith_shift_right, A.bitwise_and, ["ki" + H], ["dlT" + H], 8)
+        ts(T.dl[:, b + 24:b + 32], ti(0), 7, 15 * 16, A.arith_shift_right, A.bitwise_and, ["ki" + H], ["dlF" + H], 8)
+        tt(T.dl[:, b + 8:b + 16], hx, T.base[:, b + 8:b + 16], A.subtract, ["hx" + H, "baseS" + H], ["dlS" + H], 8)
+        ts(T.base[:, b + 16:b + 24], ti(1), 15, None, A.bitwise_and, None, ["ki" + H], ["bases" + H], 8)
+        tt(T.dl[:, b + 16:b + 24], sF, T.base[:, b + 16:b + 24], A.subtract, ["sF" + H, "bases" + H], ["dls" + H], 8)
+        tt(T.wd[:, c], T.pd[:, 128:256], T.thr[:], A.is_lt, ["thr"], ["pd", "wd" + H], 128, 1.0)
+        vop(lambda: V.tensor_tensor_scan(WS[h][:], T.r01[:], T.wd[:, c], 0.0, A.mult, A.add), ["r01", "wd" + H], ["ws" + H], 128)
+        tt(T.xa[:, b:b + 32], WS[h][:, 0:128].indirect(offW), T.dl[:, b:b + 32], A.mult,
+           ["ws" + H, "offW", "dlT" + H, "dlF" + H, "dlS" + H, "dls" + H], ["xa" + H], 32, GAT)
+        tt(T.xb[:, b:b + 32], T.xa[:, b:b + 32], T.base[:, b:b + 32], A.add,
+           ["xa" + H, "baseT" + H, "baseS" + H, "baseF" + H, "bases" + H], ["xb" + H], 32)
+        so = (t * 2 + h) * SW
+        OF = "of%d%d" % (t, h)
+        cp(T.snd[:, so + 128:so + 160], T.xb[:, b:b + 32], ["xb" + H], [OF], 32)
+        cp(T.gi[:, c], TB[h][:, 0:1024].indirect(T.snd[:, so + 128:so + 136]), [OF, "tt%d0" % h, "tt%d1" % h], ["gi" + H], 128, GAT)
+        o = h * 128
+        arr = "arr%d" % (t * 2 + h)
+        if t < STEPS - 1:
+            ts(T.lp[:, o:o + 64], T.gi[:, o:o + 128:2], 2047, None, A.bitwise_and, None, ["gi" + H], ["lp0" + H], 64)
+            ts(T.lp[:, o + 64:o + 128], T.gi[:, o + 1:o + 128:2], 11, None, A.arith_shift_right, None, ["gi" + H], ["lp1" + H], 64)
+            cp(T.snd[:, so:so + 128], T.lp[:, c], ["lp0" + H, "lp1" + H], ["sl%d%d" % (t, h)], 128)
+            lo = so + 2 * SW
+            src, dst, R, W = T.snd[:, so:so + SW], T.lb[:, lo:lo + SW], [OF, "sl%d%d" % (t, h)], ["lb%d%d" % (t + 1, h)]
+        else:
+            ts(T.lp[:, o:o + 128:2], T.gi[:, o:o + 128:2], 2047, None, A.bitwise_and, None, ["gi" + H], ["lp0" + H], 64)
+            ts(T.lp[:, o + 1:o + 128:2], T.gi[:, o + 1:o + 128:2], 11, None, A.arith_shift_right, None, ["gi" + H], ["lp1" + H], 64)
+            cp(T.fo[:, h * 256:h * 256 + 128], T.lp[:, c], ["lp0" + H, "lp1" + H], ["foL" + H], 128)
+            tt(T.rs[:, c], T.xb[:, b + 16:b + 24].indirect(offE), T.diag[:], A.mult, ["xb" + H, "offE", "diag"], ["rsb" + H], 128, GAT)
+            pop([mm(T.pd[:, 0:128], T.bob[:], T.rs[:, c], True, True)], ["bob", "rsb" + H], ["pd"], 128)
+            act(T.fo[:, h * 256 + 128:h * 256 + 256], T.pd[:, 0:128], AF.Copy, [], ["pd", "foS" + H], 128)
+            src, dst, R, W = T.fo[:, h * 256:h * 256 + 256], T.fl[:, h * 256:h * 256 + 256], ["foL" + H, "foS" + H], ["fl" + H]
+        op("r", lambda: [g.remote_dma(dst, src, T.sem[arr], T.sem.sent, pid, rid, msk)], R, W, 4.0, arr, len(eng))
+        act(T.fs[:, c], FB[h][:, 0:1936].indirect(T.snd[:, so + 152:so + 160]), AF.Copy,
+            [OF, "fz" + H] + ["f%d%d" % (h, n) for n in range(4)], ["fs" + H], 128, GAT)
+        if t < STEPS - 1:
+            pop([mm(T.pd[:, 256 + h * 8:264 + h * 8], T.bob[:], WS[h][:, 15:128:16], True, True)], ["bob", "ws" + H], ["pd"], 64)
+
+    def stage_w(t, h):
+        so = (t * 2 + h) * SW
+        cp(T.vm[:, 0:2304].indirect(T.snd[:, so + 136:so + 144]), T.fs[:, h * 128:h * 128 + 128],
+           ["of%d%d" % (t, h), "fs%d" % h], VM, 128, 3.5)
+        if h == 1 and t < STEPS - 1:
+            vop(lambda: V.tensor_reduce(T.tol[:, 1:2], T.pd[:, 256:272], AxisListType.X, A.add, negate=True), [], ["pd", "tn"], 16)
+            cp(T.toli[:, 0:1], T.tol[:, 1:2], ["tn"], ["tni"], 1)
+            ts(T.toli[:, 1:2], T.toli[:, 0:1], 3, None, A.bitwise_and, None, ["tni"], ["tn3"], 1)
+            ts(T.tol[:, 0:1], T.toli[:, 1:2], 2.5, None, A.add, None, ["tn3"], ["tol"], 1)
+
+    for t in range(STEPS):
+        for fn, h in ORDER:
+            pr[0] += 1
+            {"a": stage_a, "b": stage_b, "t": stage_t, "d": stage_d, "w": stage_w}[fn](t, h)
+    pr[0] += 1
+
+    dma(T.yv[:, 0:2048 - ROT], T.vm[:, ROT:2048], VM, [], "o0", 4.0)
+    dma(T.yv[:, 2048 - ROT:2048], T.vm[:, 0:ROT], VM, [], "o1", 4.0, "a")
+    for h in range(2):
+        dma(T.yl[:, h * 128:h * 128 + 128], T.fl[:, h * 256:h * 256 + 128], ["fl%d" % h], [], "o%d" % (2 + h), 2.5)
+        dma(T.ys[:, h * 128:h * 128 + 128], T.fl[0:128:16, h * 256 + 128:h * 256 + 256], ["fl%d" % h], [], "o%d" % (4 + h), 2.5)
+    return ops, len(eng)
+
+
+def order_ops(ops):
+    n = len(ops)
+    lastw, readers = {}, {}
+    deps = []
+    for i, o in enumerate(ops):
+        d = set()
+        for k in o["R"]:
+            if k in lastw:
+                d.add(lastw[k])
+        for k in o["W"]:
+            if k in lastw:
+                d.add(lastw[k])
+            d.update(readers.get(k, []))
+        d.discard(i)
+        deps.append(sorted(d))
+        for k in o["R"]:
+            readers.setdefault(k, []).append(i)
+        for k in o["W"]:
+            lastw[k] = i
+            readers[k] = []
+    succ = [[] for _ in range(n)]
+    for i in range(n):
+        for j in deps[i]:
+            succ[j].append(i)
+    LAT = 0.08
+    lev = [0.0] * n
+    for i in range(n - 1, -1, -1):
+        lev[i] = ops[i]["dur"] + max([lev[j] + LAT for j in succ[i]], default=0.0)
+    queue = lambda o: "g" if o["e"] == "r" else o["e"]
+    hold = lambda o: (1.0 if o["e"] == "r" else 0.1) if o["sem"] else o["dur"]
+    qs = [queue(o) for o in ops]
+    hs = [hold(o) for o in ops]
+    pr = [o["pr"] for o in ops]
+    for i in range(n - 1, -1, -1):
+        if pr[i] == 0 and succ[i]:
+            pr[i] = min(pr[j] for j in succ[i])
+
+    dur = [o["dur"] for o in ops]
+
+    def place(rank_of, pre, post, back):
+        busy = {e: [] for e in "vapgs"}
+        left = [len(d) for d in pre]
+        ready = [(rank_of[i], i) for i in range(n) if left[i] == 0]
+        st = [0.0] * n
+        while ready:
+            ready.sort(reverse=True)
+            i = ready.pop()[1]
+            r = max([st[k] + dur[k] + LAT for k in pre[i]], default=0.0)
+            lead = dur[i] - hs[i] if back else 0.0
+            a = r + lead
+            lst = busy[qs[i]]
+            at = len(lst)
+            for x in range(len(lst)):
+                if lst[x][1] <= a:
+                    continue
+                if lst[x][0] >= a + hs[i]:
+                    at = x
+                    break
+                a = lst[x][1]
+            lst.insert(at, (a, a + hs[i]))
+            st[i] = a - lead
+            for j in post[i]:
+                left[j] -= 1
+                if left[j] == 0:
+                    ready.append((rank_of[j], j))
+        return st
+
+    best = None
+    for seed in SEEDS:
+        rng = np.random.default_rng(seed)
+        w, noise = rng.uniform(0.0, 8.0), rng.uniform(0.0, 1.0)
+        st = place([float(pr[i] * w - lev[i] + noise * rng.random()) for i in range(n)], deps, succ, False)
+        for rnd in range(ROUNDS):
+            span = max(st[i] + dur[i] for i in range(n))
+            if best is None or span < best[0]:
+                best = (span, st)
+            bk = place([-(st[i] + dur[i]) for i in range(n)], succ, deps, True)
+            st = place([-(bk[i] + dur[i]) for i in range(n)], deps, succ, False)
+    st = best[1]
+    return deps, sorted(range(n), key=lambda i: (st[i], i)), [st[i] + dur[i] for i in range(n)]
+
+
+def rank_program(g, core, T, topo):
+    rank = T.rank_of(core)
+    if rank is None:
+        return
+    ops, ne = build_ops(g, core, T, topo, rank)
+    deps, order, end = order_ops(ops)
+    Q = {"v": g.vector, "a": g.scalar, "p": g.tensor, "g": g, "s": g.sync, "r": g}
+    own = {"v": "cv", "a": "ca", "p": "cp", "g": "cg"}
+    count = {s: 0 for s in SEMAPHORES}
+    done = {}
+    seen = {e: {} for e in "vapgs"}
+    nsent = 0
+    for i in order:
+        o = ops[i]
+        e = "g" if o["e"] == "r" else o["e"]
+        need = {}
+        for j in deps[i]:
+            s, v = done[j]
+            need[s] = max(need.get(s, 0), v)
+        for s, v in need.items():
+            if seen[e].get(s, 0) < v:
+                Q[e].wait_ge(T.sem[s], v)
+                seen[e][s] = v
+        ins = o["fn"]()
+        if o["e"] == "r":
+            done[i] = (o["sem"], o["val"])
+            count[o["sem"]] = o["val"]
+            nsent += 1
+        elif o["sem"]:
+            ins[0].then_inc(T.sem[o["sem"]], 16)
+            count[o["sem"]] = 16
+            done[i] = (o["sem"], 16)
+        else:
+            s = own[e]
+            for x in ins:
+                x.then_inc(T.sem[s], 1)
+            count[s] += len(ins)
+            done[i] = (s, count[s])
+    count["sent"] = nsent * ne
+    for s in SEMAPHORES:
+        if count[s]:
+            g.wait_ge(T.sem[s], count[s])

@@ -111,12 +111,12 @@ ORDER = [("a", 0), ("b", 0), ("t", 0), ("d", 0), ("a", 1), ("t", 1), ("b", 1), (
 V_GATHER = [(0, 0, 1, 1)] + [(t, h, 0, 1) for t in range(STEPS) for h in range(2)]
 V_TURN = [(0, 0, 0), (0, 0, 1)]
 A_NEAR = [(t, h, 0) for t in range(STEPS) for h in range(2)]
-A_MOD = []
+A_MOD = [(t, h, 3) for t in range(STEPS) for h in range(2)]
 A_MARK = [(t, h, 1) for t in range(STEPS) for h in range(2)]
-BANKS = {"a": [[0, 1]] * 2, "t": [[2]] * 2, "m": [[3]] * 2}
-SEEDS = [46]
+BANKS = {"a": [[0, 1]] * 2, "t": [[2, 3]] * 2, "m": [[2, 3]] * 2}
+SEEDS = [73]
 ROUNDS = 4
-PLAN = {}
+TUNE = {"lat": 0.16, "gtt": 1.75}
 
 
 def build_ops(g, core, T, topo, rank):
@@ -157,7 +157,7 @@ def build_ops(g, core, T, topo, rank):
             vop(lambda: V.tensor_scalar(out, in0, s1, s2, o0, o1), R, W, n, c)
 
     def tt(out, in0, in1, o, R, W, n, c=2.0):
-        vop(lambda: V.tensor_tensor(out, in0, in1, o), R, W, n, c)
+        vop(lambda: V.tensor_tensor(out, in0, in1, o), R, W, n, TUNE["gtt"] if c == GAT else c)
 
     def cp(out, in_, R, W, n, c=1.0):
         vop(lambda: V.tensor_copy(out, in_), R, W, n, c)
@@ -504,7 +504,7 @@ def order_ops(ops):
     for i in range(n):
         for j in deps[i]:
             succ[j].append(i)
-    LAT = 0.08
+    LAT = TUNE["lat"]
     lev = [0.0] * n
     for i in range(n - 1, -1, -1):
         lev[i] = ops[i]["dur"] + max([lev[j] + LAT for j in succ[i]], default=0.0)

@@ -4,53 +4,64 @@ from concourse.mybir import dt, AluOpType, AxisListType, ActivationFunctionType
 A = AluOpType
 AF = ActivationFunctionType
 STEPS = 4
-ROT = 712
-BIG = float(2 ** 23)
 SW = 160
+XW = 2192
+MW = 2304
+UW = 144
+BIG = float(2 ** 29)
+SHIFT = -127.0625
+LIFT = 288.0
 
 SCRATCH = {
-    "xs": ("sbuf", [128, 2048], "bfloat16"),
-    "vm": ("sbuf", [128, 2304], "bfloat16"),
+    "xs": ("sbuf", [128, 4 * XW], "bfloat16"),
+    "vm": ("sbuf", [128, 5 * MW], "bfloat16"),
     "li": ("sbuf", [128, 256], "int32"),
     "sraw": ("sbuf", [128, 256], "int32"),
     "sbf": ("sbuf", [128, 256], "bfloat16"),
     "wi": ("sbuf", [128, 8], "int32"),
-    "lb": ("sbuf", [128, 8 * SW], "uint16"),
-    "snd": ("sbuf", [128, 8 * SW], "uint16"),
+    "lb": ("sbuf", [128, 10 * SW], "uint16"),
+    "fs": ("sbuf", [128, 8 * UW], "bfloat16"),
+    "uf": ("sbuf", [128, 8 * UW], "bfloat16"),
+    "uo": ("sbuf", [128, 8 * 8], "uint16"),
     "fo": ("sbuf", [128, 512], "float32"),
-    "fl": ("sbuf", [128, 512], "float32"),
     "pint": ("sbuf", [128, 8], "int32"),
     "pcol": ("sbuf", [128, 16], "float32"),
     "ion": ("sbuf", [128, 144], "float32"),
     "kio": ("sbuf", [128, 256], "float32"),
     "r16": ("sbuf", [128, 128], "float32"),
     "idb": ("sbuf", [128, 128], "bfloat16"),
+    "idl": ("sbuf", [128, 128], "bfloat16"),
+    "idh": ("sbuf", [128, 128], "float16"),
     "bob": ("sbuf", [128, 128], "bfloat16"),
     "boh": ("sbuf", [128, 128], "float16"),
     "bof": ("sbuf", [128, 8], "float32"),
     "diag": ("sbuf", [128, 128], "float32"),
-    "mc": ("sbuf", [128, 128], "float32"),
-    "m16": ("sbuf", [128, 128], "bfloat16"),
-    "m15": ("sbuf", [128, 240], "float32"),
+    "dtop": ("sbuf", [128, 128], "float32"),
+    "m64": ("sbuf", [128, 240], "bfloat16"),
+    "c3": ("sbuf", [128, 256], "bfloat16"),
+    "c16": ("sbuf", [128, 128], "bfloat16"),
+    "ck": ("sbuf", [128, 128], "bfloat16"),
+    "r30": ("sbuf", [128, 480], "bfloat16"),
+    "r48": ("sbuf", [128, 128], "bfloat16"),
+    "r22": ("sbuf", [128, 128], "bfloat16"),
     "otmp": ("sbuf", [128, 8], "float32"),
     "otmi": ("sbuf", [128, 8], "int32"),
     "rbig": ("sbuf", [128, 240], "float32"),
-    "r01": ("sbuf", [128, 128], "float32"),
-    "zw": ("sbuf", [128, 144], "bfloat16"),
+    "r01": ("sbuf", [128, 128], "bfloat16"),
     "zc": ("sbuf", [128, 144], "bfloat16"),
     "zs": ("sbuf", [128, 144], "bfloat16"),
-    "c3": ("sbuf", [128, 64], "bfloat16"),
     "zf": ("sbuf", [128, 144], "float16"),
-    "cf": ("sbuf", [128, 48], "float32"),
+    "cf": ("sbuf", [128, 64], "float32"),
     "coef": ("sbuf", [128, 128], "float16"),
-    "ee": ("sbuf", [128, 256], "float32"),
+    "coen": ("sbuf", [128, 128], "float16"),
+    "coeq": ("sbuf", [128, 128], "float16"),
+    "ee": ("sbuf", [128, 256], "float16"),
     "pm": ("sbuf", [128, 2048], "float16"),
     "ofc": ("sbuf", [128, 48], "uint16"),
     "wrow": ("sbuf", [128, 128], "float32"),
     "wd0": ("sbuf", [128, 128], "float32"),
     "thr": ("sbuf", [128, 128], "float32"),
     "wsc": ("sbuf", [128, 128], "float32"),
-    "base": ("sbuf", [128, 64], "int32"),
     "tol": ("sbuf", [128, 8], "float32"),
     "toli": ("sbuf", [128, 8], "int32"),
     "a": ("sbuf", [128, 4096], "bfloat16"),
@@ -63,8 +74,7 @@ SCRATCH = {
     "cl": ("sbuf", [128, 4096], "bfloat16"),
     "tt0": ("sbuf", [128, 1024], "float32"),
     "tt1": ("sbuf", [128, 1024], "float32"),
-    "eq": ("sbuf", [128, 17 * 128], "bfloat16"),
-    "fs": ("sbuf", [128, 256], "bfloat16"),
+    "eq": ("sbuf", [128, 26 * 128], "bfloat16"),
     "lh": ("sbuf", [128, 256], "float16"),
     "ui": ("sbuf", [128, 256], "int32"),
     "u2": ("sbuf", [128, 256], "int32"),
@@ -72,24 +82,21 @@ SCRATCH = {
     "sq": ("sbuf", [128, 256], "int32"),
     "h0": ("sbuf", [128, 256], "int32"),
     "h16": ("sbuf", [128, 256], "uint16"),
+    "hf": ("sbuf", [128, 256], "float16"),
     "ul": ("sbuf", [128, 256], "int32"),
     "um": ("sbuf", [128, 256], "bfloat16"),
-    "t1": ("sbuf", [128, 256], "int32"),
-    "t2": ("sbuf", [128, 256], "int32"),
-    "b2": ("sbuf", [128, 256], "float32"),
+    "lt": ("sbuf", [128, 256], "bfloat16"),
     "sc": ("sbuf", [128, 512], "float32"),
     "rb": ("sbuf", [128, 256], "float16"),
     "rs": ("sbuf", [128, 256], "bfloat16"),
     "hb": ("sbuf", [128, 256], "float16"),
-    "wd": ("sbuf", [128, 256], "float32"),
+    "wd": ("sbuf", [128, 256], "bfloat16"),
     "ws0": ("sbuf", [128, 128], "bfloat16"),
     "ws1": ("sbuf", [128, 128], "bfloat16"),
     "gi": ("sbuf", [128, 256], "int32"),
     "lp": ("sbuf", [128, 256], "int32"),
-    "sn": ("sbuf", [128, 32], "float32"),
-    "hx": ("sbuf", [128, 16], "float32"),
-    "ti": ("sbuf", [128, 128], "int32"),
-    "dl": ("sbuf", [128, 64], "int32"),
+    "ki": ("sbuf", [128, 64], "int32"),
+    "dl": ("sbuf", [128, 128], "int32"),
     "xa": ("sbuf", [128, 64], "float32"),
     "xb": ("sbuf", [128, 64], "float32"),
     "pt": ("psum", [128, 1024], "bfloat16"),
@@ -101,47 +108,48 @@ SCRATCH = {
     "pc": ("psum", [128, 512], "float32"),
     "pd": ("psum", [128, 512], "float32"),
 }
-DMA_SEMS = ["dx0", "dx1", "dl", "dw", "ds", "dv0", "dv1", "o0", "o1", "o2", "o3", "o4", "o5"]
-SEMAPHORES = ["cv", "ca", "cp", "cg", "sent"] + DMA_SEMS + ["arr%d" % i for i in range(8)]
+PSUM = [k for k in SCRATCH if SCRATCH[k][0] == "psum"]
+DMA_SEMS = ["dx0", "dx1", "dl", "dw", "ds", "dv0", "o0", "o1", "o2", "o3", "o4", "o5"]
+ARRIVE = ["ax%d" % i for i in range(1, 4)] + ["av%d" % i for i in range(1, 5)] + ["au%d" % i for i in range(8)] + ["ao%d" % i for i in range(8)]
+SEMAPHORES = ["cv", "ca", "cp", "cg", "sent"] + DMA_SEMS + ARRIVE
 
-CYC = 0.83e-3 * 1.2
-GAT = 1.5
 NENG = 8
-ORDER = [("a", 0), ("b", 0), ("t", 0), ("d", 0), ("a", 1), ("t", 1), ("b", 1), ("w", 0), ("d", 1), ("w", 1)]
-V_GATHER = [(0, 0, 1, 1)] + [(t, h, 0, 1) for t in range(STEPS) for h in range(2)]
-V_TURN = [(0, 0, 0), (0, 0, 1)]
-A_NEAR = [(t, h, 0) for t in range(STEPS) for h in range(2)]
-A_MOD = [(t, h, 3) for t in range(STEPS) for h in range(2)]
-A_MARK = [(t, h, 1) for t in range(STEPS) for h in range(2)]
-BANKS = {"a": [[0, 1]] * 2, "t": [[2, 3]] * 2, "m": [[2, 3]] * 2}
-SEEDS = [73]
-ROUNDS = 4
-TUNE = {"lat": 0.16, "gtt": 1.75}
+ORDER = [("a", 0), ("t", 0), ("a", 1), ("b", 0), ("t", 1), ("b", 1), ("d", 0), ("w", 0), ("d", 1), ("w", 1)]
+PLAN = {
+    "v_gather": [], "v_gather0": [1, 3],
+    "a_turn": [],
+    "q_mod": [0, 1, 2, 3, 4, 5, 6, 7],
+    "v_mod": [0, 1, 2, 3],
+    "v_f": [],
+    "a_mark": [],
+    "a_near": [0, 1, 2, 3],
+    "v_table": [],
+    "a_hb": [0, 1],
+    "fine": [0, 2], "fine_near": [1, 3],
+    "banks": {"a": [0, 1, 2], "t": [3], "m": [3]},
+}
+TUNE = {"cyc": 0.83e-3 * 1.1, "pe": 0.42e-3 * 1.25, "lat": 0.14, "gat": 1.5, "gtt": 1.75, "sca": 3.5, "hop": 3.6, "bulk": 12.0,
+        "vfix": 0.045, "afix": 0.06, "pfix": 0.06, "w": 6.0, "noise": [0.05, 0.2, 0.5, 1.0, 2.0], "slack": 0.4, "seed": 0, "rounds": 3000}
 
 
 def build_ops(g, core, T, topo, rank):
     V, S, P = g.vector, g.scalar, g.tensor
     ops = []
     pr = [0]
-    nxt = T.cores[(rank + 1) % len(T.cores)]
-    rid, pid = topo.addr(nxt, core)
-    eng = topo.engines(core, nxt)[:NENG]
-    msk = sum(1 << e for e in eng)
+    CYC, GAT, GTT = TUNE["cyc"], TUNE["gat"], TUNE["gtt"]
 
     def op(e, fn, R, W, dur, sem=None, val=0):
-        ops.append({"pr": pr[0], "e": e, "fn": fn, "R": list(R), "W": list(W), "dur": dur, "sem": sem, "val": val})
-
-    def vd(n, c=1.0):
-        return 0.03 + max(64, n * c) * CYC
+        ops.append({"pr": pr[0], "e": e, "fn": fn, "R": list(R), "W": [k for k in W if k not in PSUM],
+                    "X": [k for k in W if k in PSUM], "dur": dur, "sem": sem, "val": val})
 
     def vop(fn, R, W, n, c=1.0):
-        op("v", lambda: [fn()], R, W, vd(n, c))
+        op("v", lambda: [fn()], R, W, TUNE["vfix"] + max(64, n * c) * CYC)
 
     def aop(fn, R, W, n, c=1.0):
-        op("a", lambda: [fn()], R, W, 0.06 + max(64, n * c) * CYC)
+        op("a", lambda: [fn()], R, W, TUNE["afix"] + max(64, n * c) * CYC)
 
     def pop(fns, R, W, cyc):
-        op("p", lambda: [f() for f in fns], R, W, 0.08 + cyc * 0.42e-3 * 1.2)
+        op("p", lambda: [f() for f in fns], R, W, TUNE["pfix"] + cyc * TUNE["pe"])
 
     def gop(fn, R, W, n):
         op("g", lambda: [fn()], R, W, 0.15 + 2 * n * CYC)
@@ -150,6 +158,12 @@ def build_ops(g, core, T, topo, rank):
         q = g.sync if e == "s" else g.scalar
         op(e, lambda: [q.dma_start(out, in_)], R, W, dur, sem, 16)
 
+    def send(back, dst, src, R, W, sem, dur):
+        to = T.cores[(rank - back) % len(T.cores)]
+        rid, pid = topo.addr(to, core)
+        eng = topo.engines(core, to)[:NENG]
+        op("r", lambda: [g.remote_dma(dst, src, T.sem[sem], T.sem.sent, pid, rid, sum(1 << e for e in eng))], R, W, dur, sem, len(eng))
+
     def ts(out, in0, s1, s2, o0, o1, R, W, n, c=1.0):
         if o1 is None:
             vop(lambda: V.tensor_scalar(out, in0, s1, None, o0), R, W, n, c)
@@ -157,7 +171,7 @@ def build_ops(g, core, T, topo, rank):
             vop(lambda: V.tensor_scalar(out, in0, s1, s2, o0, o1), R, W, n, c)
 
     def tt(out, in0, in1, o, R, W, n, c=2.0):
-        vop(lambda: V.tensor_tensor(out, in0, in1, o), R, W, n, TUNE["gtt"] if c == GAT else c)
+        vop(lambda: V.tensor_tensor(out, in0, in1, o), R, W, n, c)
 
     def cp(out, in_, R, W, n, c=1.0):
         vop(lambda: V.tensor_copy(out, in_), R, W, n, c)
@@ -168,50 +182,72 @@ def build_ops(g, core, T, topo, rank):
     def mm(out, l, r, st, sp):
         return lambda: P.matmul(out, l, r, st, sp)
 
+    def iota(out, pat, base, W, n, step=0):
+        gop(lambda: g.iota(out, pat, base, step, allow_small_or_imprecise_dtypes=True), [], W, n)
+
     dma(T.li[:], T.lanes[:], [], ["li"], "dl", 2.5)
-    dma(T.xs[:, 0:1024], T.x[:, 0:1024], [], ["xs0"], "dx0", 3.5)
-    dma(T.xs[:, 1024:2048], T.x[:, 1024:2048], [], ["xs1"], "dx1", 3.5, "a")
+    dma(T.xs[:, 0:1024], T.x[:, 0:1024], [], ["x0"], "dx0", 3.5)
+    dma(T.xs[:, 1024:2048], T.x[:, 1024:2048], [], ["x0b"], "dx1", 3.5, "a")
     dma(T.wi[:, 0:1], T.wt[:], [], ["wi"], "dw", 2.5)
     vop(lambda: V.memset(T.sraw[:], 0), [], ["sraw"], 256)
     dma(T.sraw[0:128:16, :], T.s0[:], [], ["sraw"], "ds", 2.5)
-    dma(T.vm[:, ROT:2048], T.v[:, 0:2048 - ROT], [], ["vm"], "dv0", 4.5)
-    dma(T.vm[:, 0:ROT], T.v[:, 2048 - ROT:2048], [], ["vmb"], "dv1", 4.5)
-    XS = ["xs0", "xs1"]
-    VM = ["vm", "vmb"]
+    dma(T.vm[:, 0:2048], T.v[:], [], ["vm0"], "dv0", 5.0)
 
     gop(lambda: g.iota(T.pint[:, 0:1], [[0, 1]], 0, 1), [], ["pi0"], 1)
-    gop(lambda: g.iota(T.ion[:], [[1, 144]], 0, 0, allow_small_or_imprecise_dtypes=True), [], ["ion"], 144)
-    gop(lambda: g.iota(T.r16[:], [[0, 8], [1, 16]], 0, 0, allow_small_or_imprecise_dtypes=True), [], ["r16"], 128)
-    gop(lambda: g.iota(T.kio[:], [[1, 16], [0, 16]], 0, 0, allow_small_or_imprecise_dtypes=True), [], ["kio"], 256)
+    iota(T.ion[:], [[1, 144]], 0, ["ion"], 144)
+    iota(T.r16[:], [[0, 8], [1, 16]], 0, ["r16"], 128)
+    iota(T.kio[:], [[1, 16], [0, 16]], 0, ["kio"], 256)
+    iota(T.c3[:], [[6, 2], [0, 128]], -3, ["c3"], 256)
+    iota(T.m64[:], [[0, 16], [64, 15]], 64, ["m64"], 240)
+    iota(T.c16[:], [[0, 128]], 16, ["c16"], 128)
+    iota(T.ck[:], [[0, 128]], 1, ["ck"], 128, 32767)
+    pe_mod = len(PLAN["q_mod"]) < 8
+    if pe_mod:
+        vop(lambda: V.memset(T.r30[0:32, :], float(2 ** 30)), [], ["r30"], 480, 0.5)
+    vop(lambda: V.memset(T.r48[0:32, :], float(2 ** 48)), [], ["r48"], 128, 0.5)
+    if PLAN["a_near"]:
+        vop(lambda: V.memset(T.r22[0:32, :], 1.5 * 2 ** 22), [], ["r22"], 128, 0.5)
+    neg3, pos3 = T.c3[0:1, 0:128], T.c3[0:1, 128:256]
     ts(T.pint[:, 1:2], T.pint[:, 0:1], 15, None, A.bitwise_and, None, ["pi0"], ["pi1"], 1)
     ts(T.pint[:, 2:3], T.pint[:, 0:1], 4, None, A.arith_shift_right, None, ["pi0"], ["pi2"], 1)
     ts(T.pint[:, 3:4], T.pint[:, 0:1], 7, None, A.bitwise_and, None, ["pi0"], ["pi3"], 1)
     ts(T.pint[:, 4:5], T.pint[:, 0:1], 1, 7, A.arith_shift_right, A.bitwise_and, ["pi0"], ["pi4"], 1)
-    cp(T.pcol[:, 0:5], T.pint[:, 0:5], ["pi0", "pi1", "pi2", "pi3", "pi4"], ["pc"], 5)
+    CP = "pcol"
+    cp(T.pcol[:, 0:5], T.pint[:, 0:5], ["pi0", "pi1", "pi2", "pi3", "pi4"], [CP], 5)
     pP, pK, pG, p7, pH = (T.pcol[:, i:i + 1] for i in range(5))
-    pZ, pW = T.pcol[:, 5:6], T.pcol[:, 6:7]
-    ts(pZ, pG, 16.0, 15.0, A.mult, A.add, ["pc"], ["pz"], 1)
+    pZ, pW, p0 = T.pcol[:, 5:6], T.pcol[:, 6:7], T.pcol[:, 8:9]
+    ts(pZ, pG, 16.0, 15.0, A.mult, A.add, [CP], ["pz"], 1)
     cp(pW, T.wi[:, 0:1], ["wi"], ["pw"], 1)
-    ts(T.idb[:], T.ion[:, 0:128], pP, None, A.is_equal, None, ["ion", "pc"], ["idb"], 128)
-    ts(T.bof[:], T.ion[:, 0:8], pG, None, A.is_equal, None, ["ion", "pc"], ["bof"], 8)
-    ts(T.cf[:, 16:32], T.r16[:, 0:16], pK, None, A.subtract, None, ["r16", "pc"], ["cf1"], 16)
-    ts(T.cf[:, 32:48], T.r16[:, 0:16], pK, pK, A.is_lt, A.mult, ["r16", "pc"], ["cf2"], 16)
+    ts(T.idb[:], T.ion[:, 0:128], pP, None, A.is_equal, None, ["ion", CP], ["idb"], 128)
+    act(T.idl[:], T.idb[:], AF.Copy, ["idb"], ["idl"], 128, scale=float(2 ** 25))
+    act(T.idh[:], T.idb[:], AF.Copy, ["idb"], ["idh"], 128, scale=1024.0)
+    ts(T.bof[:], T.ion[:, 0:8], pG, None, A.is_equal, None, ["ion", CP], ["bof"], 8)
+    ts(T.cf[:, 16:32], T.r16[:, 0:16], pK, None, A.subtract, None, ["r16", CP], ["cf1"], 16)
+    ts(T.cf[:, 32:48], T.r16[:, 0:16], pK, pK, A.is_lt, A.mult, ["r16", CP], ["cf2"], 16)
     tt(T.cf[:, 0:16], T.cf[:, 16:32], T.cf[:, 32:48], A.max, ["cf1", "cf2"], ["cf"], 16)
-    for r in range(8):
-        ts(T.coef[:, r:120:8], T.cf[:, 1:16], T.bof[:, r:r + 1], None, A.mult, None, ["cf", "bof"], ["coef%d" % r], 16)
     COEF = ["coef%d" % r for r in range(8)]
-    ts(T.zw[:], T.ion[:], pZ, pW, A.is_equal, A.mult, ["ion", "pz", "pw"], ["zw"], 144)
-    ts(T.zc[:], T.ion[:], pZ, float(2 ** 20), A.is_equal, A.mult, ["ion", "pz"], ["zc"], 144)
-    ts(T.zf[:], T.ion[:], pZ, 256.0, A.is_equal, A.mult, ["ion", "pz"], ["zf"], 144)
-    ts(T.bob[:], T.kio[:, 0:128], pG, None, A.is_equal, None, ["kio", "pc"], ["bob"], 128)
+    COEQ = ["coeq%d" % r for r in range(8)]
+    if pe_mod:
+        ts(p0, pK, 0.0, 256.0, A.is_equal, A.mult, [CP], ["p0"], 1)
+        ts(T.cf[:, 48:64], T.cf[:, 0:16], p0, None, A.subtract, None, ["cf", "p0"], ["cf3"], 16)
+        for r in range(8):
+            ts(T.coef[:, r:120:8], T.cf[:, 49:64], T.bof[:, r:r + 1], None, A.mult, None, ["cf3", "bof"], [COEF[r]], 16)
+        act(T.coen[:, 0:120], T.coef[:, 0:120], AF.Copy, COEF, ["coen"], 120, scale=-1.0)
+    if PLAN["q_mod"]:
+        for r in range(8):
+            ts(T.coeq[:, r:120:8], T.cf[:, 1:16], T.bof[:, r:r + 1], None, A.mult, None, ["cf", "bof"], [COEQ[r]], 16)
+    ts(T.xs[:, 2048:XW], T.ion[:], pZ, pW, A.is_equal, A.mult, ["ion", "pz", "pw"], ["x0w"], 144)
+    ts(T.zc[:], T.ion[:], pZ, float(2 ** 22), A.is_equal, A.mult, ["ion", "pz"], ["zc"], 144)
+    act(T.zf[:], T.zc[:], AF.Copy, ["zc"], ["zf"], 144, scale=2.0 ** -8)
+    if PLAN["a_near"]:
+        act(T.zs[:], T.zc[:], AF.Copy, ["zc"], ["zs"], 144, scale=0.5)
+    ts(T.bob[:], T.kio[:, 0:128], pG, None, A.is_equal, None, ["kio", CP], ["bob"], 128)
     act(T.boh[:], T.bob[:], AF.Copy, ["bob"], ["boh"], 128)
-    ts(T.diag[:], T.r16[:], pK, None, A.is_equal, None, ["r16", "pc"], ["diag"], 128)
-    gop(lambda: g.iota(T.m15[:], [[0, 16], [1, 15]], 1, 0, allow_small_or_imprecise_dtypes=True), [], ["m15"], 240)
-    act(T.mc[:], T.m15[:, 0:128], AF.Copy, ["m15"], ["mc"], 128, scale=float(2 ** 15 + 2 ** 11))
-    act(T.m16[:], T.m15[:, 0:128], AF.Copy, ["m15"], ["m16"], 128, scale=16.0)
-    ts(T.rbig[:], T.m15[:], 1.0, BIG, A.is_equal, A.mult, ["m15"], ["rbig"], 240)
+    ts(T.diag[:], T.r16[:], pK, None, A.is_equal, None, ["r16", CP], ["diag"], 128)
+    act(T.dtop[:], T.diag[:], AF.Copy, ["diag"], ["dtop"], 128, scale=2048.0)
+    ts(T.rbig[:], T.m64[:], 64.0, BIG, A.is_equal, A.mult, ["m64"], ["rbig"], 240)
     offM = T.ofc[:, 32:40]
-    ts(T.otmp[:], T.ion[:, 0:128:16], pK, 1.0 / 15, A.add, A.mult, ["ion", "pc"], ["otmp"], 8)
+    ts(T.otmp[:], T.ion[:, 0:128:16], pK, 1.0 / 15, A.add, A.mult, ["ion", CP], ["otmp"], 8)
     ts(T.otmi[:], T.otmp[:], -0.47, None, A.add, None, ["otmp"], ["otmi"], 8)
     ts(offM, T.otmi[:], 7.0, None, A.min, None, ["otmi"], ["offM"], 8)
     for h in range(2):
@@ -219,13 +255,13 @@ def build_ops(g, core, T, topo, rank):
     act(T.r01[:], T.r16[:], AF.Sign, ["r16"], ["r01"], 128)
     offE, offW, offK = T.ofc[:, 0:8], T.ofc[:, 8:10], T.ofc[:, 16:32]
     cp(offE, T.ion[:, 0:8], ["ion"], ["offE"], 8)
-    ts(T.pcol[:, 7:8], p7, 16.0, 15.0, A.mult, A.add, ["pc"], ["pw7"], 1)
+    ts(T.pcol[:, 7:8], p7, 16.0, 15.0, A.mult, A.add, [CP], ["pw7"], 1)
     ts(offW, T.ion[:, 0:2], 0.0, T.pcol[:, 7:8], A.mult, A.add, ["ion", "pw7"], ["offW"], 2)
-    ts(offK, T.ion[:, 0:16], 0.0, pK, A.mult, A.add, ["ion", "pc"], ["offK"], 16)
-    tt(T.ee[:], T.cf[:, 0:16].indirect(offK), T.kio[:], A.is_equal, ["cf", "offK", "kio"], ["ee"], 256, GAT)
-    for r in range(8):
-        act(T.pm[:, r * 256:(r + 1) * 256], T.ee[:], AF.Copy, ["ee", "bof"], ["pm%d" % r], 256, scale=T.bof[:, r:r + 1])
+    ts(offK, T.ion[:, 0:16], 0.0, pK, A.mult, A.add, ["ion", CP], ["offK"], 16)
+    tt(T.ee[:], T.cf[:, 0:16].indirect(offK), T.kio[:], A.is_equal, ["cf", "offK", "kio"], ["ee"], 256, GTT)
     PM = ["pm%d" % r for r in range(8)]
+    for r in range(8):
+        ts(T.pm[:, r * 256:(r + 1) * 256], T.ee[:], T.bof[:, r:r + 1], None, A.mult, None, ["ee", "bof"], [PM[r]], 256, 0.5)
     vop(lambda: V.memset(T.wd0[:], 0.5), [], ["wd0"], 128)
     vop(lambda: V.memset(T.thr[:], 0.0), [], ["thr"], 128)
     vop(lambda: V.tensor_tensor_scan(T.wrow[:], T.wd0[:], T.thr[:], float(2 ** 61), A.mult, A.add), ["wd0", "thr"], ["wrow"], 128)
@@ -233,13 +269,11 @@ def build_ops(g, core, T, topo, rank):
     act(T.thr[:], T.wd0[:], AF.Copy, ["wd0"], ["thr"], 128, scale=2.5)
     vop(lambda: V.tensor_tensor_scan(T.wsc[:], T.r01[:], T.wd0[:], 0.0, A.mult, A.add), ["r01", "wd0"], ["wsc"], 128)
     for h in range(2):
-        b = h * 32
-        ts(T.base[:, b:b + 8], T.ion[:, 0:8], 8.0, pH, A.mult, A.add, ["ion", "pc"], ["baseT%d" % h], 8)
-        ts(T.base[:, b + 8:b + 16], T.ion[:, 0:128:16], pK, 2048.0 + 128 * h, A.add, A.add, ["ion", "pc"], ["baseS%d" % h], 8)
-        ts(T.base[:, b + 24:b + 32], T.ion[:, 0:8], 240.0, pK, A.mult, A.add, ["ion", "pc"], ["baseF%d" % h], 8)
-    vop(lambda: V.memset(T.tol[:, 0:1], 2.5), [], ["tol"], 1)
-    vop(lambda: V.memset(T.c3[:], -3.0 * 2 ** 20), [], ["c3"], 64)
-    act(T.zs[:], T.zc[:], AF.Copy, ["zc"], ["zs"], 144, scale=0.5)
+        b = h * 64 + 32
+        ts(T.dl[:, b + 8:b + 16], T.ion[:, 0:128:16], pK, 2048.0 + 128 * h, A.add, A.add, ["ion", CP], ["baseS%d" % h], 8)
+        ts(T.dl[:, b + 16:b + 24], T.ion[:, 0:8], 240.0, pK, A.mult, A.add, ["ion", CP], ["baseF%d" % h], 8)
+        ts(T.dl[:, b + 24:b + 32], T.ion[:, 0:8], 8.0, pH, A.mult, A.add, ["ion", CP], ["baseT%d" % h], 8)
+    vop(lambda: V.memset(T.tol[:, 0:1], 2.5), [], ["tol0"], 1)
 
     for h in range(2):
         for b in range(2):
@@ -248,15 +282,25 @@ def build_ops(g, core, T, topo, rank):
     pop([mm(T.pd[:, 0:16], T.zc[:, 15 - r:143 - r], T.sbf[:, r:256:16], r == 0, r == 15) for r in range(16)],
         ["zc", "sbf"], ["pd"], 16 * 64)
     for h in range(2):
-        ts(T.lb[:, h * SW + 144:h * SW + 152], T.pd[:, h * 8:h * 8 + 8], 2.0 ** -20, None, A.mult, None, [], ["pd", "ls0%d" % h], 8)
+        ts(T.xb[:, h * 32:h * 32 + 8], T.pd[:, h * 8:h * 8 + 8], 2.0 ** -16, None, A.mult, None, [], ["pd", "s%d" % h], 8)
+    X0 = ["x0", "x0b", "x0w"]
+
+    def send_items(t, after):
+        send(t, T.xs[:, t * XW:(t + 1) * XW], T.xs[:, 0:XW], X0 + after, ["x%d" % t], "ax%d" % t, TUNE["bulk"] * (2 if t == 1 else 1))
+
+    def send_memory(t, after):
+        send(1, T.vm[:, (t + 1) * MW:(t + 1) * MW + 2048], T.vm[:, t * MW:t * MW + 2048], ["vm%d" % t] + after, ["vm%d" % (t + 1)],
+             "av%d" % (t + 1), TUNE["bulk"] * (2 if t == 0 else 1))
+    send_items(1, [])
+    send_memory(0, [])
 
     bank = {}
     FB = [T.f0, T.f1]
     TB = [T.tt0, T.tt1]
     WS = [T.ws0, T.ws1]
 
-    def nb(kind, h):
-        ring = BANKS[kind][h]
+    def nb(kind):
+        ring = PLAN["banks"][kind]
         key = tuple(ring)
         bank[key] = (bank.get(key, -1) + 1) % len(ring)
         return ring[bank[key]]
@@ -265,69 +309,86 @@ def build_ops(g, core, T, topo, rank):
         lo = (t * 2 + h) * SW
         LB = "lb%d%d" % (t, h)
         F = FB[h]
-        o = h * 2048
-        for Q in range(2):
-            for b in range(2):
-                c0 = b * 64 + Q * 32
-                out, src = T.a[:, o + c0 * 16:o + c0 * 16 + 512], T.xs[:, 0:2048].indirect(T.lb[:, lo + c0:lo + c0 + 32])
-                if (t, h, Q, b) in V_GATHER:
-                    cp(out, src, XS + [LB], ["a%d%d%d" % (h, Q, b)], 512, GAT)
-                else:
-                    act(out, src, AF.Copy, XS + [LB], ["a%d%d%d" % (h, Q, b)], 512, GAT)
-            fns = []
-            for el in range(4):
-                for b in range(2):
-                    c = o + (b * 8 + Q * 4 + el) * 128
-                    fns.append(lambda c=c, j=el * 2 + b: P.transpose(T.pt[:, j * 128:(j + 1) * 128], T.a[:, c:c + 128], T.idb[:]))
-            pop(fns, ["a%d%d0" % (h, Q), "a%d%d1" % (h, Q), "idb"], ["pt"], 1024)
-            ao = o + Q * 1024
-            if (t, h, Q) in V_TURN:
-                ts(T.at[:, ao:ao + 1024], T.pt[:], 288.0, None, A.add, None, [], ["pt", "at%d%d" % (h, Q)], 1024, 0.5)
-            else:
-                act(T.at[:, ao:ao + 1024], T.pt[:], AF.Identity, [], ["pt", "at%d%d" % (h, Q)], 1024, bias=288.0)
-            for n2 in range(2):
-                n = Q * 2 + n2
-                k = nb("a", h)
-                pf = T["pf%d" % k]
-                fns = []
-                for j in range(4):
-                    c = ao + (n2 * 4 + j) * 128
-                    s = (j >> 1) * 240
-                    fns.append(mm(pf[:, s + (j & 1):s + 240:2], T.at[:, c:c + 128], T.coef[:, 0:120], j == 0, j == 3))
-                pop(fns, ["at%d%d" % (h, Q)] + COEF, ["pf%d" % k], 480)
-                qq = T.q[:, k * 512:k * 512 + 480]
-                act(qq, pf[:, 0:480], AF.Identity, [], ["pf%d" % k, "q%d" % k], 480, bias=127.5, scale=-1.0)
-                if (t, h, n) in A_MOD:
-                    fns = [mm(pf[:, 0:480], T.idb[:], qq, True, False)]
-                    for j in range(4):
-                        c = ao + (n2 * 4 + j) * 128
-                        s = (j >> 1) * 240
-                        fns.append(mm(pf[:, s + (j & 1):s + 240:2], T.at[:, c:c + 128], T.coef[:, 0:120], False, j == 3))
-                    pop(fns, ["at%d%d" % (h, Q), "q%d" % k, "idb"] + COEF, ["pf%d" % k], 960)
-                    act(F[:, 16 + n * 480:496 + n * 480], pf[:, 0:480], AF.Copy, [], ["pf%d" % k, "f%d%d" % (h, n)], 480)
-                else:
-                    tt(F[:, 16 + n * 480:496 + n * 480], pf[:, 0:480], qq, A.add, ["q%d" % k], ["pf%d" % k, "f%d%d" % (h, n)], 480, 1.0)
-            pop([mm(T.pu[:, Q * 60:Q * 60 + 60], T.zw[:, 15 - r:143 - r], F[:, 16 + Q * 960 + r:976 + Q * 960:16], r == 0, r == 15)
-                 for r in range(16)], ["zw", "f%d%d" % (h, 2 * Q), "f%d%d" % (h, 2 * Q + 1)], ["pu"], 1024)
-            c = slice(h * 128 + Q * 60, h * 128 + Q * 60 + 60)
-            H = "%d%d" % (h, Q)
-            cp(T.ui[:, c], T.pu[:, Q * 60:Q * 60 + 60], [], ["pu", "ui" + H], 60)
-            ts(T.u2[:, c], T.ui[:, c], 4095, None, A.bitwise_and, None, ["ui" + H], ["u2" + H], 60)
-            ts(T.yy[:, c], T.u2[:, c], 592.0, None, A.add, None, ["u2" + H], ["yy" + H], 60)
-            tt(T.sq[:, c], T.yy[:, c], T.yy[:, c], A.mult, ["yy" + H], ["sq" + H], 60)
-            ts(T.h0[:, c], T.sq[:, c], 5, 2047, A.arith_shift_right, A.bitwise_and, ["sq" + H], ["h0" + H], 60)
-            cp(T.h16[:, c], T.h0[:, c], ["h0" + H], ["h16" + H], 60)
-        c = slice(h * 128, h * 128 + 120)
         H = str(h)
+        o = h * 2048
+        XS, XZ = (["x0", "x0b"], "x0w") if t == 0 else (["x%d" % t], "x%d" % t)
+        zw = t * XW + 2048
+        for Q in range(2):
+            ao = o + Q * 1024
+            for e0, e1 in ([(0, 2), (2, 4)] if h * 2 + Q in PLAN["fine"] else [(0, 4)]):
+                AK = ["a%d%d%d%d" % (h, Q, e0, b) for b in range(2)]
+                w = (e1 - e0) * 8
+                for b in range(2):
+                    c0 = b * 64 + Q * 32 + e0 * 8
+                    out, src = T.a[:, o + c0 * 16:o + (c0 + w) * 16], T.xs[:, t * XW:t * XW + 2048].indirect(T.lb[:, lo + c0:lo + c0 + w])
+                    if h * 4 + Q * 2 + b in PLAN["v_gather0" if t == 0 else "v_gather"]:
+                        cp(out, src, XS + [LB], [AK[b]], w * 16, GAT)
+                    else:
+                        act(out, src, AF.Copy, XS + [LB], [AK[b]], w * 16, GAT)
+                fns = []
+                for el in range(e0, e1):
+                    for b in range(2):
+                        c = o + (b * 8 + Q * 4 + el) * 128
+                        fns.append(lambda c=c, j=el * 2 + b: P.transpose(T.pt[:, j * 128:(j + 1) * 128], T.a[:, c:c + 128], T.idb[:]))
+                pop(fns, AK + ["idb"], ["pt"], w * 32)
+                AT = ["at%d%d" % (h, Q * 2 + x) for x in range(e0 // 2, e1 // 2)]
+                kinds = {h * 4 + Q * 2 + x in PLAN["q_mod"] for x in range(e0 // 2, e1 // 2)}
+                assert len(kinds) == 1
+                shift = LIFT if True in kinds else SHIFT
+                if h * 2 + Q in PLAN["a_turn"]:
+                    act(T.at[:, ao + e0 * 256:ao + e1 * 256], T.pt[:, e0 * 256:e1 * 256], AF.Identity, [], ["pt"] + AT, w * 32, bias=shift)
+                else:
+                    ts(T.at[:, ao + e0 * 256:ao + e1 * 256], T.pt[:, e0 * 256:e1 * 256], shift, None, A.add, None, [], ["pt"] + AT, w * 32, 0.5)
+            for n in (2 * Q, 2 * Q + 1):
+                k = nb("a")
+                AT = "at%d%d" % (h, n)
+                pf, PF = T["pf%d" % k], "pf%d" % k
+                Fo, FK = F[:, 16 + n * 480:496 + n * 480], "f%d%d" % (h, n)
+
+                def sums(coef, first, last):
+                    fns = []
+                    for j in range(4):
+                        c = o + (n * 4 + j) * 128
+                        s = (j >> 1) * 240
+                        fns.append(mm(pf[:, s + (j & 1):s + 240:2], T.at[:, c:c + 128], coef[:, 0:120], first and j == 0, last and j == 3))
+                    return fns
+                if h * 4 + n in PLAN["q_mod"]:
+                    qq = T.q[:, k * 512:k * 512 + 480]
+                    pop(sums(T.coeq, True, True), [AT] + COEQ, [PF], 480)
+                    if h * 4 + n in PLAN["v_mod"]:
+                        act(qq, pf[:, 0:480], AF.Identity, [], [PF, "q%d" % k], 480, bias=127.5, scale=-1.0)
+                        tt(Fo, pf[:, 0:480], qq, A.add, ["q%d" % k], [PF, FK], 480, 1.0)
+                        continue
+                    act(qq, pf[:, 0:480], AF.Identity, [], [PF, "q%d" % k], 480, bias=127.5, scale=-1.0)
+                    pop([mm(pf[:, 0:480], T.idb[:], qq, True, False)] + sums(T.coeq, False, True), [AT, "q%d" % k, "idb"], [PF], 960)
+                    off = 0.0
+                else:
+                    pop([mm(pf[:, 0:480], neg3, T.r30[0:1, :], True, False)] + sums(T.coen, False, False), [AT, "coen", "c3", "r30"], [PF], 960)
+                    pop([mm(pf[:, 0:480], pos3, T.r30[0:1, :], False, False)] + sums(T.coef, False, True), [AT] + COEF, [PF], 960)
+                    off = 127.5
+                if h * 4 + n in PLAN["v_f"]:
+                    ts(Fo, pf[:, 0:480], off, None, A.add, None, [], [PF, FK], 480)
+                else:
+                    act(Fo, pf[:, 0:480], AF.Identity, [], [PF, FK], 480, bias=off)
+            u0 = Q * 60
+            pop([mm(T.pu[:, u0:u0 + 60], T.xs[:, zw + 15 - r:zw + 143 - r], F[:, 16 + Q * 960 + r:976 + Q * 960:16], r == 0, r == 15)
+                 for r in range(16)], [XZ, "f%d%d" % (h, 2 * Q), "f%d%d" % (h, 2 * Q + 1)], ["pu"], 1024)
+            c = slice(h * 128 + u0, h * 128 + u0 + 60)
+            K = "%d%d" % (h, Q)
+            cp(T.ui[:, c], T.pu[:, u0:u0 + 60], [], ["pu", "ui" + K], 60)
+            ts(T.u2[:, c], T.ui[:, c], 4095, None, A.bitwise_and, None, ["ui" + K], ["u2" + K], 60)
+            ts(T.yy[:, c], T.u2[:, c], 1184.0, None, A.add, None, ["u2" + K], ["yy" + K], 60)
+            tt(T.sq[:, c], T.yy[:, c], T.u2[:, c], A.mult, ["yy" + K, "u2" + K], ["sq" + K], 60)
+            ts(T.h0[:, c], T.sq[:, c], 5, 2047, A.arith_shift_right, A.bitwise_and, ["sq" + K], ["h0" + K], 60)
+            cp(T.h16[:, c], T.h0[:, c], ["h0" + K], ["h16" + K], 60)
+        c = slice(h * 128, h * 128 + 120)
         ts(T.ul[:, c], T.ui[:, c], 15, None, A.bitwise_and, None, ["ui%d0" % h, "ui%d1" % h], ["ul" + H], 120)
-        cp(T.um[:, c], T.ul[:, c], ["ul" + H], ["um" + H], 120)
-        LS = ("ls%d%d" if t == 0 else "lb%d%d") % (t, h)
-        sN, sF = T.sn[:, h * 16:h * 16 + 8], T.sn[:, h * 16 + 8:h * 16 + 16]
-        ts(sN, T.lb[:, lo + 144:lo + 152], -32768.0, None, A.mult, None, [LS], ["sN" + H], 8)
-        cp(sF, T.lb[:, lo + 144:lo + 152], [LS], ["sF" + H], 8)
-        tt(T.t1[:, h * 128:h * 128 + 128], sN.indirect(offM), T.mc[:], A.add, ["sN" + H, "offM", "mc"], ["t1" + H], 128, GAT)
-        ts(T.t2[:, c], T.t1[:, c], 0xFFFFF, None, A.bitwise_and, None, ["t1" + H], ["t2" + H], 120)
-        tt(T.b2[:, c], T.t2[:, c], T.h0[:, c], A.add, ["t2" + H, "h0%d0" % h, "h0%d1" % h], ["b2" + H], 120)
+        ts(T.um[:, c], T.ul[:, c], 64.0, None, A.mult, None, ["ul" + H], ["um" + H], 120)
+        ts(T.hf[:, c], T.h16[:, c], 1.0, None, A.mult, None, ["h16%d0" % h, "h16%d1" % h], ["hf" + H], 120, 0.5)
+        tt(T.lt[:, h * 128:h * 128 + 128], T.xb[:, h * 32:h * 32 + 8].indirect(offM), T.m64[:, 0:128], A.is_gt,
+           ["s" + H, "offM", "m64"], ["lt" + H], 128, GTT)
+        if h == 1 and t < STEPS - 2:
+            send_items(t + 2, ["hf1"])
 
     def stage_t(t, h):
         lo = (t * 2 + h) * SW
@@ -337,134 +398,145 @@ def build_ops(g, core, T, topo, rank):
         ts(T.lh[:, o:o + 64], T.lb[:, lo:lo + 64], 1.0 / 2048, None, A.mult, None, [LB], ["lh0" + H], 64, 0.5)
         ts(T.lh[:, o + 64:o + 128], T.lb[:, lo + 64:lo + 128], 1.0, None, A.mult, None, [LB], ["lh1" + H], 64, 0.5)
         for n in range(2):
-            k = nb("t", h)
+            k = nb("t")
             pf = T["pf%d" % k]
             fns = []
             for m in range(8):
                 for b in range(2):
                     fns.append(mm(pf[:, m * 64:m * 64 + 64], T.pm[:, n * 8 + m:2048:16], T.lh[:, o + b * 64:o + b * 64 + 64], b == 0, b == 1))
             pop(fns, PM + ["lh0" + H, "lh1" + H], ["pf%d" % k], 1024)
-            act(TB[h][:, n * 512:(n + 1) * 512], pf[:], AF.Copy, [], ["pf%d" % k, "tt%d%d" % (h, n)], 512, scale=2048.0)
+            if h * 2 + n in PLAN["v_table"]:
+                ts(TB[h][:, n * 512:(n + 1) * 512], pf[:], 2048.0, None, A.mult, None, [], ["pf%d" % k, "tt%d%d" % (h, n)], 512)
+            else:
+                act(TB[h][:, n * 512:(n + 1) * 512], pf[:], AF.Copy, [], ["pf%d" % k, "tt%d%d" % (h, n)], 512, scale=2048.0)
 
     def stage_b(t, h):
         F = FB[h]
         H = str(h)
         o = h * 2048
+        VM = "vm%d" % t
+        tol, TOL = (T.tol[:, 0:1], "tol0") if t == 0 else (T.uf[:, (2 * t - 1) * UW + 128:(2 * t - 1) * UW + 129], "uf%d1" % (t - 1))
+        nc = slice(h * 128, h * 128 + 120)
+        pop([mm(T.pc[:, 120:240], T.c16[0:1, :], T.m64[0:1, 0:120], True, False)], ["c16", "m64"], ["pc", "key"], 120)
+        pop([mm(T.pc[:, 120:240], T.idb[:], T.um[:, nc], False, False)], ["key", "idb", "um" + H], ["far2"], 120)
         for Q in range(2):
             for n in (2 * Q, 2 * Q + 1):
                 c = slice(o + n * 480, o + n * 480 + 480)
                 K = "%d%d" % (h, n)
-                if (t, h, n) in A_MARK:
-                    k = nb("m", h)
+                src = T.vm[:, t * MW:t * MW + 2048].indirect(T.h16[:, h * 128 + n * 30:h * 128 + n * 30 + 30])
+                if h * 4 + n in PLAN["a_mark"]:
+                    k = nb("m")
                     pf = T["pf%d" % k]
                     mk = T.q[:, k * 512:k * 512 + 480]
-                    act(mk, T.vm[:, 0:2048].indirect(T.h16[:, h * 128 + n * 30:h * 128 + n * 30 + 30]), AF.Copy,
-                        VM + ["h16%d%d" % (h, Q)], ["q%d" % k], 480, GAT, scale=-1.0)
+                    act(mk, src, AF.Copy, [VM, "h16%d%d" % (h, Q)], ["q%d" % k], 480, GAT, scale=-1.0)
                     pop([mm(pf[:, 0:480], T.idb[:], F[:, 16 + n * 480:496 + n * 480], True, False), mm(pf[:, 0:480], T.idb[:], mk, False, True)],
                         ["idb", "q%d" % k, "f" + K], ["pf%d" % k], 960)
                     act(T.ab[:, c], pf[:, 0:480], AF.Abs, [], ["pf%d" % k, "ab" + K], 480)
                     continue
-                tt(T.d[:, c], T.vm[:, 0:2048].indirect(T.h16[:, h * 128 + n * 30:h * 128 + n * 30 + 30]), F[:, 16 + n * 480:496 + n * 480],
-                   A.subtract, VM + ["h16%d%d" % (h, Q), "f" + K], ["d" + K], 480, GAT)
+                tt(T.d[:, c], src, F[:, 16 + n * 480:496 + n * 480], A.subtract, [VM, "h16%d%d" % (h, Q), "f" + K], ["d" + K], 480, GTT)
                 act(T.ab[:, c], T.d[:, c], AF.Abs, ["d" + K], ["ab" + K], 480)
+            sign = h * 2 + Q in PLAN["a_near"]
+            for n0, n1 in ([(0, 1), (1, 2)] if h * 2 + Q in PLAN["fine_near"] else [(0, 2)]):
+                c = slice(o + (2 * Q + n0) * 480, o + (2 * Q + n1) * 480)
+                RK = [TOL] + ["ab%d%d" % (h, 2 * Q + x) for x in range(n0, n1)]
+                WK = ["cl%d%d" % (h, 2 * Q + x) for x in range(n0, n1)]
+                if sign:
+                    act(T.cl[:, c], T.ab[:, c], AF.Sign, RK, WK, 480 * (n1 - n0), bias=tol, scale=-1.0)
+                else:
+                    ts(T.cl[:, c], T.ab[:, c], tol, -0.21875, A.is_le, A.add, RK, WK, 480 * (n1 - n0), 0.5)
             s = o + Q * 960
-            K2 = ["%d%d" % (h, 2 * Q), "%d%d" % (h, 2 * Q + 1)]
-            sign = (t, h, Q) in A_NEAR
-            if sign:
-                act(T.cl[:, s:s + 960], T.ab[:, s:s + 960], AF.Sign, ["tol"] + ["ab" + k for k in K2], ["cl%d%d" % (h, Q)], 960,
-                    bias=T.tol[:, 0:1], scale=-1.0)
-            else:
-                ts(T.cl[:, s:s + 960], T.ab[:, s:s + 960], T.tol[:, 0:1], -0.6875, A.is_le, A.add, ["tol"] + ["ab" + k for k in K2],
-                   ["cl%d%d" % (h, Q)], 960, 0.5)
-            far = T.pc[:, 120 + Q * 60:180 + Q * 60]
-            pop([mm(far, T.zf[:, 15 - r:143 - r], T.ab[:, s + r:s + 960:16], r == 0, False) for r in range(16)]
-                + [mm(far, T.idb[:], T.m16[:, 0:60], False, False),
-                   mm(far, T.idb[:], T.um[:, h * 128 + Q * 60:h * 128 + Q * 60 + 60], False, True)],
-                ["zf", "idb", "m16", "um" + H] + ["ab" + k for k in K2], ["pc"], 1152)
-            cnt = T.pc[:, Q * 60:Q * 60 + 60]
-            if sign:
-                pop([mm(cnt, T.idb[:], T.c3[:, 0:60], True, False)]
-                    + [mm(cnt, T.zs[:, 15 - r:143 - r], T.cl[:, s + r:s + 960:16], False, r == 15) for r in range(16)],
-                    ["zs", "c3", "idb", "cl%d%d" % (h, Q)], ["pc"], 1088)
-            else:
-                pop([mm(cnt, T.zc[:, 15 - r:143 - r], T.cl[:, s + r:s + 960:16], r == 0, r == 15) for r in range(16)],
-                    ["zc", "cl%d%d" % (h, Q)], ["pc"], 1024)
-        tt(T.pc[:, 0:120], T.pc[:, 0:120], T.b2[:, h * 128:h * 128 + 120], A.max, ["b2" + H], ["pc"], 120, 1.0)
+            far, cnt = T.pc[:, 120 + Q * 60:180 + Q * 60], T.pc[:, Q * 60:Q * 60 + 60]
+            pop([mm(far, T.zf[:, 15 - r:143 - r], T.ab[:, s + r:s + 960:16], False, False) for r in range(16)],
+                ["zf", "key", "ab%d%d" % (h, 2 * Q), "ab%d%d" % (h, 2 * Q + 1)], ["far%d" % Q], 1024)
+            z = T.zs if sign else T.zc
+            pop([mm(cnt, z[:, 15 - r:143 - r], T.cl[:, s + r:s + 960:16], False, False) for r in range(16)]
+                + ([mm(cnt, pos3, T.r22[0:1, 0:60], False, False)] if sign else []),
+                ["zc", "key", "cl%d%d" % (h, 2 * Q), "cl%d%d" % (h, 2 * Q + 1)] + (["zs", "r22", "c3"] if sign else []), ["cnt%d" % Q], 1024 + 64 * sign)
+        cnt = T.pc[:, 0:120]
+        pop([mm(cnt, pos3, T.r48[0:1, 0:120], False, False), mm(cnt, neg3, T.r48[0:1, 0:120], False, False),
+             mm(cnt, T.ck[0:2, :], T.m64[0:2, 0:120], False, False), mm(cnt, T.idl[:], T.lt[:, nc], False, False),
+             mm(cnt, T.idh[:], T.hf[:, nc], False, True)],
+            ["c3", "r48", "ck", "m64", "idl", "idh", "lt" + H, "hf" + H, "far0", "far1", "far2", "cnt0", "cnt1"], ["pc"], 600)
         vop(lambda: V.tensor_tensor_scan(T.sc[:, h * 256:h * 256 + 240], T.rbig[:], T.pc[:, 0:240], 0.0, A.add, A.min), ["rbig"], ["pc", "sc" + H], 240)
 
     def stage_d(t, h):
         H = str(h)
         c = slice(h * 128, h * 128 + 128)
-        ti = lambda j: T.ti[:, h * 64 + j * 8:h * 64 + j * 8 + 8]
-        hx = T.hx[:, h * 8:h * 8 + 8]
-        sF = T.sn[:, h * 16 + 8:h * 16 + 16]
-        b = h * 32
-        cp(T.ti[:, h * 64:h * 64 + 16], T.sc[:, h * 256 + 14:h * 256 + 240:15], ["sc" + H], ["ki" + H], 16)
-        ts(ti(2), ti(0), 0x7007FF, None, A.bitwise_and, None, ["ki" + H], ["hi" + H], 8)
-        ts(hx, ti(2), 2048.0, None, A.min, None, ["hi" + H], ["hx" + H], 8)
-        tt(T.rb[:, c], hx.indirect(offE), T.diag[:], A.mult, ["hx" + H, "offE", "diag"], ["rb" + H], 128, GAT)
+        ki = lambda j, n=8: T.ki[:, h * 32 + j * 8:h * 32 + j * 8 + n]
+        b = h * 64
+        x = h * 32
+        u = t * 2 + h
+        cp(ki(0, 16), T.sc[:, h * 256 + 14:h * 256 + 240:15], ["sc" + H], ["ki" + H], 16)
+        ts(ki(2), ki(0), 10, 0x107FF, A.arith_shift_right, A.bitwise_and, ["ki" + H], ["hi" + H], 8)
+        ts(T.xb[:, x + 8:x + 16], ki(2), 2048.0, None, A.min, None, ["hi" + H], ["hx" + H], 8)
+        tt(T.rb[:, c], ki(2).indirect(offE), T.dtop[:], A.min, ["hi" + H, "offE", "dtop"], ["rb" + H], 128, GTT)
         pop([mm(T.pd[:, 0:128], T.boh[:], T.rb[:, c], True, True)], ["boh", "rb" + H], ["pd"], 128)
-        cp(T.hb[:, c], T.pd[:, 0:128], [], ["pd", "hb" + H], 128)
+        if h in PLAN["a_hb"]:
+            act(T.hb[:, c], T.pd[:, 0:128], AF.Copy, [], ["pd", "hb" + H], 128)
+        else:
+            cp(T.hb[:, c], T.pd[:, 0:128], [], ["pd", "hb" + H], 128)
         ne = 9 if h == 0 else 17
+        e0 = 9 * h
         for j in range(ne):
-            out = T.eq[:, j * 128:(j + 1) * 128]
+            out = T.eq[:, (e0 + j) * 128:(e0 + j + 1) * 128]
+            E = ["eq%d" % (e0 + j)]
             if j < 8:
-                ts(out, T.hb[:, c], T.hx[:, h * 8 + j:h * 8 + j + 1], T.wsc[:, j * 16 + 15:j * 16 + 16], A.is_equal, A.mult,
-                   ["hb" + H, "hx" + H, "wsc"], ["eq%d" % j], 128, 0.5)
+                ts(out, T.hb[:, c], T.xb[:, x + 8 + j:x + 9 + j], T.wsc[:, j * 16 + 15:j * 16 + 16], A.is_equal, A.mult,
+                   ["hb" + H, "hx" + H, "wsc"], E, 128, 0.5)
             elif j == 8:
-                ts(out, T.hb[:, c], 2048.0, float(2 ** 62), A.is_equal, A.mult, ["hb" + H], ["eq%d" % j], 128, 0.5)
+                ts(out, T.hb[:, c], 2048.0, float(2 ** 62), A.is_equal, A.mult, ["hb" + H], E, 128, 0.5)
             else:
-                ts(out, T.hb[:, c], T.hx[:, j - 9:j - 8], float(2 ** 62), A.is_equal, A.mult, ["hb" + H, "hx0"], ["eq%d" % j], 128, 0.5)
-        grp = [list(range(0, 5)), list(range(5, 9))] + ([list(range(9, 13)), list(range(13, 17))] if h else [])
-        for gi_, js in enumerate(grp):
-            pop([mm(T.pd[:, 128:256], T.bob[:], T.eq[:, j * 128:(j + 1) * 128], j == 0, j == ne - 1) for j in js],
-                ["bob"] + ["eq%d" % j for j in js], ["pd"], 128 * len(js))
-        ts(T.dl[:, b:b + 8], ti(0), 5, 15 * 64, A.arith_shift_right, A.bitwise_and, ["ki" + H], ["dlT" + H], 8)
-        ts(T.dl[:, b + 24:b + 32], ti(0), 7, 15 * 16, A.arith_shift_right, A.bitwise_and, ["ki" + H], ["dlF" + H], 8)
-        tt(T.dl[:, b + 8:b + 16], hx, T.base[:, b + 8:b + 16], A.subtract, ["hx" + H, "baseS" + H], ["dlS" + H], 8)
-        ts(T.base[:, b + 16:b + 24], ti(1), 15, None, A.bitwise_and, None, ["ki" + H], ["bases" + H], 8)
-        tt(T.dl[:, b + 16:b + 24], sF, T.base[:, b + 16:b + 24], A.subtract, ["sF" + H, "bases" + H], ["dls" + H], 8)
+                ts(out, T.hb[:, c], T.xb[:, j - 1:j], float(2 ** 62), A.is_equal, A.mult, ["hb" + H, "hx0"], E, 128, 0.5)
+        cut = [0, 4, 7, 9] if h == 0 else [0, 5, 10, 14, 17]
+        for i in range(len(cut) - 1):
+            js = range(cut[i], cut[i + 1])
+            pop([mm(T.pd[:, 128:256], T.bob[:], T.eq[:, (e0 + j) * 128:(e0 + j + 1) * 128], j == 0, j == ne - 1) for j in js],
+                ["bob"] + ["eq%d" % (e0 + j) for j in js], ["pd"], 128 * len(js))
+        ts(T.dl[:, b + 24:b + 40], ki(0, 16), 960, None, A.bitwise_and, None, ["ki" + H], ["dlT" + H], 16)
+        ts(T.dl[:, b + 16:b + 24], ki(0), 2, 240, A.arith_shift_right, A.bitwise_and, ["ki" + H], ["dlF" + H], 8)
+        tt(T.dl[:, b:b + 16], T.xb[:, x:x + 16], T.dl[:, b + 32:b + 48], A.subtract, ["s" + H, "hx" + H, "dlT" + H, "baseS" + H], ["dlS" + H], 16)
         tt(T.wd[:, c], T.pd[:, 128:256], T.thr[:], A.is_lt, ["thr"], ["pd", "wd" + H], 128, 1.0)
-        vop(lambda: V.tensor_tensor_scan(WS[h][:], T.r01[:], T.wd[:, c], 0.0, A.mult, A.add), ["r01", "wd" + H], ["ws" + H], 128)
-        tt(T.xa[:, b:b + 32], WS[h][:, 0:128].indirect(offW), T.dl[:, b:b + 32], A.mult,
-           ["ws" + H, "offW", "dlT" + H, "dlF" + H, "dlS" + H, "dls" + H], ["xa" + H], 32, GAT)
-        tt(T.xb[:, b:b + 32], T.xa[:, b:b + 32], T.base[:, b:b + 32], A.add,
-           ["xa" + H, "baseT" + H, "baseS" + H, "baseF" + H, "bases" + H], ["xb" + H], 32)
-        so = (t * 2 + h) * SW
+        vop(lambda: V.tensor_tensor_scan(WS[h][:], T.r01[:], T.wd[:, c], 0.0, A.mult, A.add), ["r01", "wd" + H], ["ws" + H], 128, 0.5)
+        tt(T.xa[:, x:x + 32], WS[h][:, 0:128].indirect(offW), T.dl[:, b:b + 32], A.mult,
+           ["ws" + H, "offW", "dlT" + H, "dlF" + H, "dlS" + H], ["xa" + H], 32, GTT)
+        tt(T.xb[:, x:x + 32], T.xa[:, x:x + 32], T.dl[:, b + 32:b + 64], A.add,
+           ["xa" + H, "baseT" + H, "baseS" + H, "baseF" + H, "dlT" + H], ["xb" + H, "s" + H, "hx" + H], 32)
+        so = (u + 2) * SW
         OF = "of%d%d" % (t, h)
-        cp(T.snd[:, so + 128:so + 160], T.xb[:, b:b + 32], ["xb" + H], [OF], 32)
-        cp(T.gi[:, c], TB[h][:, 0:1024].indirect(T.snd[:, so + 128:so + 136]), [OF, "tt%d0" % h, "tt%d1" % h], ["gi" + H], 128, GAT)
+        cp(T.lb[:, so + 128:so + 152], T.xb[:, x + 8:x + 32], ["xb" + H, "hx" + H], [OF], 24)
+        cp(T.gi[:, c], TB[h][:, 0:1024].indirect(T.lb[:, so + 144:so + 152]), [OF, "tt%d0" % h, "tt%d1" % h], ["gi" + H], 128, GAT)
         o = h * 128
-        arr = "arr%d" % (t * 2 + h)
         if t < STEPS - 1:
             ts(T.lp[:, o:o + 64], T.gi[:, o:o + 128:2], 2047, None, A.bitwise_and, None, ["gi" + H], ["lp0" + H], 64)
             ts(T.lp[:, o + 64:o + 128], T.gi[:, o + 1:o + 128:2], 11, None, A.arith_shift_right, None, ["gi" + H], ["lp1" + H], 64)
-            cp(T.snd[:, so:so + 128], T.lp[:, c], ["lp0" + H, "lp1" + H], ["sl%d%d" % (t, h)], 128)
-            lo = so + 2 * SW
-            src, dst, R, W = T.snd[:, so:so + SW], T.lb[:, lo:lo + SW], [OF, "sl%d%d" % (t, h)], ["lb%d%d" % (t + 1, h)]
+            cp(T.lb[:, so:so + 128], T.lp[:, c], ["lp0" + H, "lp1" + H], ["lb%d%d" % (t + 1, h)], 128)
         else:
             ts(T.lp[:, o:o + 128:2], T.gi[:, o:o + 128:2], 2047, None, A.bitwise_and, None, ["gi" + H], ["lp0" + H], 64)
             ts(T.lp[:, o + 1:o + 128:2], T.gi[:, o + 1:o + 128:2], 11, None, A.arith_shift_right, None, ["gi" + H], ["lp1" + H], 64)
-            cp(T.fo[:, h * 256:h * 256 + 128], T.lp[:, c], ["lp0" + H, "lp1" + H], ["foL" + H], 128)
-            tt(T.rs[:, c], T.xb[:, b + 16:b + 24].indirect(offE), T.diag[:], A.mult, ["xb" + H, "offE", "diag"], ["rsb" + H], 128, GAT)
+            cp(T.fo[:, c], T.lp[:, c], ["lp0" + H, "lp1" + H], ["foL" + H], 128)
+            tt(T.rs[:, c], T.xb[:, x:x + 8].indirect(offE), T.diag[:], A.mult, ["s" + H, "offE", "diag"], ["rsb" + H], 128, GTT)
             pop([mm(T.pd[:, 0:128], T.bob[:], T.rs[:, c], True, True)], ["bob", "rsb" + H], ["pd"], 128)
-            act(T.fo[:, h * 256 + 128:h * 256 + 256], T.pd[:, 0:128], AF.Copy, [], ["pd", "foS" + H], 128)
-            src, dst, R, W = T.fo[:, h * 256:h * 256 + 256], T.fl[:, h * 256:h * 256 + 256], ["foL" + H, "foS" + H], ["fl" + H]
-        op("r", lambda: [g.remote_dma(dst, src, T.sem[arr], T.sem.sent, pid, rid, msk)], R, W, 4.0, arr, len(eng))
-        act(T.fs[:, c], FB[h][:, 0:1936].indirect(T.snd[:, so + 152:so + 160]), AF.Copy,
-            [OF, "fz" + H] + ["f%d%d" % (h, n) for n in range(4)], ["fs" + H], 128, GAT)
+            act(T.fo[:, 256 + o:384 + o], T.pd[:, 0:128], AF.Copy, [], ["pd", "foS" + H], 128, scale=1.0 / 64)
+        send(1, T.uo[:, u * 8:u * 8 + 8], T.lb[:, so + 128:so + 136], [OF], ["uo%d%d" % (t, h)], "ao%d" % u, TUNE["hop"])
+        act(T.fs[:, u * UW:u * UW + 128], FB[h][:, 0:1936].indirect(T.lb[:, so + 136:so + 144]), AF.Copy,
+            [OF, "fz" + H] + ["f%d%d" % (h, n) for n in range(4)], ["fs%d%d" % (t, h)], 128, GAT)
+        R, w = ["fs%d%d" % (t, h)], 128
         if t < STEPS - 1:
             pop([mm(T.pd[:, 256 + h * 8:264 + h * 8], T.bob[:], WS[h][:, 15:128:16], True, True)], ["bob", "ws" + H], ["pd"], 64)
+            if h == 1:
+                vop(lambda: V.tensor_reduce(T.tol[:, 1:2], T.pd[:, 256:272], AxisListType.X, A.add, negate=True), [], ["pd", "tn"], 16)
+                cp(T.toli[:, 0:1], T.tol[:, 1:2], ["tn"], ["tni"], 1)
+                ts(T.toli[:, 1:2], T.toli[:, 0:1], 3, None, A.bitwise_and, None, ["tni"], ["tn3"], 1)
+                ts(T.fs[:, u * UW + 128:u * UW + 129], T.toli[:, 1:2], 2.5, None, A.add, None, ["tn3"], ["tl%d" % t], 1)
+                R, w = R + ["tl%d" % t], 129
+        send(1, T.uf[:, u * UW:u * UW + w], T.fs[:, u * UW:u * UW + w], R, ["uf%d%d" % (t, h)], "au%d" % u, TUNE["hop"])
 
     def stage_w(t, h):
-        so = (t * 2 + h) * SW
-        cp(T.vm[:, 0:2304].indirect(T.snd[:, so + 136:so + 144]), T.fs[:, h * 128:h * 128 + 128],
-           ["of%d%d" % (t, h), "fs%d" % h], VM, 128, 3.5)
+        u = t * 2 + h
+        cp(T.vm[:, (t + 1) * MW:(t + 2) * MW].indirect(T.uo[:, u * 8:u * 8 + 8]), T.uf[:, u * UW:u * UW + 128],
+           ["uo%d%d" % (t, h), "uf%d%d" % (t, h)], ["vm%d" % (t + 1)], 128, TUNE["sca"])
         if h == 1 and t < STEPS - 1:
-            vop(lambda: V.tensor_reduce(T.tol[:, 1:2], T.pd[:, 256:272], AxisListType.X, A.add, negate=True), [], ["pd", "tn"], 16)
-            cp(T.toli[:, 0:1], T.tol[:, 1:2], ["tn"], ["tni"], 1)
-            ts(T.toli[:, 1:2], T.toli[:, 0:1], 3, None, A.bitwise_and, None, ["tni"], ["tn3"], 1)
-            ts(T.tol[:, 0:1], T.toli[:, 1:2], 2.5, None, A.add, None, ["tn3"], ["tol"], 1)
+            send_memory(t + 1, [])
 
     for t in range(STEPS):
         for fn, h in ORDER:
@@ -472,124 +544,141 @@ def build_ops(g, core, T, topo, rank):
             {"a": stage_a, "b": stage_b, "t": stage_t, "d": stage_d, "w": stage_w}[fn](t, h)
     pr[0] += 1
 
-    dma(T.yv[:, 0:2048 - ROT], T.vm[:, ROT:2048], VM, [], "o0", 4.0)
-    dma(T.yv[:, 2048 - ROT:2048], T.vm[:, 0:ROT], VM, [], "o1", 4.0, "a")
-    for h in range(2):
-        dma(T.yl[:, h * 128:h * 128 + 128], T.fl[:, h * 256:h * 256 + 128], ["fl%d" % h], [], "o%d" % (2 + h), 2.5)
-        dma(T.ys[:, h * 128:h * 128 + 128], T.fl[0:128:16, h * 256 + 128:h * 256 + 256], ["fl%d" % h], [], "o%d" % (4 + h), 2.5)
-    return ops, len(eng)
+    dma(T.yv[:, 0:1024], T.vm[:, 4 * MW:4 * MW + 1024], ["vm4"], [], "o0", 3.5)
+    dma(T.yv[:, 1024:2048], T.vm[:, 4 * MW + 1024:4 * MW + 2048], ["vm4"], [], "o1", 3.5, "a")
+    dma(T.yl[:], T.fo[:, 0:256], ["foL0", "foL1"], [], "o2", 2.5)
+    dma(T.ys[:], T.fo[0:128:16, 256:512], ["foS0", "foS1"], [], "o3", 2.5)
+    return ops
 
 
-def order_ops(ops):
-    n = len(ops)
-    lastw, readers = {}, {}
-    deps = []
+def graph(ops):
+    lastw, readers, lastx = {}, {}, {}
+    deps, hard = [], []
     for i, o in enumerate(ops):
-        d = set()
-        for k in o["R"]:
-            if k in lastw:
-                d.add(lastw[k])
+        raw = {lastw[k] for k in o["R"] if k in lastw}
+        d = set(raw)
         for k in o["W"]:
             if k in lastw:
                 d.add(lastw[k])
             d.update(readers.get(k, []))
+        raw = set(d)
+        d.update(lastx[k] for k in o["X"] if k in lastx)
         d.discard(i)
         deps.append(sorted(d))
+        hard.append({j for j in d if j != i and (j in raw and o["e"] != "p") or ops[j]["e"] != o["e"] or ops[j]["sem"] or o["sem"]})
         for k in o["R"]:
             readers.setdefault(k, []).append(i)
         for k in o["W"]:
             lastw[k] = i
             readers[k] = []
-    succ = [[] for _ in range(n)]
+        for k in o["X"]:
+            lastx[k] = i
+    return deps, hard
+
+
+def place(pre, post, queue, hold, rank):
+    n = len(pre)
+    S, E = {e: [] for e in "vapgs"}, {e: [] for e in "vapgs"}
+    left = [len(p) for p in pre]
+    ready = [(rank[i], i) for i in range(n) if not left[i]]
+    st = [0.0] * n
+    while ready:
+        ready.sort(reverse=True)
+        i = ready.pop()[1]
+        a = 0.0
+        for j, w in pre[i]:
+            if st[j] + w > a:
+                a = st[j] + w
+        s, e, h = S[queue[i]], E[queue[i]], hold[i]
+        x = m = len(s)
+        while x > 0 and e[x - 1] > a:
+            x -= 1
+        while x < m and s[x] < a + h:
+            a = e[x]
+            x += 1
+        s.insert(x, a)
+        e.insert(x, a + h)
+        st[i] = a
+        for j in post[i]:
+            left[j] -= 1
+            if not left[j]:
+                ready.append((rank[j], j))
+    return np.array(st)
+
+
+def order_ops(ops):
+    n = len(ops)
+    deps, hard = graph(ops)
+    queue = ["g" if o["e"] == "r" else o["e"] for o in ops]
+    hold = [(1.0 if o["e"] == "r" else 0.1) if o["sem"] else o["dur"] for o in ops]
+    dur = [o["dur"] for o in ops]
+    pre = [[(j, dur[j] + (TUNE["lat"] if j in hard[i] else 0.0)) for j in deps[i]] for i in range(n)]
+    post = [[] for _ in range(n)]
+    rpre = [[(n, dur[i] - hold[i])] for i in range(n)] + [[]]
     for i in range(n):
-        for j in deps[i]:
-            succ[j].append(i)
-    LAT = TUNE["lat"]
+        for j, w in pre[i]:
+            post[j].append(i)
+            rpre[j].append((i, hold[i] + w - hold[j]))
+    rpost = [list(d) for d in deps] + [list(range(n))]
     lev = [0.0] * n
-    for i in range(n - 1, -1, -1):
-        lev[i] = ops[i]["dur"] + max([lev[j] + LAT for j in succ[i]], default=0.0)
-    queue = lambda o: "g" if o["e"] == "r" else o["e"]
-    hold = lambda o: (1.0 if o["e"] == "r" else 0.1) if o["sem"] else o["dur"]
-    qs = [queue(o) for o in ops]
-    hs = [hold(o) for o in ops]
     pr = [o["pr"] for o in ops]
     for i in range(n - 1, -1, -1):
-        if pr[i] == 0 and succ[i]:
-            pr[i] = min(pr[j] for j in succ[i])
-
-    dur = [o["dur"] for o in ops]
-
-    def place(rank_of, pre, post, back):
-        busy = {e: [] for e in "vapgs"}
-        left = [len(d) for d in pre]
-        ready = [(rank_of[i], i) for i in range(n) if left[i] == 0]
-        st = [0.0] * n
-        while ready:
-            ready.sort(reverse=True)
-            i = ready.pop()[1]
-            r = max([st[k] + dur[k] + LAT for k in pre[i]], default=0.0)
-            lead = dur[i] - hs[i] if back else 0.0
-            a = r + lead
-            lst = busy[qs[i]]
-            at = len(lst)
-            for x in range(len(lst)):
-                if lst[x][1] <= a:
-                    continue
-                if lst[x][0] >= a + hs[i]:
-                    at = x
-                    break
-                a = lst[x][1]
-            lst.insert(at, (a, a + hs[i]))
-            st[i] = a - lead
-            for j in post[i]:
-                left[j] -= 1
-                if left[j] == 0:
-                    ready.append((rank_of[j], j))
-        return st
-
-    best = None
-    for seed in SEEDS:
-        rng = np.random.default_rng(seed)
-        w, noise = rng.uniform(0.0, 8.0), rng.uniform(0.0, 1.0)
-        st = place([float(pr[i] * w - lev[i] + noise * rng.random()) for i in range(n)], deps, succ, False)
-        for rnd in range(ROUNDS):
-            span = max(st[i] + dur[i] for i in range(n))
-            if best is None or span < best[0]:
-                best = (span, st)
-            bk = place([-(st[i] + dur[i]) for i in range(n)], succ, deps, True)
-            st = place([-(bk[i] + dur[i]) for i in range(n)], deps, succ, False)
+        lev[i] = max(w - hold[j] + hold[i] + lev[j] for j, w in rpre[i] if j < n) if post[i] else dur[i]
+        if pr[i] == 0 and post[i]:
+            pr[i] = min(pr[j] for j in post[i])
+    names, role = {}, []
+    for o in ops:
+        key = ((o["pr"] - 1) % len(ORDER), o["e"], len([1 for q in ops[:len(role)] if q["pr"] == o["pr"] and q["e"] == o["e"]]))
+        role.append(names.setdefault(key if 0 < o["pr"] <= STEPS * len(ORDER) else len(role), len(names)))
+    role, hs, du = np.array(role), np.array(hold), np.array(dur)
+    rng = np.random.default_rng(TUNE["seed"])
+    noise = lambda: (rng.random(len(names)) * rng.choice(TUNE["noise"]) * (rng.random(len(names)) < rng.choice([0.05, 0.2, 1.0])))[role]
+    st = place(pre, post, queue, hold, [pr[i] * TUNE["w"] - lev[i] for i in range(n)])
+    best = cur = (max(st + du), st)
+    for rnd in range(TUNE["rounds"]):
+        bk = place(rpre, rpost, queue + ["s"], hold + [0.0], list(noise() - (cur[1] + hs)) + [-1e9])
+        st = place(pre, post, queue, hold, list(noise() - (bk[:n] + hs)))
+        if max(st + du) < cur[0] + TUNE["slack"] * (1 - rnd / TUNE["rounds"]):
+            cur = (max(st + du), st)
+        if cur[0] < best[0]:
+            best = cur
     st = best[1]
-    return deps, sorted(range(n), key=lambda i: (st[i], i)), [st[i] + dur[i] for i in range(n)]
+    return hard, sorted(range(n), key=lambda i: (st[i], i)), [float(x) for x in st + du]
+
+
+PLACED = []
 
 
 def rank_program(g, core, T, topo):
     rank = T.rank_of(core)
     if rank is None:
         return
-    ops, ne = build_ops(g, core, T, topo, rank)
-    deps, order, end = order_ops(ops)
+    ops = build_ops(g, core, T, topo, rank)
+    if not PLACED:
+        PLACED.append(order_ops(ops))
+    hard, order, end = PLACED[0]
     Q = {"v": g.vector, "a": g.scalar, "p": g.tensor, "g": g, "s": g.sync, "r": g}
     own = {"v": "cv", "a": "ca", "p": "cp", "g": "cg"}
     count = {s: 0 for s in SEMAPHORES}
-    done = {}
+    done, knew = {}, {}
     seen = {e: {} for e in "vapgs"}
-    nsent = 0
     for i in order:
         o = ops[i]
         e = "g" if o["e"] == "r" else o["e"]
-        need = {}
-        for j in deps[i]:
+        for j in sorted(hard[i], key=lambda j: -end[j]):
             s, v = done[j]
-            need[s] = max(need.get(s, 0), v)
-        for s, v in need.items():
             if seen[e].get(s, 0) < v:
+                v = max(done[k][1] for k in hard[i] if done[k][0] == s)
                 Q[e].wait_ge(T.sem[s], v)
                 seen[e][s] = v
+            for s, v in knew[j].items():
+                seen[e][s] = max(seen[e].get(s, 0), v)
         ins = o["fn"]()
+        knew[i] = {} if o["e"] == "r" else dict(seen[e])
         if o["e"] == "r":
             done[i] = (o["sem"], o["val"])
             count[o["sem"]] = o["val"]
-            nsent += 1
+            count["sent"] += o["val"]
         elif o["sem"]:
             ins[0].then_inc(T.sem[o["sem"]], 16)
             count[o["sem"]] = 16
@@ -600,7 +689,6 @@ def rank_program(g, core, T, topo):
                 x.then_inc(T.sem[s], 1)
             count[s] += len(ins)
             done[i] = (s, count[s])
-    count["sent"] = nsent * ne
     for s in SEMAPHORES:
         if count[s]:
             g.wait_ge(T.sem[s], count[s])

@@ -6,7 +6,7 @@ AF = ActivationFunctionType
 STEPS = 4
 SW = 160
 XW = 2192
-MW = 2304
+MW = 3072
 UW = 144
 BIG = float(2 ** 29)
 SHIFT = -127.0625
@@ -97,7 +97,8 @@ SCRATCH = {
     "lp": ("sbuf", [128, 256], "int32"),
     "ki": ("sbuf", [128, 64], "int32"),
     "dl": ("sbuf", [128, 128], "int32"),
-    "xa": ("sbuf", [128, 64], "float32"),
+    "xa": ("sbuf", [128, 72], "float32"),
+    "si": ("sbuf", [128, 512], "int32"),
     "xb": ("sbuf", [128, 64], "float32"),
     "pt": ("psum", [128, 1024], "bfloat16"),
     "pf0": ("psum", [128, 512], "float32"),
@@ -118,18 +119,18 @@ ORDER = [("a", 0), ("t", 0), ("a", 1), ("b", 0), ("t", 1), ("b", 1), ("d", 0), (
 PLAN = {
     "v_gather": [], "v_gather0": [1, 3],
     "a_turn": [],
-    "q_mod": [0, 1, 2, 3, 4, 5, 6, 7],
+    "q_mod": [0, 1, 2, 3],
     "v_mod": [0, 1, 2, 3],
     "v_f": [],
     "a_mark": [],
     "a_near": [0, 1, 2, 3],
     "v_table": [],
-    "a_hb": [0, 1],
+    "a_hb": [], "a_eq": [0, 1], "a_pm": 4, "a_small": ["lh0", "lh1", "um0", "um1"], "round16": True, "scan_int": True,
     "fine": [0, 2], "fine_near": [1, 3],
     "banks": {"a": [0, 1, 2], "t": [3], "m": [3]},
 }
 TUNE = {"cyc": 0.83e-3 * 1.1, "pe": 0.42e-3 * 1.25, "lat": 0.14, "gat": 1.5, "gtt": 1.75, "sca": 3.5, "hop": 3.6, "bulk": 12.0,
-        "vfix": 0.045, "afix": 0.06, "pfix": 0.06, "w": 6.0, "noise": [0.05, 0.2, 0.5, 1.0, 2.0], "slack": 0.4, "seed": 0, "rounds": 3000}
+        "vfix": 0.045, "afix": 0.06, "pfix": 0.06, "w": 6.0, "noise": [0.05, 0.2, 0.5, 1.0, 2.0], "slack": 0.4, "seed": 0, "rounds": 8000}
 
 
 def build_ops(g, core, T, topo, rank):
@@ -179,6 +180,12 @@ def build_ops(g, core, T, topo, rank):
     def act(out, in_, fn, R, W, n, c=1.0, bias=0.0, scale=1.0):
         aop(lambda: S.activation(out, in_, fn, bias=bias, scale=scale), R, W, n, c)
 
+    def lin(kind, out, in_, scale, bias, R, W, n, c=1.0):
+        if kind in PLAN["a_small"]:
+            act(out, in_, AF.Identity if bias else AF.Copy, R, W, n, 1.0, bias=bias, scale=scale)
+        else:
+            ts(out, in_, scale, bias, A.mult, A.add, R, W, n, c)
+
     def mm(out, l, r, st, sp):
         return lambda: P.matmul(out, l, r, st, sp)
 
@@ -189,7 +196,7 @@ def build_ops(g, core, T, topo, rank):
     dma(T.xs[:, 0:1024], T.x[:, 0:1024], [], ["x0"], "dx0", 3.5)
     dma(T.xs[:, 1024:2048], T.x[:, 1024:2048], [], ["x0b"], "dx1", 3.5, "a")
     dma(T.wi[:, 0:1], T.wt[:], [], ["wi"], "dw", 2.5)
-    vop(lambda: V.memset(T.sraw[:], 0), [], ["sraw"], 256)
+    gop(lambda: g.iota(T.sraw[:], [[0, 256]], 0, 0), [], ["sraw"], 256)
     dma(T.sraw[0:128:16, :], T.s0[:], [], ["sraw"], "ds", 2.5)
     dma(T.vm[:, 0:2048], T.v[:], [], ["vm0"], "dv0", 5.0)
 
@@ -231,11 +238,11 @@ def build_ops(g, core, T, topo, rank):
         ts(p0, pK, 0.0, 256.0, A.is_equal, A.mult, [CP], ["p0"], 1)
         ts(T.cf[:, 48:64], T.cf[:, 0:16], p0, None, A.subtract, None, ["cf", "p0"], ["cf3"], 16)
         for r in range(8):
-            ts(T.coef[:, r:120:8], T.cf[:, 49:64], T.bof[:, r:r + 1], None, A.mult, None, ["cf3", "bof"], [COEF[r]], 16)
+            act(T.coef[:, r:120:8], T.cf[:, 49:64], AF.Copy, ["cf3", "bof"], [COEF[r]], 16, scale=T.bof[:, r:r + 1])
         act(T.coen[:, 0:120], T.coef[:, 0:120], AF.Copy, COEF, ["coen"], 120, scale=-1.0)
     if PLAN["q_mod"]:
         for r in range(8):
-            ts(T.coeq[:, r:120:8], T.cf[:, 1:16], T.bof[:, r:r + 1], None, A.mult, None, ["cf", "bof"], [COEQ[r]], 16)
+            act(T.coeq[:, r:120:8], T.cf[:, 1:16], AF.Copy, ["cf", "bof"], [COEQ[r]], 16, scale=T.bof[:, r:r + 1])
     ts(T.xs[:, 2048:XW], T.ion[:], pZ, pW, A.is_equal, A.mult, ["ion", "pz", "pw"], ["x0w"], 144)
     ts(T.zc[:], T.ion[:], pZ, float(2 ** 22), A.is_equal, A.mult, ["ion", "pz"], ["zc"], 144)
     act(T.zf[:], T.zc[:], AF.Copy, ["zc"], ["zf"], 144, scale=2.0 ** -8)
@@ -245,13 +252,13 @@ def build_ops(g, core, T, topo, rank):
     act(T.boh[:], T.bob[:], AF.Copy, ["bob"], ["boh"], 128)
     ts(T.diag[:], T.r16[:], pK, None, A.is_equal, None, ["r16", CP], ["diag"], 128)
     act(T.dtop[:], T.diag[:], AF.Copy, ["diag"], ["dtop"], 128, scale=2048.0)
-    ts(T.rbig[:], T.m64[:], 64.0, BIG, A.is_equal, A.mult, ["m64"], ["rbig"], 240)
+    act(T.rbig[:], T.m64[:], AF.Relu, ["m64"], ["rbig"], 240, bias=2 * BIG, scale=-BIG / 64)
     offM = T.ofc[:, 32:40]
     ts(T.otmp[:], T.ion[:, 0:128:16], pK, 1.0 / 15, A.add, A.mult, ["ion", CP], ["otmp"], 8)
     ts(T.otmi[:], T.otmp[:], -0.47, None, A.add, None, ["otmp"], ["otmi"], 8)
     ts(offM, T.otmi[:], 7.0, None, A.min, None, ["otmi"], ["offM"], 8)
     for h in range(2):
-        vop(lambda h=h: V.memset(T["f%d" % h][:, 0:16], 0.0), [], ["fz%d" % h], 16)
+        iota(T["f%d" % h][:, 0:16], [[0, 16]], 0, ["fz%d" % h], 16)
     act(T.r01[:], T.r16[:], AF.Sign, ["r16"], ["r01"], 128)
     offE, offW, offK = T.ofc[:, 0:8], T.ofc[:, 8:10], T.ofc[:, 16:32]
     cp(offE, T.ion[:, 0:8], ["ion"], ["offE"], 8)
@@ -261,28 +268,31 @@ def build_ops(g, core, T, topo, rank):
     tt(T.ee[:], T.cf[:, 0:16].indirect(offK), T.kio[:], A.is_equal, ["cf", "offK", "kio"], ["ee"], 256, GTT)
     PM = ["pm%d" % r for r in range(8)]
     for r in range(8):
-        ts(T.pm[:, r * 256:(r + 1) * 256], T.ee[:], T.bof[:, r:r + 1], None, A.mult, None, ["ee", "bof"], [PM[r]], 256, 0.5)
+        if r < PLAN["a_pm"]:
+            act(T.pm[:, r * 256:(r + 1) * 256], T.ee[:], AF.Copy, ["ee", "bof"], [PM[r]], 256, scale=T.bof[:, r:r + 1])
+        else:
+            ts(T.pm[:, r * 256:(r + 1) * 256], T.ee[:], T.bof[:, r:r + 1], None, A.mult, None, ["ee", "bof"], [PM[r]], 256, 0.5)
     vop(lambda: V.memset(T.wd0[:], 0.5), [], ["wd0"], 128)
-    vop(lambda: V.memset(T.thr[:], 0.0), [], ["thr"], 128)
+    iota(T.thr[:], [[0, 128]], 0, ["thr"], 128)
     vop(lambda: V.tensor_tensor_scan(T.wrow[:], T.wd0[:], T.thr[:], float(2 ** 61), A.mult, A.add), ["wd0", "thr"], ["wrow"], 128)
     tt(T.wd0[:], T.wrow[:], T.diag[:], A.mult, ["wrow", "diag"], ["wd0"], 128)
     act(T.thr[:], T.wd0[:], AF.Copy, ["wd0"], ["thr"], 128, scale=2.5)
     vop(lambda: V.tensor_tensor_scan(T.wsc[:], T.r01[:], T.wd0[:], 0.0, A.mult, A.add), ["r01", "wd0"], ["wsc"], 128)
     for h in range(2):
         b = h * 64 + 32
-        ts(T.dl[:, b + 8:b + 16], T.ion[:, 0:128:16], pK, 2048.0 + 128 * h, A.add, A.add, ["ion", CP], ["baseS%d" % h], 8)
+        gop(lambda b=b: g.iota(T.dl[:, b + 8:b + 16], [[128, 8]], 2048, 1), [], ["baseS%d" % h], 8)
         ts(T.dl[:, b + 16:b + 24], T.ion[:, 0:8], 240.0, pK, A.mult, A.add, ["ion", CP], ["baseF%d" % h], 8)
         ts(T.dl[:, b + 24:b + 32], T.ion[:, 0:8], 8.0, pH, A.mult, A.add, ["ion", CP], ["baseT%d" % h], 8)
     vop(lambda: V.memset(T.tol[:, 0:1], 2.5), [], ["tol0"], 1)
 
     for h in range(2):
         for b in range(2):
-            cp(T.lb[:, h * SW + b * 64:h * SW + b * 64 + 64], T.li[:, h * 128 + b:h * 128 + 128:2], ["li"], ["lb0%d" % h], 64)
+            cp(T.lb[:, h * SW + b * 64:h * SW + b * 64 + 64], T.li[:, h * 128 + b:h * 128 + 128:2], ["li"], ["lb0%d" % h + "eo"[b]], 64)
     cp(T.sbf[:], T.sraw[:], ["sraw"], ["sbf"], 256)
     pop([mm(T.pd[:, 0:16], T.zc[:, 15 - r:143 - r], T.sbf[:, r:256:16], r == 0, r == 15) for r in range(16)],
         ["zc", "sbf"], ["pd"], 16 * 64)
     for h in range(2):
-        ts(T.xb[:, h * 32:h * 32 + 8], T.pd[:, h * 8:h * 8 + 8], 2.0 ** -16, None, A.mult, None, [], ["pd", "s%d" % h], 8)
+        act(T.xb[:, h * 32:h * 32 + 8], T.pd[:, h * 8:h * 8 + 8], AF.Copy, [], ["pd", "s%d" % h], 8, scale=2.0 ** -16)
     X0 = ["x0", "x0b", "x0w"]
 
     def send_items(t, after):
@@ -322,9 +332,9 @@ def build_ops(g, core, T, topo, rank):
                     c0 = b * 64 + Q * 32 + e0 * 8
                     out, src = T.a[:, o + c0 * 16:o + (c0 + w) * 16], T.xs[:, t * XW:t * XW + 2048].indirect(T.lb[:, lo + c0:lo + c0 + w])
                     if h * 4 + Q * 2 + b in PLAN["v_gather0" if t == 0 else "v_gather"]:
-                        cp(out, src, XS + [LB], [AK[b]], w * 16, GAT)
+                        cp(out, src, XS + [LB + "eo"[b]], [AK[b]], w * 16, GAT)
                     else:
-                        act(out, src, AF.Copy, XS + [LB], [AK[b]], w * 16, GAT)
+                        act(out, src, AF.Copy, XS + [LB + "eo"[b]], [AK[b]], w * 16, GAT)
                 fns = []
                 for el in range(e0, e1):
                     for b in range(2):
@@ -375,16 +385,16 @@ def build_ops(g, core, T, topo, rank):
                  for r in range(16)], [XZ, "f%d%d" % (h, 2 * Q), "f%d%d" % (h, 2 * Q + 1)], ["pu"], 1024)
             c = slice(h * 128 + u0, h * 128 + u0 + 60)
             K = "%d%d" % (h, Q)
-            cp(T.ui[:, c], T.pu[:, u0:u0 + 60], [], ["pu", "ui" + K], 60)
+            lin("ui" + H, T.ui[:, c], T.pu[:, u0:u0 + 60], 1.0, 0.0, [], ["pu", "ui" + K], 60)
             ts(T.u2[:, c], T.ui[:, c], 4095, None, A.bitwise_and, None, ["ui" + K], ["u2" + K], 60)
-            ts(T.yy[:, c], T.u2[:, c], 1184.0, None, A.add, None, ["u2" + K], ["yy" + K], 60)
+            lin("yy" + H, T.yy[:, c], T.u2[:, c], 1.0, 1184.0, ["u2" + K], ["yy" + K], 60)
             tt(T.sq[:, c], T.yy[:, c], T.u2[:, c], A.mult, ["yy" + K, "u2" + K], ["sq" + K], 60)
             ts(T.h0[:, c], T.sq[:, c], 5, 2047, A.arith_shift_right, A.bitwise_and, ["sq" + K], ["h0" + K], 60)
             cp(T.h16[:, c], T.h0[:, c], ["h0" + K], ["h16" + K], 60)
         c = slice(h * 128, h * 128 + 120)
         ts(T.ul[:, c], T.ui[:, c], 15, None, A.bitwise_and, None, ["ui%d0" % h, "ui%d1" % h], ["ul" + H], 120)
-        ts(T.um[:, c], T.ul[:, c], 64.0, None, A.mult, None, ["ul" + H], ["um" + H], 120)
-        ts(T.hf[:, c], T.h16[:, c], 1.0, None, A.mult, None, ["h16%d0" % h, "h16%d1" % h], ["hf" + H], 120, 0.5)
+        lin("um" + H, T.um[:, c], T.ul[:, c], 64.0, 0.0, ["ul" + H], ["um" + H], 120)
+        lin("hf" + H, T.hf[:, c], T.h16[:, c], 1.0, 0.0, ["h16%d0" % h, "h16%d1" % h], ["hf" + H], 120, 0.5)
         tt(T.lt[:, h * 128:h * 128 + 128], T.xb[:, h * 32:h * 32 + 8].indirect(offM), T.m64[:, 0:128], A.is_gt,
            ["s" + H, "offM", "m64"], ["lt" + H], 128, GTT)
         if h == 1 and t < STEPS - 2:
@@ -395,8 +405,8 @@ def build_ops(g, core, T, topo, rank):
         LB = "lb%d%d" % (t, h)
         H = str(h)
         o = h * 128
-        ts(T.lh[:, o:o + 64], T.lb[:, lo:lo + 64], 1.0 / 2048, None, A.mult, None, [LB], ["lh0" + H], 64, 0.5)
-        ts(T.lh[:, o + 64:o + 128], T.lb[:, lo + 64:lo + 128], 1.0, None, A.mult, None, [LB], ["lh1" + H], 64, 0.5)
+        lin("lh" + H, T.lh[:, o:o + 64], T.lb[:, lo:lo + 64], 1.0 / 2048, 0.0, [LB + "e"], ["lh0" + H], 64, 0.5)
+        lin("lh" + H, T.lh[:, o + 64:o + 128], T.lb[:, lo + 64:lo + 128], 1.0, 0.0, [LB + "o"], ["lh1" + H], 64, 0.5)
         for n in range(2):
             k = nb("t")
             pf = T["pf%d" % k]
@@ -457,7 +467,7 @@ def build_ops(g, core, T, topo, rank):
              mm(cnt, T.ck[0:2, :], T.m64[0:2, 0:120], False, False), mm(cnt, T.idl[:], T.lt[:, nc], False, False),
              mm(cnt, T.idh[:], T.hf[:, nc], False, True)],
             ["c3", "r48", "ck", "m64", "idl", "idh", "lt" + H, "hf" + H, "far0", "far1", "far2", "cnt0", "cnt1"], ["pc"], 600)
-        vop(lambda: V.tensor_tensor_scan(T.sc[:, h * 256:h * 256 + 240], T.rbig[:], T.pc[:, 0:240], 0.0, A.add, A.min), ["rbig"], ["pc", "sc" + H], 240)
+        vop(lambda: V.tensor_tensor_scan((T.si if PLAN["scan_int"] else T.sc)[:, h * 256:h * 256 + 240], T.rbig[:], T.pc[:, 0:240], 0.0, A.add, A.min), ["rbig"], ["pc", "sc" + H], 240)
 
     def stage_d(t, h):
         H = str(h)
@@ -466,8 +476,12 @@ def build_ops(g, core, T, topo, rank):
         b = h * 64
         x = h * 32
         u = t * 2 + h
-        cp(ki(0, 16), T.sc[:, h * 256 + 14:h * 256 + 240:15], ["sc" + H], ["ki" + H], 16)
-        ts(ki(2), ki(0), 10, 0x107FF, A.arith_shift_right, A.bitwise_and, ["ki" + H], ["hi" + H], 8)
+        if PLAN["scan_int"]:
+            key, KI = (lambda n: T.si[:, h * 256 + 14:h * 256 + n * 15:15]), "sc" + H
+        else:
+            key, KI = (lambda n: ki(0, n)), "ki" + H
+            cp(ki(0, 16), T.sc[:, h * 256 + 14:h * 256 + 240:15], ["sc" + H], ["ki" + H], 16)
+        ts(ki(2), key(8), 10, 0x107FF, A.arith_shift_right, A.bitwise_and, [KI], ["hi" + H], 8)
         ts(T.xb[:, x + 8:x + 16], ki(2), 2048.0, None, A.min, None, ["hi" + H], ["hx" + H], 8)
         tt(T.rb[:, c], ki(2).indirect(offE), T.dtop[:], A.min, ["hi" + H, "offE", "dtop"], ["rb" + H], 128, GTT)
         pop([mm(T.pd[:, 0:128], T.boh[:], T.rb[:, c], True, True)], ["boh", "rb" + H], ["pd"], 128)
@@ -484,7 +498,10 @@ def build_ops(g, core, T, topo, rank):
                 ts(out, T.hb[:, c], T.xb[:, x + 8 + j:x + 9 + j], T.wsc[:, j * 16 + 15:j * 16 + 16], A.is_equal, A.mult,
                    ["hb" + H, "hx" + H, "wsc"], E, 128, 0.5)
             elif j == 8:
-                ts(out, T.hb[:, c], 2048.0, float(2 ** 62), A.is_equal, A.mult, ["hb" + H], E, 128, 0.5)
+                if h in PLAN["a_eq"]:
+                    act(out, T.hb[:, c], AF.Relu, ["hb" + H], E, 128, bias=-2047.0 * 2 ** 62, scale=float(2 ** 62))
+                else:
+                    ts(out, T.hb[:, c], 2048.0, float(2 ** 62), A.is_equal, A.mult, ["hb" + H], E, 128, 0.5)
             else:
                 ts(out, T.hb[:, c], T.xb[:, j - 1:j], float(2 ** 62), A.is_equal, A.mult, ["hb" + H, "hx0"], E, 128, 0.5)
         cut = [0, 4, 7, 9] if h == 0 else [0, 5, 10, 14, 17]
@@ -492,8 +509,8 @@ def build_ops(g, core, T, topo, rank):
             js = range(cut[i], cut[i + 1])
             pop([mm(T.pd[:, 128:256], T.bob[:], T.eq[:, (e0 + j) * 128:(e0 + j + 1) * 128], j == 0, j == ne - 1) for j in js],
                 ["bob"] + ["eq%d" % (e0 + j) for j in js], ["pd"], 128 * len(js))
-        ts(T.dl[:, b + 24:b + 40], ki(0, 16), 960, None, A.bitwise_and, None, ["ki" + H], ["dlT" + H], 16)
-        ts(T.dl[:, b + 16:b + 24], ki(0), 2, 240, A.arith_shift_right, A.bitwise_and, ["ki" + H], ["dlF" + H], 8)
+        ts(T.dl[:, b + 24:b + 40], key(16), 960, None, A.bitwise_and, None, [KI], ["dlT" + H], 16)
+        ts(T.dl[:, b + 16:b + 24], key(8), 2, 240, A.arith_shift_right, A.bitwise_and, [KI], ["dlF" + H], 8)
         tt(T.dl[:, b:b + 16], T.xb[:, x:x + 16], T.dl[:, b + 32:b + 48], A.subtract, ["s" + H, "hx" + H, "dlT" + H, "baseS" + H], ["dlS" + H], 16)
         tt(T.wd[:, c], T.pd[:, 128:256], T.thr[:], A.is_lt, ["thr"], ["pd", "wd" + H], 128, 1.0)
         vop(lambda: V.tensor_tensor_scan(WS[h][:], T.r01[:], T.wd[:, c], 0.0, A.mult, A.add), ["r01", "wd" + H], ["ws" + H], 128, 0.5)
@@ -508,8 +525,12 @@ def build_ops(g, core, T, topo, rank):
         o = h * 128
         if t < STEPS - 1:
             ts(T.lp[:, o:o + 64], T.gi[:, o:o + 128:2], 2047, None, A.bitwise_and, None, ["gi" + H], ["lp0" + H], 64)
-            ts(T.lp[:, o + 64:o + 128], T.gi[:, o + 1:o + 128:2], 11, None, A.arith_shift_right, None, ["gi" + H], ["lp1" + H], 64)
-            cp(T.lb[:, so:so + 128], T.lp[:, c], ["lp0" + H, "lp1" + H], ["lb%d%d" % (t + 1, h)], 128)
+            if PLAN["round16"]:
+                lin("lo" + H, T.lb[:, so + 64:so + 128], T.gi[:, o + 1:o + 128:2], 1.0 / 2048, 1.0 / 4096 - 0.5, ["gi" + H], ["lb%d%do" % (t + 1, h)], 64)
+                lin("le" + H, T.lb[:, so:so + 64], T.lp[:, o:o + 64], 1.0, 0.0, ["lp0" + H], ["lb%d%de" % (t + 1, h)], 64)
+            else:
+                ts(T.lp[:, o + 64:o + 128], T.gi[:, o + 1:o + 128:2], 11, None, A.arith_shift_right, None, ["gi" + H], ["lp1" + H], 64)
+                cp(T.lb[:, so:so + 128], T.lp[:, c], ["lp0" + H, "lp1" + H], ["lb%d%de" % (t + 1, h), "lb%d%do" % (t + 1, h)], 128)
         else:
             ts(T.lp[:, o:o + 128:2], T.gi[:, o:o + 128:2], 2047, None, A.bitwise_and, None, ["gi" + H], ["lp0" + H], 64)
             ts(T.lp[:, o + 1:o + 128:2], T.gi[:, o + 1:o + 128:2], 11, None, A.arith_shift_right, None, ["gi" + H], ["lp1" + H], 64)
@@ -517,9 +538,14 @@ def build_ops(g, core, T, topo, rank):
             tt(T.rs[:, c], T.xb[:, x:x + 8].indirect(offE), T.diag[:], A.mult, ["s" + H, "offE", "diag"], ["rsb" + H], 128, GTT)
             pop([mm(T.pd[:, 0:128], T.bob[:], T.rs[:, c], True, True)], ["bob", "rsb" + H], ["pd"], 128)
             act(T.fo[:, 256 + o:384 + o], T.pd[:, 0:128], AF.Copy, [], ["pd", "foS" + H], 128, scale=1.0 / 64)
+        FO, fo = OF, so + 136
+        if u == 2 * STEPS - 1:
+            FO, fo = "ofF", so + 152
+            tt(T.xa[:, 64:72], T.dl[:, b + 16:b + 24], T.dl[:, b + 48:b + 56], A.add, ["dlF" + H, "baseF" + H], ["xaF"], 8)
+            cp(T.lb[:, fo:fo + 8], T.xa[:, 64:72], ["xaF"], [FO], 8)
         send(1, T.uo[:, u * 8:u * 8 + 8], T.lb[:, so + 128:so + 136], [OF], ["uo%d%d" % (t, h)], "ao%d" % u, TUNE["hop"])
-        act(T.fs[:, u * UW:u * UW + 128], FB[h][:, 0:1936].indirect(T.lb[:, so + 136:so + 144]), AF.Copy,
-            [OF, "fz" + H] + ["f%d%d" % (h, n) for n in range(4)], ["fs%d%d" % (t, h)], 128, GAT)
+        act(T.fs[:, u * UW:u * UW + 128], FB[h][:, 0:1936].indirect(T.lb[:, fo:fo + 8]), AF.Copy,
+            [FO, "fz" + H] + ["f%d%d" % (h, n) for n in range(4)], ["fs%d%d" % (t, h)], 128, GAT)
         R, w = ["fs%d%d" % (t, h)], 128
         if t < STEPS - 1:
             pop([mm(T.pd[:, 256 + h * 8:264 + h * 8], T.bob[:], WS[h][:, 15:128:16], True, True)], ["bob", "ws" + H], ["pd"], 64)

import numpy as np
from concourse.mybir import dt, AluOpType, AxisListType, ActivationFunctionType

A = AluOpType
AF = ActivationFunctionType
STEPS = 4
SW = 160
XW = 2192
MW = 3072
UW = 144
BIG = float(2 ** 29)
SHIFT = -127.0625
LIFT = 288.0

SCRATCH = {
    "xs": ("sbuf", [128, 4 * XW], "bfloat16"),
    "vm": ("sbuf", [128, 5 * MW], "bfloat16"),
    "li": ("sbuf", [128, 256], "int32"),
    "sraw": ("sbuf", [128, 256], "int32"),
    "sbf": ("sbuf", [128, 256], "bfloat16"),
    "wi": ("sbuf", [128, 8], "int32"),
    "lb": ("sbuf", [128, 10 * SW], "uint16"),
    "fs": ("sbuf", [128, 8 * UW], "bfloat16"),
    "uf": ("sbuf", [128, 8 * UW], "bfloat16"),
    "uo": ("sbuf", [128, 8 * 8], "uint16"),
    "fo": ("sbuf", [128, 512], "float32"),
    "pint": ("sbuf", [128, 8], "int32"),
    "pcol": ("sbuf", [128, 16], "float32"),
    "ion": ("sbuf", [128, 144], "float32"),
    "kio": ("sbuf", [128, 256], "float32"),
    "r16": ("sbuf", [128, 128], "float32"),
    "idb": ("sbuf", [128, 128], "bfloat16"),
    "idl": ("sbuf", [128, 128], "bfloat16"),
    "idh": ("sbuf", [128, 128], "float16"),
    "bob": ("sbuf", [128, 128], "bfloat16"),
    "boh": ("sbuf", [128, 128], "float16"),
    "bof": ("sbuf", [128, 8], "float32"),
    "diag": ("sbuf", [128, 128], "float32"),
    "dtop": ("sbuf", [128, 128], "float32"),
    "m64": ("sbuf", [128, 240], "bfloat16"),
    "c3": ("sbuf", [128, 256], "bfloat16"),
    "c16": ("sbuf", [128, 128], "bfloat16"),
    "ck": ("sbuf", [128, 128], "bfloat16"),
    "r30": ("sbuf", [128, 480], "bfloat16"),
    "r48": ("sbuf", [128, 128], "bfloat16"),
    "r22": ("sbuf", [128, 128], "bfloat16"),
    "otmp": ("sbuf", [128, 8], "float32"),
    "otmi": ("sbuf", [128, 8], "int32"),
    "rbig": ("sbuf", [128, 240], "float32"),
    "r01": ("sbuf", [128, 128], "bfloat16"),
    "zc": ("sbuf", [128, 144], "bfloat16"),
    "zs": ("sbuf", [128, 144], "bfloat16"),
    "zf": ("sbuf", [128, 144], "float16"),
    "cf": ("sbuf", [128, 64], "float32"),
    "coef": ("sbuf", [128, 128], "float16"),
    "coen": ("sbuf", [128, 128], "float16"),
    "coeq": ("sbuf", [128, 128], "float16"),
    "ee": ("sbuf", [128, 256], "float16"),
    "pm": ("sbuf", [128, 2048], "float16"),
    "ofc": ("sbuf", [128, 48], "uint16"),
    "wrow": ("sbuf", [128, 128], "float32"),
    "wd0": ("sbuf", [128, 128], "float32"),
    "thr": ("sbuf", [128, 128], "float32"),
    "wsc": ("sbuf", [128, 128], "float32"),
    "tol": ("sbuf", [128, 8], "float32"),
    "toli": ("sbuf", [128, 8], "int32"),
    "a": ("sbuf", [128, 4096], "bfloat16"),
    "at": ("sbuf", [128, 4096], "float16"),
    "q": ("sbuf", [128, 2048], "bfloat16"),
    "f0": ("sbuf", [128, 2048], "bfloat16"),
    "f1": ("sbuf", [128, 2048], "bfloat16"),
    "d": ("sbuf", [128, 4096], "float16"),
    "ab": ("sbuf", [128, 4096], "float16"),
    "cl": ("sbuf", [128, 4096], "bfloat16"),
    "tt0": ("sbuf", [128, 1024], "float32"),
    "tt1": ("sbuf", [128, 1024], "float32"),
    "eq": ("sbuf", [128, 26 * 128], "bfloat16"),
    "lh": ("sbuf", [128, 256], "float16"),
    "ui": ("sbuf", [128, 256], "int32"),
    "u2": ("sbuf", [128, 256], "int32"),
    "yy": ("sbuf", [128, 256], "float32"),
    "sq": ("sbuf", [128, 256], "int32"),
    "h0": ("sbuf", [128, 256], "int32"),
    "h16": ("sbuf", [128, 256], "uint16"),
    "hf": ("sbuf", [128, 256], "float16"),
    "ul": ("sbuf", [128, 256], "int32"),
    "um": ("sbuf", [128, 256], "bfloat16"),
    "lt": ("sbuf", [128, 256], "bfloat16"),
    "sc": ("sbuf", [128, 512], "float32"),
    "rb": ("sbuf", [128, 256], "float16"),
    "rs": ("sbuf", [128, 256], "bfloat16"),
    "hb": ("sbuf", [128, 256], "float16"),
    "wd": ("sbuf", [128, 256], "bfloat16"),
    "ws0": ("sbuf", [128, 128], "bfloat16"),
    "ws1": ("sbuf", [128, 128], "bfloat16"),
    "gi": ("sbuf", [128, 256], "int32"),
    "lp": ("sbuf", [128, 256], "int32"),
    "ki": ("sbuf", [128, 64], "int32"),
    "dl": ("sbuf", [128, 128], "int32"),
    "xa": ("sbuf", [128, 72], "float32"),
    "si": ("sbuf", [128, 512], "int32"),
    "xb": ("sbuf", [128, 64], "float32"),
    "pt": ("psum", [128, 1024], "bfloat16"),
    "pf0": ("psum", [128, 512], "float32"),
    "pf1": ("psum", [128, 512], "float32"),
    "pf2": ("psum", [128, 512], "float32"),
    "pf3": ("psum", [128, 512], "float32"),
    "pu": ("psum", [128, 512], "float32"),
    "pc": ("psum", [128, 512], "float32"),
    "pd": ("psum", [128, 512], "float32"),
}
PSUM = [k for k in SCRATCH if SCRATCH[k][0] == "psum"]
DMA_SEMS = ["dx0", "dx1", "dl", "dw", "ds", "dv0", "o0", "o1", "o2", "o3", "o4", "o5"]
ARRIVE = ["ax%d" % i for i in range(1, 4)] + ["av%d" % i for i in range(1, 5)] + ["au%d" % i for i in range(8)] + ["ao%d" % i for i in range(8)]
SEMAPHORES = ["cv", "ca", "cp", "cg", "sent"] + DMA_SEMS + ARRIVE

NENG = 8
ORDER = [("a", 0), ("t", 0), ("a", 1), ("b", 0), ("t", 1), ("b", 1), ("d", 0), ("w", 0), ("d", 1), ("w", 1)]
PLAN = {
    "v_gather": [], "v_gather0": [1, 3],
    "a_turn": [],
    "q_mod": [0, 1, 2, 3],
    "v_mod": [0, 1, 2, 3],
    "v_f": [],
    "a_mark": [],
    "a_near": [0, 1, 2, 3],
    "v_table": [],
    "a_hb": [], "a_eq": [0, 1], "a_pm": 4, "a_small": ["lh0", "lh1", "um0", "um1"], "round16": True, "scan_int": True,
    "fine": [0, 2], "fine_near": [1, 3],
    "banks": {"a": [0, 1, 2], "t": [3], "m": [3]},
}
TUNE = {"cyc": 0.83e-3 * 1.1, "pe": 0.42e-3 * 1.25, "lat": 0.14, "gat": 1.5, "gtt": 1.75, "sca": 3.5, "hop": 3.6, "bulk": 12.0,
        "vfix": 0.045, "afix": 0.06, "pfix": 0.06, "w": 6.0, "noise": [0.05, 0.2, 0.5, 1.0, 2.0], "slack": 0.4, "seed": 0, "rounds": 8000}


def build_ops(g, core, T, topo, rank):
    V, S, P = g.vector, g.scalar, g.tensor
    ops = []
    pr = [0]
    CYC, GAT, GTT = TUNE["cyc"], TUNE["gat"], TUNE["gtt"]

    def op(e, fn, R, W, dur, sem=None, val=0):
        ops.append({"pr": pr[0], "e": e, "fn": fn, "R": list(R), "W": [k for k in W if k not in PSUM],
                    "X": [k for k in W if k in PSUM], "dur": dur, "sem": sem, "val": val})

    def vop(fn, R, W, n, c=1.0):
        op("v", lambda: [fn()], R, W, TUNE["vfix"] + max(64, n * c) * CYC)

    def aop(fn, R, W, n, c=1.0):
        op("a", lambda: [fn()], R, W, TUNE["afix"] + max(64, n * c) * CYC)

    def pop(fns, R, W, cyc):
        op("p", lambda: [f() for f in fns], R, W, TUNE["pfix"] + cyc * TUNE["pe"])

    def gop(fn, R, W, n):
        op("g", lambda: [fn()], R, W, 0.15 + 2 * n * CYC)

    def dma(out, in_, R, W, sem, dur, e="s"):
        q = g.sync if e == "s" else g.scalar
        op(e, lambda: [q.dma_start(out, in_)], R, W, dur, sem, 16)

    def send(back, dst, src, R, W, sem, dur):
        to = T.cores[(rank - back) % len(T.cores)]
        rid, pid = topo.addr(to, core)
        eng = topo.engines(core, to)[:NENG]
        op("r", lambda: [g.remote_dma(dst, src, T.sem[sem], T.sem.sent, pid, rid, sum(1 << e for e in eng))], R, W, dur, sem, len(eng))

    def ts(out, in0, s1, s2, o0, o1, R, W, n, c=1.0):
        if o1 is None:
            vop(lambda: V.tensor_scalar(out, in0, s1, None, o0), R, W, n, c)
        else:
            vop(lambda: V.tensor_scalar(out, in0, s1, s2, o0, o1), R, W, n, c)

    def tt(out, in0, in1, o, R, W, n, c=2.0):
        vop(lambda: V.tensor_tensor(out, in0, in1, o), R, W, n, c)

    def cp(out, in_, R, W, n, c=1.0):
        vop(lambda: V.tensor_copy(out, in_), R, W, n, c)

    def act(out, in_, fn, R, W, n, c=1.0, bias=0.0, scale=1.0):
        aop(lambda: S.activation(out, in_, fn, bias=bias, scale=scale), R, W, n, c)

    def lin(kind, out, in_, scale, bias, R, W, n, c=1.0):
        if kind in PLAN["a_small"]:
            act(out, in_, AF.Identity if bias else AF.Copy, R, W, n, 1.0, bias=bias, scale=scale)
        else:
            ts(out, in_, scale, bias, A.mult, A.add, R, W, n, c)

    def mm(out, l, r, st, sp):
        return lambda: P.matmul(out, l, r, st, sp)

    def iota(out, pat, base, W, n, step=0):
        gop(lambda: g.iota(out, pat, base, step, allow_small_or_imprecise_dtypes=True), [], W, n)

    dma(T.li[:], T.lanes[:], [], ["li"], "dl", 2.5)
    dma(T.xs[:, 0:1024], T.x[:, 0:1024], [], ["x0"], "dx0", 3.5)
    dma(T.xs[:, 1024:2048], T.x[:, 1024:2048], [], ["x0b"], "dx1", 3.5, "a")
    dma(T.wi[:, 0:1], T.wt[:], [], ["wi"], "dw", 2.5)
    gop(lambda: g.iota(T.sraw[:], [[0, 256]], 0, 0), [], ["sraw"], 256)
    dma(T.sraw[0:128:16, :], T.s0[:], [], ["sraw"], "ds", 2.5)
    dma(T.vm[:, 0:2048], T.v[:], [], ["vm0"], "dv0", 5.0)

    gop(lambda: g.iota(T.pint[:, 0:1], [[0, 1]], 0, 1), [], ["pi0"], 1)
    iota(T.ion[:], [[1, 144]], 0, ["ion"], 144)
    iota(T.r16[:], [[0, 8], [1, 16]], 0, ["r16"], 128)
    iota(T.kio[:], [[1, 16], [0, 16]], 0, ["kio"], 256)
    iota(T.c3[:], [[6, 2], [0, 128]], -3, ["c3"], 256)
    iota(T.m64[:], [[0, 16], [64, 15]], 64, ["m64"], 240)
    iota(T.c16[:], [[0, 128]], 16, ["c16"], 128)
    iota(T.ck[:], [[0, 128]], 1, ["ck"], 128, 32767)
    pe_mod = len(PLAN["q_mod"]) < 8
    if pe_mod:
        vop(lambda: V.memset(T.r30[0:32, :], float(2 ** 30)), [], ["r30"], 480, 0.5)
    vop(lambda: V.memset(T.r48[0:32, :], float(2 ** 48)), [], ["r48"], 128, 0.5)
    if PLAN["a_near"]:
        vop(lambda: V.memset(T.r22[0:32, :], 1.5 * 2 ** 22), [], ["r22"], 128, 0.5)
    neg3, pos3 = T.c3[0:1, 0:128], T.c3[0:1, 128:256]
    ts(T.pint[:, 1:2], T.pint[:, 0:1], 15, None, A.bitwise_and, None, ["pi0"], ["pi1"], 1)
    ts(T.pint[:, 2:3], T.pint[:, 0:1], 4, None, A.arith_shift_right, None, ["pi0"], ["pi2"], 1)
    ts(T.pint[:, 3:4], T.pint[:, 0:1], 7, None, A.bitwise_and, None, ["pi0"], ["pi3"], 1)
    ts(T.pint[:, 4:5], T.pint[:, 0:1], 1, 7, A.arith_shift_right, A.bitwise_and, ["pi0"], ["pi4"], 1)
    CP = "pcol"
    cp(T.pcol[:, 0:5], T.pint[:, 0:5], ["pi0", "pi1", "pi2", "pi3", "pi4"], [CP], 5)
    pP, pK, pG, p7, pH = (T.pcol[:, i:i + 1] for i in range(5))
    pZ, pW, p0 = T.pcol[:, 5:6], T.pcol[:, 6:7], T.pcol[:, 8:9]
    ts(pZ, pG, 16.0, 15.0, A.mult, A.add, [CP], ["pz"], 1)
    cp(pW, T.wi[:, 0:1], ["wi"], ["pw"], 1)
    ts(T.idb[:], T.ion[:, 0:128], pP, None, A.is_equal, None, ["ion", CP], ["idb"], 128)
    act(T.idl[:], T.idb[:], AF.Copy, ["idb"], ["idl"], 128, scale=float(2 ** 25))
    act(T.idh[:], T.idb[:], AF.Copy, ["idb"], ["idh"], 128, scale=1024.0)
    ts(T.bof[:], T.ion[:, 0:8], pG, None, A.is_equal, None, ["ion", CP], ["bof"], 8)
    ts(T.cf[:, 16:32], T.r16[:, 0:16], pK, None, A.subtract, None, ["r16", CP], ["cf1"], 16)
    ts(T.cf[:, 32:48], T.r16[:, 0:16], pK, pK, A.is_lt, A.mult, ["r16", CP], ["cf2"], 16)
    tt(T.cf[:, 0:16], T.cf[:, 16:32], T.cf[:, 32:48], A.max, ["cf1", "cf2"], ["cf"], 16)
    COEF = ["coef%d" % r for r in range(8)]
    COEQ = ["coeq%d" % r for r in range(8)]
    if pe_mod:
        ts(p0, pK, 0.0, 256.0, A.is_equal, A.mult, [CP], ["p0"], 1)
        ts(T.cf[:, 48:64], T.cf[:, 0:16], p0, None, A.subtract, None, ["cf", "p0"], ["cf3"], 16)
        for r in range(8):
            act(T.coef[:, r:120:8], T.cf[:, 49:64], AF.Copy, ["cf3", "bof"], [COEF[r]], 16, scale=T.bof[:, r:r + 1])
        act(T.coen[:, 0:120], T.coef[:, 0:120], AF.Copy, COEF, ["coen"], 120, scale=-1.0)
    if PLAN["q_mod"]:
        for r in range(8):
            act(T.coeq[:, r:120:8], T.cf[:, 1:16], AF.Copy, ["cf", "bof"], [COEQ[r]], 16, scale=T.bof[:, r:r + 1])
    ts(T.xs[:, 2048:XW], T.ion[:], pZ, pW, A.is_equal, A.mult, ["ion", "pz", "pw"], ["x0w"], 144)
    ts(T.zc[:], T.ion[:], pZ, float(2 ** 22), A.is_equal, A.mult, ["ion", "pz"], ["zc"], 144)
    act(T.zf[:], T.zc[:], AF.Copy, ["zc"], ["zf"], 144, scale=2.0 ** -8)
    if PLAN["a_near"]:
        act(T.zs[:], T.zc[:], AF.Copy, ["zc"], ["zs"], 144, scale=0.5)
    ts(T.bob[:], T.kio[:, 0:128], pG, None, A.is_equal, None, ["kio", CP], ["bob"], 128)
    act(T.boh[:], T.bob[:], AF.Copy, ["bob"], ["boh"], 128)
    ts(T.diag[:], T.r16[:], pK, None, A.is_equal, None, ["r16", CP], ["diag"], 128)
    act(T.dtop[:], T.diag[:], AF.Copy, ["diag"], ["dtop"], 128, scale=2048.0)
    act(T.rbig[:], T.m64[:], AF.Relu, ["m64"], ["rbig"], 240, bias=2 * BIG, scale=-BIG / 64)
    offM = T.ofc[:, 32:40]
    ts(T.otmp[:], T.ion[:, 0:128:16], pK, 1.0 / 15, A.add, A.mult, ["ion", CP], ["otmp"], 8)
    ts(T.otmi[:], T.otmp[:], -0.47, None, A.add, None, ["otmp"], ["otmi"], 8)
    ts(offM, T.otmi[:], 7.0, None, A.min, None, ["otmi"], ["offM"], 8)
    for h in range(2):
        iota(T["f%d" % h][:, 0:16], [[0, 16]], 0, ["fz%d" % h], 16)
    act(T.r01[:], T.r16[:], AF.Sign, ["r16"], ["r01"], 128)
    offE, offW, offK = T.ofc[:, 0:8], T.ofc[:, 8:10], T.ofc[:, 16:32]
    cp(offE, T.ion[:, 0:8], ["ion"], ["offE"], 8)
    ts(T.pcol[:, 7:8], p7, 16.0, 15.0, A.mult, A.add, [CP], ["pw7"], 1)
    ts(offW, T.ion[:, 0:2], 0.0, T.pcol[:, 7:8], A.mult, A.add, ["ion", "pw7"], ["offW"], 2)
    ts(offK, T.ion[:, 0:16], 0.0, pK, A.mult, A.add, ["ion", CP], ["offK"], 16)
    tt(T.ee[:], T.cf[:, 0:16].indirect(offK), T.kio[:], A.is_equal, ["cf", "offK", "kio"], ["ee"], 256, GTT)
    PM = ["pm%d" % r for r in range(8)]
    for r in range(8):
        if r < PLAN["a_pm"]:
            act(T.pm[:, r * 256:(r + 1) * 256], T.ee[:], AF.Copy, ["ee", "bof"], [PM[r]], 256, scale=T.bof[:, r:r + 1])
        else:
            ts(T.pm[:, r * 256:(r + 1) * 256], T.ee[:], T.bof[:, r:r + 1], None, A.mult, None, ["ee", "bof"], [PM[r]], 256, 0.5)
    vop(lambda: V.memset(T.wd0[:], 0.5), [], ["wd0"], 128)
    iota(T.thr[:], [[0, 128]], 0, ["thr"], 128)
    vop(lambda: V.tensor_tensor_scan(T.wrow[:], T.wd0[:], T.thr[:], float(2 ** 61), A.mult, A.add), ["wd0", "thr"], ["wrow"], 128)
    tt(T.wd0[:], T.wrow[:], T.diag[:], A.mult, ["wrow", "diag"], ["wd0"], 128)
    act(T.thr[:], T.wd0[:], AF.Copy, ["wd0"], ["thr"], 128, scale=2.5)
    vop(lambda: V.tensor_tensor_scan(T.wsc[:], T.r01[:], T.wd0[:], 0.0, A.mult, A.add), ["r01", "wd0"], ["wsc"], 128)
    for h in range(2):
        b = h * 64 + 32
        gop(lambda b=b: g.iota(T.dl[:, b + 8:b + 16], [[128, 8]], 2048, 1), [], ["baseS%d" % h], 8)
        ts(T.dl[:, b + 16:b + 24], T.ion[:, 0:8], 240.0, pK, A.mult, A.add, ["ion", CP], ["baseF%d" % h], 8)
        ts(T.dl[:, b + 24:b + 32], T.ion[:, 0:8], 8.0, pH, A.mult, A.add, ["ion", CP], ["baseT%d" % h], 8)
    vop(lambda: V.memset(T.tol[:, 0:1], 2.5), [], ["tol0"], 1)

    for h in range(2):
        for b in range(2):
            cp(T.lb[:, h * SW + b * 64:h * SW + b * 64 + 64], T.li[:, h * 128 + b:h * 128 + 128:2], ["li"], ["lb0%d" % h + "eo"[b]], 64)
    cp(T.sbf[:], T.sraw[:], ["sraw"], ["sbf"], 256)
    pop([mm(T.pd[:, 0:16], T.zc[:, 15 - r:143 - r], T.sbf[:, r:256:16], r == 0, r == 15) for r in range(16)],
        ["zc", "sbf"], ["pd"], 16 * 64)
    for h in range(2):
        act(T.xb[:, h * 32:h * 32 + 8], T.pd[:, h * 8:h * 8 + 8], AF.Copy, [], ["pd", "s%d" % h], 8, scale=2.0 ** -16)
    X0 = ["x0", "x0b", "x0w"]

    def send_items(t, after):
        send(t, T.xs[:, t * XW:(t + 1) * XW], T.xs[:, 0:XW], X0 + after, ["x%d" % t], "ax%d" % t, TUNE["bulk"] * (2 if t == 1 else 1))

    def send_memory(t, after):
        send(1, T.vm[:, (t + 1) * MW:(t + 1) * MW + 2048], T.vm[:, t * MW:t * MW + 2048], ["vm%d" % t] + after, ["vm%d" % (t + 1)],
             "av%d" % (t + 1), TUNE["bulk"] * (2 if t == 0 else 1))
    send_items(1, [])
    send_memory(0, [])

    bank = {}
    FB = [T.f0, T.f1]
    TB = [T.tt0, T.tt1]
    WS = [T.ws0, T.ws1]

    def nb(kind):
        ring = PLAN["banks"][kind]
        key = tuple(ring)
        bank[key] = (bank.get(key, -1) + 1) % len(ring)
        return ring[bank[key]]

    def stage_a(t, h):
        lo = (t * 2 + h) * SW
        LB = "lb%d%d" % (t, h)
        F = FB[h]
        H = str(h)
        o = h * 2048
        XS, XZ = (["x0", "x0b"], "x0w") if t == 0 else (["x%d" % t], "x%d" % t)
        zw = t * XW + 2048
        for Q in range(2):
            ao = o + Q * 1024
            for e0, e1 in ([(0, 2), (2, 4)] if h * 2 + Q in PLAN["fine"] else [(0, 4)]):
                AK = ["a%d%d%d%d" % (h, Q, e0, b) for b in range(2)]
                w = (e1 - e0) * 8
                for b in range(2):
                    c0 = b * 64 + Q * 32 + e0 * 8
                    out, src = T.a[:, o + c0 * 16:o + (c0 + w) * 16], T.xs[:, t * XW:t * XW + 2048].indirect(T.lb[:, lo + c0:lo + c0 + w])
                    if h * 4 + Q * 2 + b in PLAN["v_gather0" if t == 0 else "v_gather"]:
                        cp(out, src, XS + [LB + "eo"[b]], [AK[b]], w * 16, GAT)
                    else:
                        act(out, src, AF.Copy, XS + [LB + "eo"[b]], [AK[b]], w * 16, GAT)
                fns = []
                for el in range(e0, e1):
                    for b in range(2):
                        c = o + (b * 8 + Q * 4 + el) * 128
                        fns.append(lambda c=c, j=el * 2 + b: P.transpose(T.pt[:, j * 128:(j + 1) * 128], T.a[:, c:c + 128], T.idb[:]))
                pop(fns, AK + ["idb"], ["pt"], w * 32)
                AT = ["at%d%d" % (h, Q * 2 + x) for x in range(e0 // 2, e1 // 2)]
                kinds = {h * 4 + Q * 2 + x in PLAN["q_mod"] for x in range(e0 // 2, e1 // 2)}
                assert len(kinds) == 1
                shift = LIFT if True in kinds else SHIFT
                if h * 2 + Q in PLAN["a_turn"]:
                    act(T.at[:, ao + e0 * 256:ao + e1 * 256], T.pt[:, e0 * 256:e1 * 256], AF.Identity, [], ["pt"] + AT, w * 32, bias=shift)
                else:
                    ts(T.at[:, ao + e0 * 256:ao + e1 * 256], T.pt[:, e0 * 256:e1 * 256], shift, None, A.add, None, [], ["pt"] + AT, w * 32, 0.5)
            for n in (2 * Q, 2 * Q + 1):
                k = nb("a")
                AT = "at%d%d" % (h, n)
                pf, PF = T["pf%d" % k], "pf%d" % k
                Fo, FK = F[:, 16 + n * 480:496 + n * 480], "f%d%d" % (h, n)

                def sums(coef, first, last):
                    fns = []
                    for j in range(4):
                        c = o + (n * 4 + j) * 128
                        s = (j >> 1) * 240
                        fns.append(mm(pf[:, s + (j & 1):s + 240:2], T.at[:, c:c + 128], coef[:, 0:120], first and j == 0, last and j == 3))
                    return fns
                if h * 4 + n in PLAN["q_mod"]:
                    qq = T.q[:, k * 512:k * 512 + 480]
                    pop(sums(T.coeq, True, True), [AT] + COEQ, [PF], 480)
                    if h * 4 + n in PLAN["v_mod"]:
                        act(qq, pf[:, 0:480], AF.Identity, [], [PF, "q%d" % k], 480, bias=127.5, scale=-1.0)
                        tt(Fo, pf[:, 0:480], qq, A.add, ["q%d" % k], [PF, FK], 480, 1.0)
                        continue
                    act(qq, pf[:, 0:480], AF.Identity, [], [PF, "q%d" % k], 480, bias=127.5, scale=-1.0)
                    pop([mm(pf[:, 0:480], T.idb[:], qq, True, False)] + sums(T.coeq, False, True), [AT, "q%d" % k, "idb"], [PF], 960)
                    off = 0.0
                else:
                    pop([mm(pf[:, 0:480], neg3, T.r30[0:1, :], True, False)] + sums(T.coen, False, False), [AT, "coen", "c3", "r30"], [PF], 960)
                    pop([mm(pf[:, 0:480], pos3, T.r30[0:1, :], False, False)] + sums(T.coef, False, True), [AT] + COEF, [PF], 960)
                    off = 127.5
                if h * 4 + n in PLAN["v_f"]:
                    ts(Fo, pf[:, 0:480], off, None, A.add, None, [], [PF, FK], 480)
                else:
                    act(Fo, pf[:, 0:480], AF.Identity, [], [PF, FK], 480, bias=off)
            u0 = Q * 60
            pop([mm(T.pu[:, u0:u0 + 60], T.xs[:, zw + 15 - r:zw + 143 - r], F[:, 16 + Q * 960 + r:976 + Q * 960:16], r == 0, r == 15)
                 for r in range(16)], [XZ, "f%d%d" % (h, 2 * Q), "f%d%d" % (h, 2 * Q + 1)], ["pu"], 1024)
            c = slice(h * 128 + u0, h * 128 + u0 + 60)
            K = "%d%d" % (h, Q)
            lin("ui" + H, T.ui[:, c], T.pu[:, u0:u0 + 60], 1.0, 0.0, [], ["pu", "ui" + K], 60)
            ts(T.u2[:, c], T.ui[:, c], 4095, None, A.bitwise_and, None, ["ui" + K], ["u2" + K], 60)
            lin("yy" + H, T.yy[:, c], T.u2[:, c], 1.0, 1184.0, ["u2" + K], ["yy" + K], 60)
            tt(T.sq[:, c], T.yy[:, c], T.u2[:, c], A.mult, ["yy" + K, "u2" + K], ["sq" + K], 60)
            ts(T.h0[:, c], T.sq[:, c], 5, 2047, A.arith_shift_right, A.bitwise_and, ["sq" + K], ["h0" + K], 60)
            cp(T.h16[:, c], T.h0[:, c], ["h0" + K], ["h16" + K], 60)
        c = slice(h * 128, h * 128 + 120)
        ts(T.ul[:, c], T.ui[:, c], 15, None, A.bitwise_and, None, ["ui%d0" % h, "ui%d1" % h], ["ul" + H], 120)
        lin("um" + H, T.um[:, c], T.ul[:, c], 64.0, 0.0, ["ul" + H], ["um" + H], 120)
        lin("hf" + H, T.hf[:, c], T.h16[:, c], 1.0, 0.0, ["h16%d0" % h, "h16%d1" % h], ["hf" + H], 120, 0.5)
        tt(T.lt[:, h * 128:h * 128 + 128], T.xb[:, h * 32:h * 32 + 8].indirect(offM), T.m64[:, 0:128], A.is_gt,
           ["s" + H, "offM", "m64"], ["lt" + H], 128, GTT)
        if h == 1 and t < STEPS - 2:
            send_items(t + 2, ["hf1"])

    def stage_t(t, h):
        lo = (t * 2 + h) * SW
        LB = "lb%d%d" % (t, h)
        H = str(h)
        o = h * 128
        lin("lh" + H, T.lh[:, o:o + 64], T.lb[:, lo:lo + 64], 1.0 / 2048, 0.0, [LB + "e"], ["lh0" + H], 64, 0.5)
        lin("lh" + H, T.lh[:, o + 64:o + 128], T.lb[:, lo + 64:lo + 128], 1.0, 0.0, [LB + "o"], ["lh1" + H], 64, 0.5)
        for n in range(2):
            k = nb("t")
            pf = T["pf%d" % k]
            fns = []
            for m in range(8):
                for b in range(2):
                    fns.append(mm(pf[:, m * 64:m * 64 + 64], T.pm[:, n * 8 + m:2048:16], T.lh[:, o + b * 64:o + b * 64 + 64], b == 0, b == 1))
            pop(fns, PM + ["lh0" + H, "lh1" + H], ["pf%d" % k], 1024)
            if h * 2 + n in PLAN["v_table"]:
                ts(TB[h][:, n * 512:(n + 1) * 512], pf[:], 2048.0, None, A.mult, None, [], ["pf%d" % k, "tt%d%d" % (h, n)], 512)
            else:
                act(TB[h][:, n * 512:(n + 1) * 512], pf[:], AF.Copy, [], ["pf%d" % k, "tt%d%d" % (h, n)], 512, scale=2048.0)

    def stage_b(t, h):
        F = FB[h]
        H = str(h)
        o = h * 2048
        VM = "vm%d" % t
        tol, TOL = (T.tol[:, 0:1], "tol0") if t == 0 else (T.uf[:, (2 * t - 1) * UW + 128:(2 * t - 1) * UW + 129], "uf%d1" % (t - 1))
        nc = slice(h * 128, h * 128 + 120)
        pop([mm(T.pc[:, 120:240], T.c16[0:1, :], T.m64[0:1, 0:120], True, False)], ["c16", "m64"], ["pc", "key"], 120)
        pop([mm(T.pc[:, 120:240], T.idb[:], T.um[:, nc], False, False)], ["key", "idb", "um" + H], ["far2"], 120)
        for Q in range(2):
            for n in (2 * Q, 2 * Q + 1):
                c = slice(o + n * 480, o + n * 480 + 480)
                K = "%d%d" % (h, n)
                src = T.vm[:, t * MW:t * MW + 2048].indirect(T.h16[:, h * 128 + n * 30:h * 128 + n * 30 + 30])
                if h * 4 + n in PLAN["a_mark"]:
                    k = nb("m")
                    pf = T["pf%d" % k]
                    mk = T.q[:, k * 512:k * 512 + 480]
                    act(mk, src, AF.Copy, [VM, "h16%d%d" % (h, Q)], ["q%d" % k], 480, GAT, scale=-1.0)
                    pop([mm(pf[:, 0:480], T.idb[:], F[:, 16 + n * 480:496 + n * 480], True, False), mm(pf[:, 0:480], T.idb[:], mk, False, True)],
                        ["idb", "q%d" % k, "f" + K], ["pf%d" % k], 960)
                    act(T.ab[:, c], pf[:, 0:480], AF.Abs, [], ["pf%d" % k, "ab" + K], 480)
                    continue
                tt(T.d[:, c], src, F[:, 16 + n * 480:496 + n * 480], A.subtract, [VM, "h16%d%d" % (h, Q), "f" + K], ["d" + K], 480, GTT)
                act(T.ab[:, c], T.d[:, c], AF.Abs, ["d" + K], ["ab" + K], 480)
            sign = h * 2 + Q in PLAN["a_near"]
            for n0, n1 in ([(0, 1), (1, 2)] if h * 2 + Q in PLAN["fine_near"] else [(0, 2)]):
                c = slice(o + (2 * Q + n0) * 480, o + (2 * Q + n1) * 480)
                RK = [TOL] + ["ab%d%d" % (h, 2 * Q + x) for x in range(n0, n1)]
                WK = ["cl%d%d" % (h, 2 * Q + x) for x in range(n0, n1)]
                if sign:
                    act(T.cl[:, c], T.ab[:, c], AF.Sign, RK, WK, 480 * (n1 - n0), bias=tol, scale=-1.0)
                else:
                    ts(T.cl[:, c], T.ab[:, c], tol, -0.21875, A.is_le, A.add, RK, WK, 480 * (n1 - n0), 0.5)
            s = o + Q * 960
            far, cnt = T.pc[:, 120 + Q * 60:180 + Q * 60], T.pc[:, Q * 60:Q * 60 + 60]
            pop([mm(far, T.zf[:, 15 - r:143 - r], T.ab[:, s + r:s + 960:16], False, False) for r in range(16)],
                ["zf", "key", "ab%d%d" % (h, 2 * Q), "ab%d%d" % (h, 2 * Q + 1)], ["far%d" % Q], 1024)
            z = T.zs if sign else T.zc
            pop([mm(cnt, z[:, 15 - r:143 - r], T.cl[:, s + r:s + 960:16], False, False) for r in range(16)]
                + ([mm(cnt, pos3, T.r22[0:1, 0:60], False, False)] if sign else []),
                ["zc", "key", "cl%d%d" % (h, 2 * Q), "cl%d%d" % (h, 2 * Q + 1)] + (["zs", "r22", "c3"] if sign else []), ["cnt%d" % Q], 1024 + 64 * sign)
        cnt = T.pc[:, 0:120]
        pop([mm(cnt, pos3, T.r48[0:1, 0:120], False, False), mm(cnt, neg3, T.r48[0:1, 0:120], False, False),
             mm(cnt, T.ck[0:2, :], T.m64[0:2, 0:120], False, False), mm(cnt, T.idl[:], T.lt[:, nc], False, False),
             mm(cnt, T.idh[:], T.hf[:, nc], False, True)],
            ["c3", "r48", "ck", "m64", "idl", "idh", "lt" + H, "hf" + H, "far0", "far1", "far2", "cnt0", "cnt1"], ["pc"], 600)
        vop(lambda: V.tensor_tensor_scan((T.si if PLAN["scan_int"] else T.sc)[:, h * 256:h * 256 + 240], T.rbig[:], T.pc[:, 0:240], 0.0, A.add, A.min), ["rbig"], ["pc", "sc" + H], 240)

    def stage_d(t, h):
        H = str(h)
        c = slice(h * 128, h * 128 + 128)
        ki = lambda j, n=8: T.ki[:, h * 32 + j * 8:h * 32 + j * 8 + n]
        b = h * 64
        x = h * 32
        u = t * 2 + h
        if PLAN["scan_int"]:
            key, KI = (lambda n: T.si[:, h * 256 + 14:h * 256 + n * 15:15]), "sc" + H
        else:
            key, KI = (lambda n: ki(0, n)), "ki" + H
            cp(ki(0, 16), T.sc[:, h * 256 + 14:h * 256 + 240:15], ["sc" + H], ["ki" + H], 16)
        ts(ki(2), key(8), 10, 0x107FF, A.arith_shift_right, A.bitwise_and, [KI], ["hi" + H], 8)
        ts(T.xb[:, x + 8:x + 16], ki(2), 2048.0, None, A.min, None, ["hi" + H], ["hx" + H], 8)
        tt(T.rb[:, c], ki(2).indirect(offE), T.dtop[:], A.min, ["hi" + H, "offE", "dtop"], ["rb" + H], 128, GTT)
        pop([mm(T.pd[:, 0:128], T.boh[:], T.rb[:, c], True, True)], ["boh", "rb" + H], ["pd"], 128)
        if h in PLAN["a_hb"]:
            act(T.hb[:, c], T.pd[:, 0:128], AF.Copy, [], ["pd", "hb" + H], 128)
        else:
            cp(T.hb[:, c], T.pd[:, 0:128], [], ["pd", "hb" + H], 128)
        ne = 9 if h == 0 else 17
        e0 = 9 * h
        for j in range(ne):
            out = T.eq[:, (e0 + j) * 128:(e0 + j + 1) * 128]
            E = ["eq%d" % (e0 + j)]
            if j < 8:
                ts(out, T.hb[:, c], T.xb[:, x + 8 + j:x + 9 + j], T.wsc[:, j * 16 + 15:j * 16 + 16], A.is_equal, A.mult,
                   ["hb" + H, "hx" + H, "wsc"], E, 128, 0.5)
            elif j == 8:
                if h in PLAN["a_eq"]:
                    act(out, T.hb[:, c], AF.Relu, ["hb" + H], E, 128, bias=-2047.0 * 2 ** 62, scale=float(2 ** 62))
                else:
                    ts(out, T.hb[:, c], 2048.0, float(2 ** 62), A.is_equal, A.mult, ["hb" + H], E, 128, 0.5)
            else:
                ts(out, T.hb[:, c], T.xb[:, j - 1:j], float(2 ** 62), A.is_equal, A.mult, ["hb" + H, "hx0"], E, 128, 0.5)
        cut = [0, 4, 7, 9] if h == 0 else [0, 5, 10, 14, 17]
        for i in range(len(cut) - 1):
            js = range(cut[i], cut[i + 1])
            pop([mm(T.pd[:, 128:256], T.bob[:], T.eq[:, (e0 + j) * 128:(e0 + j + 1) * 128], j == 0, j == ne - 1) for j in js],
                ["bob"] + ["eq%d" % (e0 + j) for j in js], ["pd"], 128 * len(js))
        ts(T.dl[:, b + 24:b + 40], key(16), 960, None, A.bitwise_and, None, [KI], ["dlT" + H], 16)
        ts(T.dl[:, b + 16:b + 24], key(8), 2, 240, A.arith_shift_right, A.bitwise_and, [KI], ["dlF" + H], 8)
        tt(T.dl[:, b:b + 16], T.xb[:, x:x + 16], T.dl[:, b + 32:b + 48], A.subtract, ["s" + H, "hx" + H, "dlT" + H, "baseS" + H], ["dlS" + H], 16)
        tt(T.wd[:, c], T.pd[:, 128:256], T.thr[:], A.is_lt, ["thr"], ["pd", "wd" + H], 128, 1.0)
        vop(lambda: V.tensor_tensor_scan(WS[h][:], T.r01[:], T.wd[:, c], 0.0, A.mult, A.add), ["r01", "wd" + H], ["ws" + H], 128, 0.5)
        tt(T.xa[:, x:x + 32], WS[h][:, 0:128].indirect(offW), T.dl[:, b:b + 32], A.mult,
           ["ws" + H, "offW", "dlT" + H, "dlF" + H, "dlS" + H], ["xa" + H], 32, GTT)
        tt(T.xb[:, x:x + 32], T.xa[:, x:x + 32], T.dl[:, b + 32:b + 64], A.add,
           ["xa" + H, "baseT" + H, "baseS" + H, "baseF" + H, "dlT" + H], ["xb" + H, "s" + H, "hx" + H], 32)
        so = (u + 2) * SW
        OF = "of%d%d" % (t, h)
        cp(T.lb[:, so + 128:so + 152], T.xb[:, x + 8:x + 32], ["xb" + H, "hx" + H], [OF], 24)
        cp(T.gi[:, c], TB[h][:, 0:1024].indirect(T.lb[:, so + 144:so + 152]), [OF, "tt%d0" % h, "tt%d1" % h], ["gi" + H], 128, GAT)
        o = h * 128
        if t < STEPS - 1:
            ts(T.lp[:, o:o + 64], T.gi[:, o:o + 128:2], 2047, None, A.bitwise_and, None, ["gi" + H], ["lp0" + H], 64)
            if PLAN["round16"]:
                lin("lo" + H, T.lb[:, so + 64:so + 128], T.gi[:, o + 1:o + 128:2], 1.0 / 2048, 1.0 / 4096 - 0.5, ["gi" + H], ["lb%d%do" % (t + 1, h)], 64)
                lin("le" + H, T.lb[:, so:so + 64], T.lp[:, o:o + 64], 1.0, 0.0, ["lp0" + H], ["lb%d%de" % (t + 1, h)], 64)
            else:
                ts(T.lp[:, o + 64:o + 128], T.gi[:, o + 1:o + 128:2], 11, None, A.arith_shift_right, None, ["gi" + H], ["lp1" + H], 64)
                cp(T.lb[:, so:so + 128], T.lp[:, c], ["lp0" + H, "lp1" + H], ["lb%d%de" % (t + 1, h), "lb%d%do" % (t + 1, h)], 128)
        else:
            ts(T.lp[:, o:o + 128:2], T.gi[:, o:o + 128:2], 2047, None, A.bitwise_and, None, ["gi" + H], ["lp0" + H], 64)
            ts(T.lp[:, o + 1:o + 128:2], T.gi[:, o + 1:o + 128:2], 11, None, A.arith_shift_right, None, ["gi" + H], ["lp1" + H], 64)
            cp(T.fo[:, c], T.lp[:, c], ["lp0" + H, "lp1" + H], ["foL" + H], 128)
            tt(T.rs[:, c], T.xb[:, x:x + 8].indirect(offE), T.diag[:], A.mult, ["s" + H, "offE", "diag"], ["rsb" + H], 128, GTT)
            pop([mm(T.pd[:, 0:128], T.bob[:], T.rs[:, c], True, True)], ["bob", "rsb" + H], ["pd"], 128)
            act(T.fo[:, 256 + o:384 + o], T.pd[:, 0:128], AF.Copy, [], ["pd", "foS" + H], 128, scale=1.0 / 64)
        FO, fo = OF, so + 136
        if u == 2 * STEPS - 1:
            FO, fo = "ofF", so + 152
            tt(T.xa[:, 64:72], T.dl[:, b + 16:b + 24], T.dl[:, b + 48:b + 56], A.add, ["dlF" + H, "baseF" + H], ["xaF"], 8)
            cp(T.lb[:, fo:fo + 8], T.xa[:, 64:72], ["xaF"], [FO], 8)
        send(1, T.uo[:, u * 8:u * 8 + 8], T.lb[:, so + 128:so + 136], [OF], ["uo%d%d" % (t, h)], "ao%d" % u, TUNE["hop"])
        act(T.fs[:, u * UW:u * UW + 128], FB[h][:, 0:1936].indirect(T.lb[:, fo:fo + 8]), AF.Copy,
            [FO, "fz" + H] + ["f%d%d" % (h, n) for n in range(4)], ["fs%d%d" % (t, h)], 128, GAT)
        R, w = ["fs%d%d" % (t, h)], 128
        if t < STEPS - 1:
            pop([mm(T.pd[:, 256 + h * 8:264 + h * 8], T.bob[:], WS[h][:, 15:128:16], True, True)], ["bob", "ws" + H], ["pd"], 64)
            if h == 1:
                vop(lambda: V.tensor_reduce(T.tol[:, 1:2], T.pd[:, 256:272], AxisListType.X, A.add, negate=True), [], ["pd", "tn"], 16)
                cp(T.toli[:, 0:1], T.tol[:, 1:2], ["tn"], ["tni"], 1)
                ts(T.toli[:, 1:2], T.toli[:, 0:1], 3, None, A.bitwise_and, None, ["tni"], ["tn3"], 1)
                ts(T.fs[:, u * UW + 128:u * UW + 129], T.toli[:, 1:2], 2.5, None, A.add, None, ["tn3"], ["tl%d" % t], 1)
                R, w = R + ["tl%d" % t], 129
        send(1, T.uf[:, u * UW:u * UW + w], T.fs[:, u * UW:u * UW + w], R, ["uf%d%d" % (t, h)], "au%d" % u, TUNE["hop"])

    def stage_w(t, h):
        u = t * 2 + h
        cp(T.vm[:, (t + 1) * MW:(t + 2) * MW].indirect(T.uo[:, u * 8:u * 8 + 8]), T.uf[:, u * UW:u * UW + 128],
           ["uo%d%d" % (t, h), "uf%d%d" % (t, h)], ["vm%d" % (t + 1)], 128, TUNE["sca"])
        if h == 1 and t < STEPS - 1:
            send_memory(t + 1, [])

    for t in range(STEPS):
        for fn, h in ORDER:
            pr[0] += 1
            {"a": stage_a, "b": stage_b, "t": stage_t, "d": stage_d, "w": stage_w}[fn](t, h)
    pr[0] += 1

    dma(T.yv[:, 0:1024], T.vm[:, 4 * MW:4 * MW + 1024], ["vm4"], [], "o0", 3.5)
    dma(T.yv[:, 1024:2048], T.vm[:, 4 * MW + 1024:4 * MW + 2048], ["vm4"], [], "o1", 3.5, "a")
    dma(T.yl[:], T.fo[:, 0:256], ["foL0", "foL1"], [], "o2", 2.5)
    dma(T.ys[:], T.fo[0:128:16, 256:512], ["foS0", "foS1"], [], "o3", 2.5)
    return ops


def graph(ops):
    lastw, readers, lastx = {}, {}, {}
    deps, hard = [], []
    for i, o in enumerate(ops):
        raw = {lastw[k] for k in o["R"] if k in lastw}
        d = set(raw)
        for k in o["W"]:
            if k in lastw:
                d.add(lastw[k])
            d.update(readers.get(k, []))
        raw = set(d)
        d.update(lastx[k] for k in o["X"] if k in lastx)
        d.discard(i)
        deps.append(sorted(d))
        hard.append({j for j in d if j != i and (j in raw and o["e"] != "p") or ops[j]["e"] != o["e"] or ops[j]["sem"] or o["sem"]})
        for k in o["R"]:
            readers.setdefault(k, []).append(i)
        for k in o["W"]:
            lastw[k] = i
            readers[k] = []
        for k in o["X"]:
            lastx[k] = i
    return deps, hard


def place(pre, post, queue, hold, rank):
    n = len(pre)
    S, E = {e: [] for e in "vapgs"}, {e: [] for e in "vapgs"}
    left = [len(p) for p in pre]
    ready = [(rank[i], i) for i in range(n) if not left[i]]
    st = [0.0] * n
    while ready:
        ready.sort(reverse=True)
        i = ready.pop()[1]
        a = 0.0
        for j, w in pre[i]:
            if st[j] + w > a:
                a = st[j] + w
        s, e, h = S[queue[i]], E[queue[i]], hold[i]
        x = m = len(s)
        while x > 0 and e[x - 1] > a:
            x -= 1
        while x < m and s[x] < a + h:
            a = e[x]
            x += 1
        s.insert(x, a)
        e.insert(x, a + h)
        st[i] = a
        for j in post[i]:
            left[j] -= 1
            if not left[j]:
                ready.append((rank[j], j))
    return np.array(st)


def order_ops(ops):
    n = len(ops)
    deps, hard = graph(ops)
    queue = ["g" if o["e"] == "r" else o["e"] for o in ops]
    hold = [(1.0 if o["e"] == "r" else 0.1) if o["sem"] else o["dur"] for o in ops]
    dur = [o["dur"] for o in ops]
    pre = [[(j, dur[j] + (TUNE["lat"] if j in hard[i] else 0.0)) for j in deps[i]] for i in range(n)]
    post = [[] for _ in range(n)]
    rpre = [[(n, dur[i] - hold[i])] for i in range(n)] + [[]]
    for i in range(n):
        for j, w in pre[i]:
            post[j].append(i)
            rpre[j].append((i, hold[i] + w - hold[j]))
    rpost = [list(d) for d in deps] + [list(range(n))]
    lev = [0.0] * n
    pr = [o["pr"] for o in ops]
    for i in range(n - 1, -1, -1):
        lev[i] = max(w - hold[j] + hold[i] + lev[j] for j, w in rpre[i] if j < n) if post[i] else dur[i]
        if pr[i] == 0 and post[i]:
            pr[i] = min(pr[j] for j in post[i])
    names, role = {}, []
    for o in ops:
        key = ((o["pr"] - 1) % len(ORDER), o["e"], len([1 for q in ops[:len(role)] if q["pr"] == o["pr"] and q["e"] == o["e"]]))
        role.append(names.setdefault(key if 0 < o["pr"] <= STEPS * len(ORDER) else len(role), len(names)))
    role, hs, du = np.array(role), np.array(hold), np.array(dur)
    rng = np.random.default_rng(TUNE["seed"])
    noise = lambda: (rng.random(len(names)) * rng.choice(TUNE["noise"]) * (rng.random(len(names)) < rng.choice([0.05, 0.2, 1.0])))[role]
    st = place(pre, post, queue, hold, [pr[i] * TUNE["w"] - lev[i] for i in range(n)])
    best = cur = (max(st + du), st)
    for rnd in range(TUNE["rounds"]):
        bk = place(rpre, rpost, queue + ["s"], hold + [0.0], list(noise() - (cur[1] + hs)) + [-1e9])
        st = place(pre, post, queue, hold, list(noise() - (bk[:n] + hs)))
        if max(st + du) < cur[0] + TUNE["slack"] * (1 - rnd / TUNE["rounds"]):
            cur = (max(st + du), st)
        if cur[0] < best[0]:
            best = cur
    st = best[1]
    return hard, sorted(range(n), key=lambda i: (st[i], i)), [float(x) for x in st + du]


PLACED = []


def rank_program(g, core, T, topo):
    rank = T.rank_of(core)
    if rank is None:
        return
    ops = build_ops(g, core, T, topo, rank)
    if not PLACED:
        PLACED.append(order_ops(ops))
    hard, order, end = PLACED[0]
    Q = {"v": g.vector, "a": g.scalar, "p": g.tensor, "g": g, "s": g.sync, "r": g}
    own = {"v": "cv", "a": "ca", "p": "cp", "g": "cg"}
    count = {s: 0 for s in SEMAPHORES}
    done, knew = {}, {}
    seen = {e: {} for e in "vapgs"}
    for i in order:
        o = ops[i]
        e = "g" if o["e"] == "r" else o["e"]
        for j in sorted(hard[i], key=lambda j: -end[j]):
            s, v = done[j]
            if seen[e].get(s, 0) < v:
                v = max(done[k][1] for k in hard[i] if done[k][0] == s)
                Q[e].wait_ge(T.sem[s], v)
                seen[e][s] = v
            for s, v in knew[j].items():
                seen[e][s] = max(seen[e].get(s, 0), v)
        ins = o["fn"]()
        knew[i] = {} if o["e"] == "r" else dict(seen[e])
        if o["e"] == "r":
            done[i] = (o["sem"], o["val"])
            count[o["sem"]] = o["val"]
            count["sent"] += o["val"]
        elif o["sem"]:
            ins[0].then_inc(T.sem[o["sem"]], 16)
            count[o["sem"]] = 16
            done[i] = (o["sem"], 16)
        else:
            s = own[e]
            for x in ins:
                x.then_inc(T.sem[s], 1)
            count[s] += len(ins)
            done[i] = (s, count[s])
    for s in SEMAPHORES:
        if count[s]:
            g.wait_ge(T.sem[s], count[s])
